import numpy as np
import ml_dtypes


def mxq(x, axis, fmt="e4m3"):
    dtype, down = {"e4m3": (ml_dtypes.float8_e4m3fn, 7), "e5m2": (ml_dtypes.float8_e5m2, 14)}[fmt]
    v = np.moveaxis(np.asarray(x, np.float32).astype(ml_dtypes.bfloat16).astype(np.float64), axis, -1)
    blocks = v.reshape(v.shape[:-1] + (-1, 32))
    amax = np.abs(blocks).max(-1, keepdims=True)
    byte = np.maximum(np.where(amax > 0, np.frexp(amax)[1] - 1 + 127, 0) - down, 1)
    scale = np.exp2(byte - 127.0)
    codes = (blocks / scale).astype(np.float32).astype(dtype).astype(np.float64)
    return np.moveaxis((codes * scale).reshape(v.shape), -1, axis)


WIDE = False


def mx_kscale(k):
    if not WIDE:
        return np.ones(k)
    levels = np.array([10, -10, 5, -5, 0])
    if k % 512:
        return np.exp2(np.random.permutation(np.resize(levels, k // 32))).repeat(32)
    a = np.empty((k // 512, 16))
    for p in range(k // 512):
        a[p, :8] = np.random.permutation(np.resize(levels, 8))
        for g in range(8):
            far = levels[np.abs(levels - a[p, g]) >= 10]
            a[p, g + 8] = far[np.random.randint(len(far))]
    return np.exp2(a.ravel()).repeat(32)


def f64(x):
    return np.asarray(x).astype(np.float64)


def striped(idx):
    return np.tile(idx.reshape(-1, 16).T, (8, 1)).astype(np.uint16)


def unstriped(offs):
    return offs[:16].T.reshape(-1).astype(np.int64)


E2M1 = np.array([0.0, 0.5, 1.0, 1.5, 2.0, 3.0, 4.0, 6.0, -0.0, -0.5, -1.0, -1.5, -2.0, -3.0, -4.0, -6.0])


def pack_weight(w, fmt):
    k, n = w.shape
    w = f64(np.asarray(w, np.float32).astype(ml_dtypes.bfloat16)).reshape(k // 32, 32, n)
    amax = np.abs(w).max(1)
    if fmt == "e4m3":
        byte = np.frexp(amax)[1] - 1 + 127 - 7
    else:
        mant, ex = np.frexp(amax / 6.0)
        byte = np.where(mant > 0.5, ex, ex - 1) + 127
    byte = np.clip(np.where(amax > 0, byte, 1), 1, 254)
    scaled = (w * np.exp2(127.0 - byte)[:, None, :]).reshape(k, n).astype(np.float32)
    by_word = np.ascontiguousarray(scaled.reshape(k // 512, 128, 4, n).transpose(0, 1, 3, 2))
    if fmt == "e4m3":
        words = by_word.astype(ml_dtypes.float8_e4m3fn).view(np.uint8)
    else:
        c = by_word.astype(ml_dtypes.float4_e2m1fn).view(np.uint8) & 0xF
        words = (c[..., 0::2] | (c[..., 1::2] << 4)).reshape(k // 512, 128, 2 * n)
    return np.ascontiguousarray(words), np.ascontiguousarray(byte.astype(np.uint8).reshape(k // 512, 16, n))


def unpack_weight(words, scales, fmt):
    g, _, n = scales.shape
    words = np.ascontiguousarray(words).reshape(g, 128, n, -1)
    if fmt == "e4m3":
        vals = words.view(ml_dtypes.float8_e4m3fn).astype(np.float64)
    else:
        nib = np.empty((g, 128, n, 4), np.uint8)
        nib[..., 0::2] = words & 0xF
        nib[..., 1::2] = words >> 4
        vals = E2M1[nib]
    vals = vals * np.repeat(np.exp2(scales.astype(np.float64) - 127.0), 8, axis=1)[..., None]
    return vals.transpose(0, 1, 3, 2).reshape(g * 512, n)


def gelu(v):
    return 0.5 * v * (1.0 + np.tanh(np.sqrt(2.0 / np.pi) * (v + 0.044715 * v**3)))


def bf(x):
    return np.asarray(x, np.float32).astype(ml_dtypes.bfloat16)

def planes(Y):
    n, m = Y.shape
    b = f64(bf(Y)).reshape(n // 32, 32, m)
    amax = np.abs(b).max(1)
    byte = np.clip(np.where(amax > 0, np.frexp(amax)[1] - 1 + 127 - 7, 1), 1, 254)
    codes = (b * np.exp2(127.0 - byte)[:, None, :]).reshape(n, m).astype(np.float32).astype(ml_dtypes.float8_e4m3fn).view(np.uint8)
    words = codes.reshape(n // 512, 128, 4, m).transpose(0, 1, 3, 2)
    return np.ascontiguousarray(words), np.ascontiguousarray(byte.astype(np.uint8).reshape(n // 512, 16, m))


K, K2, T, T2, S, H, N = 1024, 512, 2048, 4096, 1024, 1024, 512

def setup_inputs():
    n = np.random.standard_normal
    s = mx_kscale(K)[:, None]
    s2 = mx_kscale(K2)[:, None]
    u = mx_kscale(H)[:, None]
    tab_words, tab_scales = pack_weight(n((K, T)) * s, "e4m3")
    tab2_words, tab2_scales = pack_weight(n((K2, T2)) * s2, "e4m3")
    w1 = n((K, H)) / np.sqrt(K) / s
    w2_words, w2_scales = pack_weight(n((K2, H)) / np.sqrt(K2) / s2, "e2m1")
    wc = n((H, N)) / np.sqrt(H) / u
    return {
        "tab_words": tab_words, "tab_scales": tab_scales,
        "tab2_words": tab2_words, "tab2_scales": tab2_scales,
        "offs": striped(np.random.permutation(T)[:S]),
        "offs2": striped(np.random.permutation(T2)[:S]),
        "w1": w1.astype(np.float32),
        "w2_words": w2_words, "w2_scales": w2_scales,
        "wc": wc.astype(np.float32),
        "gmax": (np.exp(0.3 * n(H)) * u[:, 0]).astype(np.float32),
        "vm": n((H, S)).astype(np.float32),
        "cinv": np.exp(0.8 * n(N)).astype(np.float32),
    }

def reference(tab_words, tab_scales, tab2_words, tab2_scales, offs, offs2, w1, w2_words, w2_scales, wc, gmax, vm, cinv):
    v = unpack_weight(tab_words, tab_scales, "e4m3")[:, unstriped(offs)]
    v2 = unpack_weight(tab2_words, tab2_scales, "e4m3")[:, unstriped(offs2)]
    a = mxq(f64(w1), 0, "e4m3").T @ v
    e = unpack_weight(w2_words, w2_scales, "e2m1").T @ v2
    g = f64(gmax)[:, None] * (1.0 / (1.0 + np.exp(-a)))
    cur = g * (f64(vm) - e)
    c = mxq(f64(wc), 0, "e4m3").T @ mxq(cur, 0, "e4m3")
    y = f64(cinv)[:, None] * c
    words, scales = planes(y)
    return y, words, scales

@@ -1,0 +1,277 @@
+from contextlib import ExitStack
+
+import concourse.mybir as mybir
+
+K, K2, T, T2, S, H, N = 1024, 512, 2048, 4096, 1024, 1024, 512
+FLOPS = 2 * (K * H * S + K2 * H * S + H * N * S)
+
+F32 = mybir.dt.float32
+BF16 = mybir.dt.bfloat16
+I32 = mybir.dt.int32
+U32 = mybir.dt.uint32
+U16 = mybir.dt.uint16
+U8 = mybir.dt.uint8
+E4M3 = mybir.dt.float8_e4m3fn_x4
+E2M1 = mybir.dt.float4_e2m1fn_x4
+ALU = mybir.AluOpType
+ACT = mybir.ActivationFunctionType
+
+P = 128
+PASS = 512
+CHUNKS = (((0, 256), (256, 256), (512, 512)), ((0, 512), (512, 256), (768, 256)))
+HALF = S // 2
+
+
+def tile_list_coupled_ionic_current_kernel(
+    tc, tab_words, tab_scales, tab2_words, tab2_scales, offs, offs2, w1, w2_words, w2_scales, wc, gmax, vm, cinv,
+    out_0, out_1, out_2,
+):
+    nc = tc.nc
+    small_q = nc.sync
+    with ExitStack() as ctx:
+        keep = ctx.enter_context(tc.tile_pool(name="keep", bufs=1))
+        ring = ctx.enter_context(tc.tile_pool(name="ring", bufs=2))
+        psum = ctx.enter_context(tc.psum_pool(name="psum", bufs=1))
+
+        def held(name, shape, dtype):
+            return keep.tile(shape, dtype, name=name, align_bytes=64)
+
+        idx = held("idx", [P, S // 16], U16)
+        idx2 = held("idx2", [P, S // 16], U16)
+        v_table = [held("v_table%d" % a, [P, T], I32) for a in range(2)]
+        v_table_scales = held("v_table_scales", [P, T], U8)
+        v2_table = held("v2_table", [P, T2], I32)
+        v2_table_scales = held("v2_table_scales", [P, T2], U8)
+        w2_raw = held("w2_raw", [P, 2 * H], U8)
+        w2_raw_scales = held("w2_raw_scales", [P, H], U8)
+        w2_codes = held("w2_codes", [P, 2 * H], U8)
+        w2_plane = held("w2_plane", [P, H], U8)
+        v_codes = [held("v_codes%d" % a, [P, S], U32) for a in range(2)]
+        v_planes = held("v_planes", [P, S], U8)
+        v2_codes = [held("v2_codes%d" % h, [P, HALF], U32) for h in range(2)]
+        v2_plane = held("v2_plane", [P, S], U8)
+        gain = held("gain", [P, 2, 4], F32)
+        neg_gain = held("neg_gain", [P, 2, 4], F32)
+        inv_cap = held("inv_cap", [P, 4], F32)
+        warm = held("warm", [P, 8], F32)
+        w1_raw = {
+            (a, b): ring.tile([P, 4, PASS], F32, name="w1_raw%d%d" % (a, b), tag="rows", align_bytes=64, bufs=4)
+            for b in range(2)
+            for a in range(2)
+        }
+        wc_raw = [held("wc_raw%d" % b, [P, 4, N], F32) for b in range(2)]
+        w1_codes = {ab: held("w1_codes%d%d" % ab, [P, PASS], U32) for ab in w1_raw}
+        w1_plane = {ab: held("w1_plane%d%d" % ab, [P, PASS], U8) for ab in w1_raw}
+        wc_codes = [held("wc_codes%d" % b, [P, N], U32) for b in range(2)]
+        wc_plane = [held("wc_plane%d" % b, [P, N], U8) for b in range(2)]
+        drive = {
+            (c, b): held("drive%d%d" % (c, b), [P, 4, w], F32) for b in range(2) for c, (j0, w) in enumerate(CHUNKS[b])
+        }
+        y_codes = [held("y_codes%d" % c, [P, w], U32) for c, (j0, w) in enumerate(CHUNKS[1])]
+        cur_codes = [held("cur_codes%d" % b, [P, S], U32) for b in range(2)]
+        cur_plane = [held("cur_plane%d" % b, [P, S], U8) for b in range(2)]
+        y_plane = held("y_plane", [P, S], U8)
+
+        def load_words(tile, words):
+            nc.sync.dma_start(out=tile[:], in_=words.rearrange("p t i -> p (t i)").bitcast(I32))
+
+        def load_plane(tile, scales, first_row):
+            rows = 4 * scales.shape[0]
+            for q in range(4):
+                p0 = 32 * q + first_row
+                small_q.dma_start(
+                    out=tile[p0 : p0 + rows, :].bitcast(I32), in_=scales[:, 4 * q : 4 * q + 4, :].bitcast(I32)
+                )
+
+        def load_rows(tile, rows):
+            nc.sync.dma_start(out=tile[:], in_=rows.rearrange("(p t) n -> p t n", t=4))
+
+        def load_w1(a, b):
+            load_rows(w1_raw[a, b], w1[PASS * a : PASS * (a + 1), PASS * b : PASS * (b + 1)])
+
+        def load_vm(c, b):
+            j0, w = CHUNKS[b][c]
+            load_rows(drive[c, b], vm[PASS * b : PASS * (b + 1), j0 : j0 + w])
+
+        def round_weight(raw, on_vector):
+            grouped = ring.tile([P, 4 * PASS], BF16, name="grouped", align_bytes=64, bufs=3)
+            dst = grouped[:].rearrange("p (t m i) -> p m i t", t=4, i=4)
+            src = raw[:].rearrange("p i (m t) -> p m i t", t=4)
+            if on_vector:
+                nc.vector.tensor_copy(out=dst, in_=src)
+            else:
+                nc.scalar.copy(out=dst, in_=src)
+            return grouped
+
+        def quantize(grouped, codes, plane):
+            nc.vector.quantize_mx(out=codes[:].bitcast(E4M3), scales=plane[:], in_=grouped[:])
+
+        def quantize_weight(raw, codes, plane, on_vector):
+            quantize(round_weight(raw, on_vector), codes, plane)
+
+        def gather(dst, table, offsets):
+            nc.vector.tensor_copy(out=dst, in_=table.indirect(offsets))
+
+        nc.vector.memset(warm[:], 0.0)
+        nc.scalar.activation(out=warm[:, 4:8], in_=warm[:, 0:4], func=ACT.Sigmoid)
+        for tile in (v_table_scales, v2_table_scales, w2_raw_scales):
+            nc.vector.memset(tile[:].bitcast(I32), 0)
+
+        nc.sync.dma_start(idx[:], offs)
+        load_words(v_table[0], tab_words[0])
+        load_plane(v_table_scales, tab_scales, 4)
+        load_w1(0, 0)
+        nc.sync.dma_start(idx2[:], offs2)
+        load_plane(v2_table_scales, tab2_scales, 0)
+        nc.sync.dma_start(out=w2_raw[:].bitcast(I32), in_=w2_words[0].bitcast(I32))
+        load_plane(w2_raw_scales, w2_scales, 0)
+        small_q.dma_start(out=gain[:], in_=gmax.rearrange("(b p t) -> p b t", b=2, t=4))
+        load_words(v_table[1], tab_words[1])
+        load_w1(1, 0)
+        load_words(v2_table, tab2_words[0])
+        load_vm(0, 0)
+        load_vm(1, 0)
+        load_w1(0, 1)
+        load_vm(2, 0)
+        load_w1(1, 1)
+        load_rows(wc_raw[0], wc[0:PASS, :])
+        load_vm(0, 1)
+        load_rows(wc_raw[1], wc[PASS:H, :])
+        small_q.dma_start(out=inv_cap[:], in_=cinv.rearrange("(p t) -> p t", t=4))
+        for c in range(1, len(CHUNKS[1])):
+            load_vm(c, 1)
+
+        gather(v_codes[0][:], v_table[0][:].bitcast(U32), idx[:])
+        gather(v_planes[:], v_table_scales[:], idx[:])
+        gather(v2_plane[:], v2_table_scales[:], idx2[:])
+        nc.vector.tensor_copy(
+            out=w2_codes[:].bitcast(U16).rearrange("p (b t m) -> p b m t", b=2, t=4),
+            in_=w2_raw[:].bitcast(U16).rearrange("p (b m t) -> p b m t", b=2, t=4),
+        )
+        nc.vector.tensor_copy(
+            out=w2_plane[:].rearrange("p (b t m) -> p b m t", b=2, t=4),
+            in_=w2_raw_scales[:].rearrange("p (b m t) -> p b m t", b=2, t=4),
+        )
+        nc.vector.tensor_scalar(
+            out=neg_gain[:], in0=gain[:], scalar1=-1.0, scalar2=None, op0=ALU.mult
+        )
+        quantize_weight(w1_raw[0, 0], w1_codes[0, 0], w1_plane[0, 0], False)
+        quantize_weight(w1_raw[1, 0], w1_codes[1, 0], w1_plane[1, 0], False)
+        gather(v_codes[1][:], v_table[1][:].bitcast(U32), idx[:])
+        gather(v2_codes[0][:], v2_table[:].bitcast(U32), idx2[:, 0 : HALF // 16])
+
+        def first_stage(c, b):
+            j0, w = CHUNKS[b][c]
+            cols = slice(j0, j0 + w)
+            h, h0 = divmod(j0, HALF)
+            d = drive[c, b]
+            opened = ring.tile([P, 4, w], F32, name="opened", align_bytes=64, bufs=3)
+            for t in range(4):
+                m = slice(P * t, P * (t + 1))
+                gained = ring.tile([P, w], F32, name="gained", align_bytes=64, bufs=6)
+                nc.gpsimd.tensor_scalar(
+                    out=gained[:], in0=d[:, t, :], scalar1=gain[:, b, t : t + 1], scalar2=0.0,
+                    op0=ALU.mult, op1=ALU.add,
+                )
+                a_bank = psum.tile([P, PASS], F32, name="a_bank", bufs=2)
+                for a in range(2):
+                    nc.tensor.matmul_mx(
+                        out=a_bank[:, 0:w],
+                        lhsT=w1_codes[a, b][:, m].bitcast(E4M3),
+                        lhsT_scale=w1_plane[a, b][:, m],
+                        rhs=v_codes[a][:, cols].bitcast(E4M3),
+                        rhs_scale=v_planes[4 + 4 * a : P, cols],
+                        start=(a == 0),
+                        stop=(a == 1),
+                    )
+                e_bank = psum.tile([P, PASS], F32, name="e_bank", bufs=2)
+                r0 = PASS * b + P * t
+                nc.tensor.matmul_mx(
+                    out=e_bank[:, 0:w],
+                    lhsT=w2_codes[:, 2 * r0 : 2 * (r0 + P)].bitcast(E2M1),
+                    lhsT_scale=w2_plane[:, r0 : r0 + P],
+                    rhs=v2_codes[h][:, h0 : h0 + w].bitcast(E4M3),
+                    rhs_scale=v2_plane[:, cols],
+                    start=True,
+                    stop=True,
+                )
+                nc.scalar.activation(out=opened[:, t, :], in_=a_bank[:, 0:w], func=ACT.Sigmoid)
+                nc.vector.scalar_tensor_tensor(
+                    out=d[:, t, :], in0=e_bank[:, 0:w], scalar=neg_gain[:, b, t : t + 1], in1=gained[:],
+                    op0=ALU.mult, op1=ALU.add,
+                )
+            rounded = ring.tile([P, 4 * w], BF16, name="rounded", align_bytes=64)
+            nc.vector.tensor_tensor(
+                out=rounded[:].rearrange("p (x i t) -> p x t i", t=4, i=4),
+                in0=opened[:].rearrange("p t (x i) -> p x t i", i=4),
+                in1=d[:].rearrange("p t (x i) -> p x t i", i=4),
+                op=ALU.mult,
+            )
+            nc.vector.quantize_mx(out=cur_codes[b][:, cols].bitcast(E4M3), scales=cur_plane[b][:, cols], in_=rounded[:])
+
+        def second_stage(c):
+            j0, w = CHUNKS[1][c]
+            cols = slice(j0, j0 + w)
+            banks = [psum.tile([P, PASS], F32, name="c_bank%d" % t) for t in range(4)]
+            for b in range(2):
+                for t in range(4):
+                    m = slice(P * t, P * (t + 1))
+                    nc.tensor.matmul_mx(
+                        out=banks[t][:, 0:w],
+                        lhsT=wc_codes[b][:, m].bitcast(E4M3),
+                        lhsT_scale=wc_plane[b][:, m],
+                        rhs=cur_codes[b][:, cols].bitcast(E4M3),
+                        rhs_scale=cur_plane[b][:, cols],
+                        start=(b == 0),
+                        stop=(b == 1),
+                    )
+            y = ring.tile([P, 4, w], F32, name="y", tag="rows", align_bytes=64, bufs=4)
+            last = c == len(CHUNKS[1]) - 1
+            for t in range(4):
+                if last and t % 2 == 1:
+                    nc.vector.tensor_scalar(
+                        out=y[:, t, :], in0=banks[t][:, 0:w], scalar1=inv_cap[:, t : t + 1], scalar2=None,
+                        op0=ALU.mult,
+                    )
+                else:
+                    nc.scalar.activation(
+                        out=y[:, t, :], in_=banks[t][:, 0:w], func=ACT.Copy, scale=inv_cap[:, t : t + 1]
+                    )
+            nc.sync.dma_start(out=out_0[:, j0 : j0 + w].rearrange("(p t) j -> p t j", t=4), in_=y[:])
+            y_rounded = ring.tile([P, 4 * w], BF16, name="y_rounded", align_bytes=64)
+            dst = y_rounded[:].rearrange("p (x i t) -> p x t i", t=4, i=4)
+            src = y[:].rearrange("p t (x i) -> p x t i", i=4)
+            if c in (0,):
+                nc.scalar.copy(out=dst, in_=src)
+            else:
+                nc.vector.tensor_copy(out=dst, in_=src)
+            nc.vector.quantize_mx(
+                out=y_codes[c][:].bitcast(E4M3), scales=y_plane[:, j0 : j0 + w], in_=y_rounded[:]
+            )
+            nc.sync.dma_start(
+                out=out_1[0].rearrange("p m t -> p (m t)")[:, 4 * j0 : 4 * (j0 + w)].bitcast(I32),
+                in_=y_codes[c][:].bitcast(I32),
+            )
+
+        first_stage(0, 0)
+        first_stage(1, 0)
+        gather(v2_codes[1][:], v2_table[:].bitcast(U32), idx2[:, HALF // 16 : S // 16])
+        grouped01 = round_weight(w1_raw[0, 1], False)
+        first_stage(2, 0)
+        quantize(grouped01, w1_codes[0, 1], w1_plane[0, 1])
+        quantize_weight(w1_raw[1, 1], w1_codes[1, 1], w1_plane[1, 1], False)
+        grouped_c0 = round_weight(wc_raw[0], False)
+        first_stage(0, 1)
+        quantize(grouped_c0, wc_codes[0], wc_plane[0])
+        quantize_weight(wc_raw[1], wc_codes[1], wc_plane[1], False)
+        first_stage(1, 1)
+        first_stage(2, 1)
+        second_stage(0)
+        second_stage(1)
+        second_stage(2)
+
+        for q in range(4):
+            queue = nc.sync if q % 2 == 0 else nc.scalar
+            queue.dma_start(
+                out=out_2[0, 4 * q : 4 * q + 4, :].bitcast(I32), in_=y_plane[32 * q : 32 * q + 4, :].bitcast(I32)
+            )

@@ -18,7 +18,7 @@ ACT = mybir.ActivationFunctionType
 
 P = 128
 PASS = 512
-CHUNKS = (((0, 256), (256, 256), (512, 512)), ((0, 512), (512, 256), (768, 256)))
+CHUNKS = ((0, 512), (512, 256), (768, 256))
 HALF = S // 2
 
 
@@ -51,7 +51,6 @@ def tile_list_coupled_ionic_current_kernel(
         v2_codes = [held("v2_codes%d" % h, [P, HALF], U32) for h in range(2)]
         v2_plane = held("v2_plane", [P, S], U8)
         gain = held("gain", [P, 2, 4], F32)
-        neg_gain = held("neg_gain", [P, 2, 4], F32)
         inv_cap = held("inv_cap", [P, 4], F32)
         warm = held("warm", [P, 8], F32)
         w1_raw = {
@@ -64,10 +63,11 @@ def tile_list_coupled_ionic_current_kernel(
         w1_plane = {ab: held("w1_plane%d%d" % ab, [P, PASS], U8) for ab in w1_raw}
         wc_codes = [held("wc_codes%d" % b, [P, N], U32) for b in range(2)]
         wc_plane = [held("wc_plane%d" % b, [P, N], U8) for b in range(2)]
-        drive = {
-            (c, b): held("drive%d%d" % (c, b), [P, 4, w], F32) for b in range(2) for c, (j0, w) in enumerate(CHUNKS[b])
-        }
-        y_codes = [held("y_codes%d" % c, [P, w], U32) for c, (j0, w) in enumerate(CHUNKS[1])]
+        drive = [held("drive%d" % b, [P, 4, S], F32) for b in range(2)]
+
+        def staged(name, slot, shape, dtype):
+            return ring.tile(shape, dtype, name=name, tag=slot, align_bytes=64, bufs=1)
+        y_codes = [held("y_codes%d" % c, [P, w], U32) for c, (j0, w) in enumerate(CHUNKS)]
         cur_codes = [held("cur_codes%d" % b, [P, S], U32) for b in range(2)]
         cur_plane = [held("cur_plane%d" % b, [P, S], U8) for b in range(2)]
         y_plane = held("y_plane", [P, S], U8)
@@ -83,19 +83,29 @@ def tile_list_coupled_ionic_current_kernel(
                     out=tile[p0 : p0 + rows, :].bitcast(I32), in_=scales[:, 4 * q : 4 * q + 4, :].bitcast(I32)
                 )
 
-        def load_rows(tile, rows):
-            nc.sync.dma_start(out=tile[:], in_=rows.rearrange("(p t) n -> p t n", t=4))
+        def load_rows(tile, rows, step):
+            dealt = rows.rearrange("(p t) n -> p t n", t=4)
+            for t in range(0, 4, step):
+                nc.sync.dma_start(out=tile[:, t : t + step, :], in_=dealt[:, t : t + step, :])
 
         def load_w1(a, b):
-            load_rows(w1_raw[a, b], w1[PASS * a : PASS * (a + 1), PASS * b : PASS * (b + 1)])
+            load_rows(w1_raw[a, b][:], w1[PASS * a : PASS * (a + 1), PASS * b : PASS * (b + 1)], 4)
 
-        def load_vm(c, b):
-            j0, w = CHUNKS[b][c]
-            load_rows(drive[c, b], vm[PASS * b : PASS * (b + 1), j0 : j0 + w])
+        def load_vm(b, cols):
+            load_rows(drive[b][:, :, cols], vm[PASS * b : PASS * (b + 1), cols], 4)
 
-        def round_weight(raw, on_vector):
-            grouped = ring.tile([P, 4 * PASS], BF16, name="grouped", align_bytes=64, bufs=3)
-            dst = grouped[:].rearrange("p (t m i) -> p m i t", t=4, i=4)
+        def apply_gain(b, t, d, engine):
+            if engine == "scalar":
+                nc.scalar.activation(out=d, in_=d, func=ACT.Copy, scale=gain[:, b, t : t + 1])
+            elif engine == "vector":
+                nc.vector.tensor_scalar(out=d, in0=d, scalar1=gain[:, b, t : t + 1], scalar2=None, op0=ALU.mult)
+            else:
+                nc.gpsimd.tensor_scalar(
+                    out=d, in0=d, scalar1=gain[:, b, t : t + 1], scalar2=0.0, op0=ALU.mult, op1=ALU.add
+                )
+
+        def round_weight(raw, grouped, on_vector):
+            dst = grouped.rearrange("p (t m i) -> p m i t", t=4, i=4)
             src = raw[:].rearrange("p i (m t) -> p m i t", t=4)
             if on_vector:
                 nc.vector.tensor_copy(out=dst, in_=src)
@@ -104,10 +114,7 @@ def tile_list_coupled_ionic_current_kernel(
             return grouped
 
         def quantize(grouped, codes, plane):
-            nc.vector.quantize_mx(out=codes[:].bitcast(E4M3), scales=plane[:], in_=grouped[:])
-
-        def quantize_weight(raw, codes, plane, on_vector):
-            quantize(round_weight(raw, on_vector), codes, plane)
+            nc.vector.quantize_mx(out=codes[:].bitcast(E4M3), scales=plane[:], in_=grouped)
 
         def gather(dst, table, offsets):
             nc.vector.tensor_copy(out=dst, in_=table.indirect(offsets))
@@ -120,26 +127,24 @@ def tile_list_coupled_ionic_current_kernel(
         nc.sync.dma_start(idx[:], offs)
         load_words(v_table[0], tab_words[0])
         load_plane(v_table_scales, tab_scales, 4)
-        load_w1(0, 0)
         nc.sync.dma_start(idx2[:], offs2)
         load_plane(v2_table_scales, tab2_scales, 0)
+        load_w1(0, 0)
+        load_w1(1, 0)
+        load_words(v_table[1], tab_words[1])
         nc.sync.dma_start(out=w2_raw[:].bitcast(I32), in_=w2_words[0].bitcast(I32))
         load_plane(w2_raw_scales, w2_scales, 0)
         small_q.dma_start(out=gain[:], in_=gmax.rearrange("(b p t) -> p b t", b=2, t=4))
-        load_words(v_table[1], tab_words[1])
-        load_w1(1, 0)
         load_words(v2_table, tab2_words[0])
-        load_vm(0, 0)
-        load_vm(1, 0)
+        load_vm(0, slice(0, HALF))
+        load_vm(0, slice(HALF, S))
         load_w1(0, 1)
-        load_vm(2, 0)
         load_w1(1, 1)
-        load_rows(wc_raw[0], wc[0:PASS, :])
-        load_vm(0, 1)
-        load_rows(wc_raw[1], wc[PASS:H, :])
+        load_vm(1, slice(0, HALF))
+        load_rows(wc_raw[0][:], wc[0:PASS, :], 4)
+        load_rows(wc_raw[1][:], wc[PASS:H, :], 4)
+        load_vm(1, slice(HALF, S))
         small_q.dma_start(out=inv_cap[:], in_=cinv.rearrange("(p t) -> p t", t=4))
-        for c in range(1, len(CHUNKS[1])):
-            load_vm(c, 1)
 
         gather(v_codes[0][:], v_table[0][:].bitcast(U32), idx[:])
         gather(v_planes[:], v_table_scales[:], idx[:])
@@ -152,28 +157,17 @@ def tile_list_coupled_ionic_current_kernel(
             out=w2_plane[:].rearrange("p (b t m) -> p b m t", b=2, t=4),
             in_=w2_raw_scales[:].rearrange("p (b m t) -> p b m t", b=2, t=4),
         )
-        nc.vector.tensor_scalar(
-            out=neg_gain[:], in0=gain[:], scalar1=-1.0, scalar2=None, op0=ALU.mult
-        )
-        quantize_weight(w1_raw[0, 0], w1_codes[0, 0], w1_plane[0, 0], False)
-        quantize_weight(w1_raw[1, 0], w1_codes[1, 0], w1_plane[1, 0], False)
-        gather(v_codes[1][:], v_table[1][:].bitcast(U32), idx[:])
-        gather(v2_codes[0][:], v2_table[:].bitcast(U32), idx2[:, 0 : HALF // 16])
 
-        def first_stage(c, b):
-            j0, w = CHUNKS[b][c]
+        opened = {}
+
+        def open_fraction(b, j0, w, slot, gain_engine):
             cols = slice(j0, j0 + w)
-            h, h0 = divmod(j0, HALF)
-            d = drive[c, b]
-            opened = ring.tile([P, 4, w], F32, name="opened", align_bytes=64, bufs=3)
+            tile = staged("opened", slot, [P, 4, w], F32)
+            for x in range(0, w, 128):
+                opened[b, j0 + x] = (tile, x)
             for t in range(4):
                 m = slice(P * t, P * (t + 1))
-                gained = ring.tile([P, w], F32, name="gained", align_bytes=64, bufs=6)
-                nc.gpsimd.tensor_scalar(
-                    out=gained[:], in0=d[:, t, :], scalar1=gain[:, b, t : t + 1], scalar2=0.0,
-                    op0=ALU.mult, op1=ALU.add,
-                )
-                a_bank = psum.tile([P, PASS], F32, name="a_bank", bufs=2)
+                a_bank = psum.tile([P, PASS], F32, name="a_bank", tag="bank", bufs=8)
                 for a in range(2):
                     nc.tensor.matmul_mx(
                         out=a_bank[:, 0:w],
@@ -184,40 +178,61 @@ def tile_list_coupled_ionic_current_kernel(
                         start=(a == 0),
                         stop=(a == 1),
                     )
-                e_bank = psum.tile([P, PASS], F32, name="e_bank", bufs=2)
+                nc.scalar.activation(out=tile[:, t, :], in_=a_bank[:, 0:w], func=ACT.Sigmoid)
+            for t in range(4):
+                apply_gain(b, t, tile[:, t, :], gain_engine)
+
+        def driving_force(b, h):
+            cols = slice(HALF * h, HALF * (h + 1))
+            for t in range(4):
+                d = drive[b][:, t, cols]
+                e_bank = psum.tile([P, PASS], F32, name="e_bank", tag="bank", bufs=8)
                 r0 = PASS * b + P * t
                 nc.tensor.matmul_mx(
-                    out=e_bank[:, 0:w],
+                    out=e_bank[:],
                     lhsT=w2_codes[:, 2 * r0 : 2 * (r0 + P)].bitcast(E2M1),
                     lhsT_scale=w2_plane[:, r0 : r0 + P],
-                    rhs=v2_codes[h][:, h0 : h0 + w].bitcast(E4M3),
+                    rhs=v2_codes[h][:].bitcast(E4M3),
                     rhs_scale=v2_plane[:, cols],
                     start=True,
                     stop=True,
                 )
-                nc.scalar.activation(out=opened[:, t, :], in_=a_bank[:, 0:w], func=ACT.Sigmoid)
-                nc.vector.scalar_tensor_tensor(
-                    out=d[:, t, :], in0=e_bank[:, 0:w], scalar=neg_gain[:, b, t : t + 1], in1=gained[:],
-                    op0=ALU.mult, op1=ALU.add,
-                )
-            rounded = ring.tile([P, 4 * w], BF16, name="rounded", align_bytes=64)
+                nc.vector.tensor_tensor(out=d, in0=d, in1=e_bank[:], op=ALU.subtract)
+
+        def current(b, j0, w, slot):
+            cols = slice(j0, j0 + w)
+            tile, x = opened[b, j0]
+            rounded = staged("rounded", slot, [P, 4 * w], BF16)
             nc.vector.tensor_tensor(
                 out=rounded[:].rearrange("p (x i t) -> p x t i", t=4, i=4),
-                in0=opened[:].rearrange("p t (x i) -> p x t i", i=4),
-                in1=d[:].rearrange("p t (x i) -> p x t i", i=4),
+                in0=tile[:, :, x : x + w].rearrange("p t (x i) -> p x t i", i=4),
+                in1=drive[b][:, :, cols].rearrange("p t (x i) -> p x t i", i=4),
                 op=ALU.mult,
             )
             nc.vector.quantize_mx(out=cur_codes[b][:, cols].bitcast(E4M3), scales=cur_plane[b][:, cols], in_=rounded[:])
 
+        def prepare_w1(a, b, slot, on_vector):
+            grouped = staged("grouped", slot, [P, 4 * PASS], BF16)
+            quantize(round_weight(w1_raw[a, b], grouped[:], on_vector), w1_codes[a, b], w1_plane[a, b])
+
+        def prepare_wc(b, slot, on_vector):
+            grouped = staged("grouped", slot, [P, 4 * PASS], BF16)
+            quantize(round_weight(wc_raw[b], grouped[:], on_vector), wc_codes[b], wc_plane[b])
+
+        def gather_v2(h):
+            gather(v2_codes[h][:], v2_table[:].bitcast(U32), idx2[:, h * HALF // 16 : (h + 1) * HALF // 16])
+
         def second_stage(c):
-            j0, w = CHUNKS[1][c]
+            j0, w = CHUNKS[c]
             cols = slice(j0, j0 + w)
-            banks = [psum.tile([P, PASS], F32, name="c_bank%d" % t) for t in range(4)]
-            for b in range(2):
-                for t in range(4):
-                    m = slice(P * t, P * (t + 1))
+            y = ring.tile([P, 4, w], F32, name="y", tag="rows", align_bytes=64, bufs=4)
+            last = c >= 2
+            for t in range(4):
+                m = slice(P * t, P * (t + 1))
+                c_bank = psum.tile([P, PASS], F32, name="c_bank", tag="bank", bufs=8)
+                for b in range(2):
                     nc.tensor.matmul_mx(
-                        out=banks[t][:, 0:w],
+                        out=c_bank[:, 0:w],
                         lhsT=wc_codes[b][:, m].bitcast(E4M3),
                         lhsT_scale=wc_plane[b][:, m],
                         rhs=cur_codes[b][:, cols].bitcast(E4M3),
@@ -225,17 +240,14 @@ def tile_list_coupled_ionic_current_kernel(
                         start=(b == 0),
                         stop=(b == 1),
                     )
-            y = ring.tile([P, 4, w], F32, name="y", tag="rows", align_bytes=64, bufs=4)
-            last = c == len(CHUNKS[1]) - 1
-            for t in range(4):
                 if last and t % 2 == 1:
                     nc.vector.tensor_scalar(
-                        out=y[:, t, :], in0=banks[t][:, 0:w], scalar1=inv_cap[:, t : t + 1], scalar2=None,
+                        out=y[:, t, :], in0=c_bank[:, 0:w], scalar1=inv_cap[:, t : t + 1], scalar2=None,
                         op0=ALU.mult,
                     )
                 else:
                     nc.scalar.activation(
-                        out=y[:, t, :], in_=banks[t][:, 0:w], func=ACT.Copy, scale=inv_cap[:, t : t + 1]
+                        out=y[:, t, :], in_=c_bank[:, 0:w], func=ACT.Copy, scale=inv_cap[:, t : t + 1]
                     )
             nc.sync.dma_start(out=out_0[:, j0 : j0 + w].rearrange("(p t) j -> p t j", t=4), in_=y[:])
             y_rounded = ring.tile([P, 4 * w], BF16, name="y_rounded", align_bytes=64)
@@ -253,20 +265,30 @@ def tile_list_coupled_ionic_current_kernel(
                 in_=y_codes[c][:].bitcast(I32),
             )
 
-        first_stage(0, 0)
-        first_stage(1, 0)
-        gather(v2_codes[1][:], v2_table[:].bitcast(U32), idx2[:, HALF // 16 : S // 16])
-        grouped01 = round_weight(w1_raw[0, 1], False)
-        first_stage(2, 0)
-        quantize(grouped01, w1_codes[0, 1], w1_plane[0, 1])
-        quantize_weight(w1_raw[1, 1], w1_codes[1, 1], w1_plane[1, 1], False)
-        grouped_c0 = round_weight(wc_raw[0], False)
-        first_stage(0, 1)
-        quantize(grouped_c0, wc_codes[0], wc_plane[0])
-        quantize_weight(wc_raw[1], wc_codes[1], wc_plane[1], False)
-        first_stage(1, 1)
-        first_stage(2, 1)
+        prepare_w1(0, 0, "g0", False)
+        prepare_w1(1, 0, "g1", False)
+        gather(v_codes[1][:, 0:HALF], v_table[1][:].bitcast(U32), idx[:, 0 : HALF // 16])
+        gather(v_codes[1][:, HALF:S], v_table[1][:].bitcast(U32), idx[:, HALF // 16 : S // 16])
+        open_fraction(0, 0, 512, "o0", "scalar")
+        gather_v2(0)
+        gather_v2(1)
+        driving_force(0, 0)
+        open_fraction(0, 512, 512, "o1", "scalar")
+        current(0, 0, 512, "r0")
+        prepare_w1(0, 1, "g0", False)
+        prepare_w1(1, 1, "g1", False)
+        driving_force(0, 1)
+        open_fraction(1, 0, 512, "o2", "vector")
+        current(0, 512, 512, "g1")
+        driving_force(1, 0)
+        prepare_wc(0, "g0", False)
+        open_fraction(1, 512, 512, "o0", "vector")
+        prepare_wc(1, "r0", False)
+        current(1, 0, 512, "r1")
+        driving_force(1, 1)
         second_stage(0)
+        current(1, 512, 256, "g0")
+        current(1, 768, 256, "g1")
         second_stage(1)
         second_stage(2)
 

@@ -17,9 +17,14 @@ ALU = mybir.AluOpType
 ACT = mybir.ActivationFunctionType
 
 P = 128
-PASS = 512
-CHUNKS = ((0, 512), (512, 256), (768, 256))
+PACK = 4
+PASS = P * PACK
+QUADRANT = 32
+BANKS = 8
 HALF = S // 2
+QUARTER = S // 4
+V_PLANE_ROW = 4
+OUT_RANGES = ((0, HALF), (HALF, QUARTER), (HALF + QUARTER, QUARTER))
 
 
 def tile_list_coupled_ionic_current_kernel(
@@ -27,7 +32,6 @@ def tile_list_coupled_ionic_current_kernel(
     out_0, out_1, out_2,
 ):
     nc = tc.nc
-    small_q = nc.sync
     with ExitStack() as ctx:
         keep = ctx.enter_context(tc.tile_pool(name="keep", bufs=1))
         ring = ctx.enter_context(tc.tile_pool(name="ring", bufs=2))
@@ -36,264 +40,260 @@ def tile_list_coupled_ionic_current_kernel(
         def held(name, shape, dtype):
             return keep.tile(shape, dtype, name=name, align_bytes=64)
 
+        def staged(name, slot, shape, dtype):
+            return ring.tile(shape, dtype, name=name, tag=slot, align_bytes=64, bufs=1)
+
+        def float_rows(name, width):
+            return ring.tile([P, PACK, width], F32, name=name, tag="float_rows", align_bytes=64, bufs=4)
+
+        def four_banks(name):
+            return [psum.tile([P, HALF], F32, name=name, tag="bank", bufs=BANKS) for t in range(PACK)]
+
         idx = held("idx", [P, S // 16], U16)
         idx2 = held("idx2", [P, S // 16], U16)
         v_table = [held("v_table%d" % a, [P, T], I32) for a in range(2)]
-        v_table_scales = held("v_table_scales", [P, T], U8)
+        v_table_planes = held("v_table_planes", [P, T], U8)
         v2_table = held("v2_table", [P, T2], I32)
-        v2_table_scales = held("v2_table_scales", [P, T2], U8)
+        v2_table_plane = held("v2_table_plane", [P, T2], U8)
         w2_raw = held("w2_raw", [P, 2 * H], U8)
-        w2_raw_scales = held("w2_raw_scales", [P, H], U8)
+        w2_raw_plane = held("w2_raw_plane", [P, H], U8)
         w2_codes = held("w2_codes", [P, 2 * H], U8)
         w2_plane = held("w2_plane", [P, H], U8)
         v_codes = [held("v_codes%d" % a, [P, S], U32) for a in range(2)]
         v_planes = held("v_planes", [P, S], U8)
         v2_codes = [held("v2_codes%d" % h, [P, HALF], U32) for h in range(2)]
         v2_plane = held("v2_plane", [P, S], U8)
-        gain = held("gain", [P, 2, 4], F32)
-        inv_cap = held("inv_cap", [P, 4], F32)
+        gain = held("gain", [P, 2, PACK], F32)
+        inv_cap = held("inv_cap", [P, PACK], F32)
         warm = held("warm", [P, 8], F32)
-        w1_raw = {
-            (a, b): ring.tile([P, 4, PASS], F32, name="w1_raw%d%d" % (a, b), tag="rows", align_bytes=64, bufs=4)
-            for b in range(2)
-            for a in range(2)
-        }
-        wc_raw = [held("wc_raw%d" % b, [P, 4, N], F32) for b in range(2)]
+        w1_raw = {(a, b): float_rows("w1_raw%d%d" % (a, b), PASS) for b in range(2) for a in range(2)}
+        wc_raw = [held("wc_raw%d" % b, [P, PACK, N], F32) for b in range(2)]
         w1_codes = {ab: held("w1_codes%d%d" % ab, [P, PASS], U32) for ab in w1_raw}
         w1_plane = {ab: held("w1_plane%d%d" % ab, [P, PASS], U8) for ab in w1_raw}
         wc_codes = [held("wc_codes%d" % b, [P, N], U32) for b in range(2)]
         wc_plane = [held("wc_plane%d" % b, [P, N], U8) for b in range(2)]
-        drive = [held("drive%d" % b, [P, 4, S], F32) for b in range(2)]
-
-        def staged(name, slot, shape, dtype):
-            return ring.tile(shape, dtype, name=name, tag=slot, align_bytes=64, bufs=1)
-        y_codes = [held("y_codes%d" % c, [P, w], U32) for c, (j0, w) in enumerate(CHUNKS)]
+        force = [held("force%d" % b, [P, PACK, S], F32) for b in range(2)]
+        y_codes = [held("y_codes%d" % c, [P, w], U32) for c, (j0, w) in enumerate(OUT_RANGES)]
         cur_codes = [held("cur_codes%d" % b, [P, S], U32) for b in range(2)]
         cur_plane = [held("cur_plane%d" % b, [P, S], U8) for b in range(2)]
         y_plane = held("y_plane", [P, S], U8)
+        conductance = {}
+
+        def half(h):
+            return slice(HALF * h, HALF * (h + 1))
 
         def load_words(tile, words):
             nc.sync.dma_start(out=tile[:], in_=words.rearrange("p t i -> p (t i)").bitcast(I32))
 
-        def load_plane(tile, scales, first_row):
-            rows = 4 * scales.shape[0]
+        def load_two_planes(tile, scales):
             for q in range(4):
-                p0 = 32 * q + first_row
-                small_q.dma_start(
-                    out=tile[p0 : p0 + rows, :].bitcast(I32), in_=scales[:, 4 * q : 4 * q + 4, :].bitcast(I32)
+                p0 = QUADRANT * q + V_PLANE_ROW
+                nc.sync.dma_start(
+                    out=tile[p0 : p0 + 8, :].bitcast(I32), in_=scales[:, 4 * q : 4 * q + 4, :].bitcast(I32)
                 )
 
-        def load_rows(tile, rows, step):
-            dealt = rows.rearrange("(p t) n -> p t n", t=4)
-            for t in range(0, 4, step):
-                nc.sync.dma_start(out=tile[:, t : t + step, :], in_=dealt[:, t : t + step, :])
+        def load_plane(tile, scales):
+            rows = scales.rearrange("(q r) n -> r q n", r=4)
+            for r in range(4):
+                nc.sync.dma_start(out=tile[r:P:QUADRANT, :].bitcast(I32), in_=rows[r].bitcast(I32))
+
+        def load_rows(tile, rows):
+            nc.sync.dma_start(out=tile, in_=rows.rearrange("(p t) n -> p t n", t=PACK))
 
         def load_w1(a, b):
-            load_rows(w1_raw[a, b][:], w1[PASS * a : PASS * (a + 1), PASS * b : PASS * (b + 1)], 4)
+            load_rows(w1_raw[a, b][:], w1[PASS * a : PASS * (a + 1), PASS * b : PASS * (b + 1)])
 
-        def load_vm(b, cols):
-            load_rows(drive[b][:, :, cols], vm[PASS * b : PASS * (b + 1), cols], 4)
+        def load_wc(b):
+            load_rows(wc_raw[b][:], wc[PASS * b : PASS * (b + 1), :])
 
-        def apply_gain(b, t, d, engine):
-            if engine == "scalar":
-                nc.scalar.activation(out=d, in_=d, func=ACT.Copy, scale=gain[:, b, t : t + 1])
-            elif engine == "vector":
-                nc.vector.tensor_scalar(out=d, in0=d, scalar1=gain[:, b, t : t + 1], scalar2=None, op0=ALU.mult)
-            else:
-                nc.gpsimd.tensor_scalar(
-                    out=d, in0=d, scalar1=gain[:, b, t : t + 1], scalar2=0.0, op0=ALU.mult, op1=ALU.add
-                )
-
-        def round_weight(raw, grouped, on_vector):
-            dst = grouped.rearrange("p (t m i) -> p m i t", t=4, i=4)
-            src = raw[:].rearrange("p i (m t) -> p m i t", t=4)
-            if on_vector:
-                nc.vector.tensor_copy(out=dst, in_=src)
-            else:
-                nc.scalar.copy(out=dst, in_=src)
-            return grouped
-
-        def quantize(grouped, codes, plane):
-            nc.vector.quantize_mx(out=codes[:].bitcast(E4M3), scales=plane[:], in_=grouped)
+        def load_vm(b, h):
+            load_rows(force[b][:, :, half(h)], vm[PASS * b : PASS * (b + 1), half(h)])
 
         def gather(dst, table, offsets):
             nc.vector.tensor_copy(out=dst, in_=table.indirect(offsets))
 
-        nc.vector.memset(warm[:], 0.0)
-        nc.scalar.activation(out=warm[:, 4:8], in_=warm[:, 0:4], func=ACT.Sigmoid)
-        for tile in (v_table_scales, v2_table_scales, w2_raw_scales):
-            nc.vector.memset(tile[:].bitcast(I32), 0)
+        def entries(offsets, h):
+            return offsets[:, h * HALF // 16 : (h + 1) * HALF // 16]
 
-        nc.sync.dma_start(idx[:], offs)
-        load_words(v_table[0], tab_words[0])
-        load_plane(v_table_scales, tab_scales, 4)
-        nc.sync.dma_start(idx2[:], offs2)
-        load_plane(v2_table_scales, tab2_scales, 0)
-        load_w1(0, 0)
-        load_w1(1, 0)
-        load_words(v_table[1], tab_words[1])
-        nc.sync.dma_start(out=w2_raw[:].bitcast(I32), in_=w2_words[0].bitcast(I32))
-        load_plane(w2_raw_scales, w2_scales, 0)
-        small_q.dma_start(out=gain[:], in_=gmax.rearrange("(b p t) -> p b t", b=2, t=4))
-        load_words(v2_table, tab2_words[0])
-        load_vm(0, slice(0, HALF))
-        load_vm(0, slice(HALF, S))
-        load_w1(0, 1)
-        load_w1(1, 1)
-        load_vm(1, slice(0, HALF))
-        load_rows(wc_raw[0][:], wc[0:PASS, :], 4)
-        load_rows(wc_raw[1][:], wc[PASS:H, :], 4)
-        load_vm(1, slice(HALF, S))
-        small_q.dma_start(out=inv_cap[:], in_=cinv.rearrange("(p t) -> p t", t=4))
+        def word_walk(side_by_side, by_rows):
+            return (
+                side_by_side.rearrange("p (x i t) -> p x t i", t=PACK, i=4),
+                [rows.rearrange("p t (x i) -> p x t i", i=4) for rows in by_rows],
+            )
 
-        gather(v_codes[0][:], v_table[0][:].bitcast(U32), idx[:])
-        gather(v_planes[:], v_table_scales[:], idx[:])
-        gather(v2_plane[:], v2_table_scales[:], idx2[:])
-        nc.vector.tensor_copy(
-            out=w2_codes[:].bitcast(U16).rearrange("p (b t m) -> p b m t", b=2, t=4),
-            in_=w2_raw[:].bitcast(U16).rearrange("p (b m t) -> p b m t", b=2, t=4),
-        )
-        nc.vector.tensor_copy(
-            out=w2_plane[:].rearrange("p (b t m) -> p b m t", b=2, t=4),
-            in_=w2_raw_scales[:].rearrange("p (b m t) -> p b m t", b=2, t=4),
-        )
+        def quantize_weight(raw, codes, plane, slot):
+            rounded = staged("weight_rounded", slot, [P, PACK * PASS], BF16)
+            nc.scalar.copy(
+                out=rounded[:].rearrange("p (t m i) -> p m i t", t=PACK, i=PACK),
+                in_=raw[:].rearrange("p i (m t) -> p m i t", t=PACK),
+            )
+            nc.vector.quantize_mx(out=codes[:].bitcast(E4M3), scales=plane[:], in_=rounded[:])
 
-        opened = {}
+        def quantize_w1(a, b, slot):
+            quantize_weight(w1_raw[a, b], w1_codes[a, b], w1_plane[a, b], slot)
 
-        def open_fraction(b, j0, w, slot, gain_engine):
-            cols = slice(j0, j0 + w)
-            tile = staged("opened", slot, [P, 4, w], F32)
-            for x in range(0, w, 128):
-                opened[b, j0 + x] = (tile, x)
-            for t in range(4):
-                m = slice(P * t, P * (t + 1))
-                a_bank = psum.tile([P, PASS], F32, name="a_bank", tag="bank", bufs=8)
-                for a in range(2):
+        def quantize_wc(b, slot):
+            quantize_weight(wc_raw[b], wc_codes[b], wc_plane[b], slot)
+
+        def make_conductance(b, h, slot):
+            tile = staged("conductance", slot, [P, PACK, HALF], F32)
+            conductance[b, h] = tile
+            banks = four_banks("a_bank")
+            for a in range(2):
+                for t in range(PACK):
+                    places = slice(P * t, P * (t + 1))
                     nc.tensor.matmul_mx(
-                        out=a_bank[:, 0:w],
-                        lhsT=w1_codes[a, b][:, m].bitcast(E4M3),
-                        lhsT_scale=w1_plane[a, b][:, m],
-                        rhs=v_codes[a][:, cols].bitcast(E4M3),
-                        rhs_scale=v_planes[4 + 4 * a : P, cols],
+                        out=banks[t][:],
+                        lhsT=w1_codes[a, b][:, places].bitcast(E4M3),
+                        lhsT_scale=w1_plane[a, b][:, places],
+                        rhs=v_codes[a][:, half(h)].bitcast(E4M3),
+                        rhs_scale=v_planes[V_PLANE_ROW + 4 * a : P, half(h)],
                         start=(a == 0),
                         stop=(a == 1),
                     )
-                nc.scalar.activation(out=tile[:, t, :], in_=a_bank[:, 0:w], func=ACT.Sigmoid)
-            for t in range(4):
-                apply_gain(b, t, tile[:, t, :], gain_engine)
+            for t in range(PACK):
+                nc.scalar.activation(out=tile[:, t, :], in_=banks[t][:], func=ACT.Sigmoid)
+            for t in range(PACK):
+                g, factor = tile[:, t, :], gain[:, b, t : t + 1]
+                if b == 0:
+                    nc.scalar.activation(out=g, in_=g, func=ACT.Copy, scale=factor)
+                else:
+                    nc.vector.tensor_scalar(out=g, in0=g, scalar1=factor, scalar2=None, op0=ALU.mult)
 
-        def driving_force(b, h):
-            cols = slice(HALF * h, HALF * (h + 1))
-            for t in range(4):
-                d = drive[b][:, t, cols]
-                e_bank = psum.tile([P, PASS], F32, name="e_bank", tag="bank", bufs=8)
-                r0 = PASS * b + P * t
+        def make_force(b, h):
+            banks = four_banks("e_bank")
+            for t in range(PACK):
+                place = PASS * b + P * t
                 nc.tensor.matmul_mx(
-                    out=e_bank[:],
-                    lhsT=w2_codes[:, 2 * r0 : 2 * (r0 + P)].bitcast(E2M1),
-                    lhsT_scale=w2_plane[:, r0 : r0 + P],
+                    out=banks[t][:],
+                    lhsT=w2_codes[:, 2 * place : 2 * (place + P)].bitcast(E2M1),
+                    lhsT_scale=w2_plane[:, place : place + P],
                     rhs=v2_codes[h][:].bitcast(E4M3),
-                    rhs_scale=v2_plane[:, cols],
+                    rhs_scale=v2_plane[:, half(h)],
                     start=True,
                     stop=True,
                 )
-                nc.vector.tensor_tensor(out=d, in0=d, in1=e_bank[:], op=ALU.subtract)
+                d = force[b][:, t, half(h)]
+                nc.vector.tensor_tensor(out=d, in0=d, in1=banks[t][:], op=ALU.subtract)
 
-        def current(b, j0, w, slot):
+        def make_current(b, j0, w, slot):
             cols = slice(j0, j0 + w)
-            tile, x = opened[b, j0]
-            rounded = staged("rounded", slot, [P, 4 * w], BF16)
-            nc.vector.tensor_tensor(
-                out=rounded[:].rearrange("p (x i t) -> p x t i", t=4, i=4),
-                in0=tile[:, :, x : x + w].rearrange("p t (x i) -> p x t i", i=4),
-                in1=drive[b][:, :, cols].rearrange("p t (x i) -> p x t i", i=4),
-                op=ALU.mult,
+            h, x0 = divmod(j0, HALF)
+            rounded = staged("cur_rounded", slot, [P, PACK * w], BF16)
+            dst, (g, d) = word_walk(rounded[:], [conductance[b, h][:, :, x0 : x0 + w], force[b][:, :, cols]])
+            nc.vector.tensor_tensor(out=dst, in0=g, in1=d, op=ALU.mult)
+            nc.vector.quantize_mx(
+                out=cur_codes[b][:, cols].bitcast(E4M3), scales=cur_plane[b][:, cols], in_=rounded[:]
             )
-            nc.vector.quantize_mx(out=cur_codes[b][:, cols].bitcast(E4M3), scales=cur_plane[b][:, cols], in_=rounded[:])
 
-        def prepare_w1(a, b, slot, on_vector):
-            grouped = staged("grouped", slot, [P, 4 * PASS], BF16)
-            quantize(round_weight(w1_raw[a, b], grouped[:], on_vector), w1_codes[a, b], w1_plane[a, b])
-
-        def prepare_wc(b, slot, on_vector):
-            grouped = staged("grouped", slot, [P, 4 * PASS], BF16)
-            quantize(round_weight(wc_raw[b], grouped[:], on_vector), wc_codes[b], wc_plane[b])
-
-        def gather_v2(h):
-            gather(v2_codes[h][:], v2_table[:].bitcast(U32), idx2[:, h * HALF // 16 : (h + 1) * HALF // 16])
-
-        def second_stage(c):
-            j0, w = CHUNKS[c]
+        def make_output(c):
+            j0, w = OUT_RANGES[c]
             cols = slice(j0, j0 + w)
-            y = ring.tile([P, 4, w], F32, name="y", tag="rows", align_bytes=64, bufs=4)
-            last = c >= 2
-            for t in range(4):
-                m = slice(P * t, P * (t + 1))
-                c_bank = psum.tile([P, PASS], F32, name="c_bank", tag="bank", bufs=8)
-                for b in range(2):
+            y = float_rows("y", w)
+            banks = four_banks("c_bank")
+            for b in range(2):
+                for t in range(PACK):
+                    places = slice(P * t, P * (t + 1))
                     nc.tensor.matmul_mx(
-                        out=c_bank[:, 0:w],
-                        lhsT=wc_codes[b][:, m].bitcast(E4M3),
-                        lhsT_scale=wc_plane[b][:, m],
+                        out=banks[t][:, 0:w],
+                        lhsT=wc_codes[b][:, places].bitcast(E4M3),
+                        lhsT_scale=wc_plane[b][:, places],
                         rhs=cur_codes[b][:, cols].bitcast(E4M3),
                         rhs_scale=cur_plane[b][:, cols],
                         start=(b == 0),
                         stop=(b == 1),
                     )
-                if last and t % 2 == 1:
+            shared = c == len(OUT_RANGES) - 1
+            for t in range(PACK):
+                factor = inv_cap[:, t : t + 1]
+                if shared and t % 2 == 1:
                     nc.vector.tensor_scalar(
-                        out=y[:, t, :], in0=c_bank[:, 0:w], scalar1=inv_cap[:, t : t + 1], scalar2=None,
-                        op0=ALU.mult,
+                        out=y[:, t, :], in0=banks[t][:, 0:w], scalar1=factor, scalar2=None, op0=ALU.mult
                     )
                 else:
-                    nc.scalar.activation(
-                        out=y[:, t, :], in_=c_bank[:, 0:w], func=ACT.Copy, scale=inv_cap[:, t : t + 1]
-                    )
-            nc.sync.dma_start(out=out_0[:, j0 : j0 + w].rearrange("(p t) j -> p t j", t=4), in_=y[:])
-            y_rounded = ring.tile([P, 4 * w], BF16, name="y_rounded", align_bytes=64)
-            dst = y_rounded[:].rearrange("p (x i t) -> p x t i", t=4, i=4)
-            src = y[:].rearrange("p t (x i) -> p x t i", i=4)
-            if c in (0,):
+                    nc.scalar.activation(out=y[:, t, :], in_=banks[t][:, 0:w], func=ACT.Copy, scale=factor)
+            nc.sync.dma_start(out=out_0[:, cols].rearrange("(p t) j -> p t j", t=PACK), in_=y[:])
+            rounded = ring.tile([P, PACK * w], BF16, name="y_rounded", align_bytes=64)
+            dst, (src,) = word_walk(rounded[:], [y[:]])
+            if c == 0:
                 nc.scalar.copy(out=dst, in_=src)
             else:
                 nc.vector.tensor_copy(out=dst, in_=src)
-            nc.vector.quantize_mx(
-                out=y_codes[c][:].bitcast(E4M3), scales=y_plane[:, j0 : j0 + w], in_=y_rounded[:]
-            )
+            nc.vector.quantize_mx(out=y_codes[c][:].bitcast(E4M3), scales=y_plane[:, cols], in_=rounded[:])
             nc.sync.dma_start(
-                out=out_1[0].rearrange("p m t -> p (m t)")[:, 4 * j0 : 4 * (j0 + w)].bitcast(I32),
+                out=out_1[0].rearrange("p m t -> p (m t)")[:, PACK * j0 : PACK * (j0 + w)].bitcast(I32),
                 in_=y_codes[c][:].bitcast(I32),
             )
 
-        prepare_w1(0, 0, "g0", False)
-        prepare_w1(1, 0, "g1", False)
-        gather(v_codes[1][:, 0:HALF], v_table[1][:].bitcast(U32), idx[:, 0 : HALF // 16])
-        gather(v_codes[1][:, HALF:S], v_table[1][:].bitcast(U32), idx[:, HALF // 16 : S // 16])
-        open_fraction(0, 0, 512, "o0", "scalar")
-        gather_v2(0)
-        gather_v2(1)
-        driving_force(0, 0)
-        open_fraction(0, 512, 512, "o1", "scalar")
-        current(0, 0, 512, "r0")
-        prepare_w1(0, 1, "g0", False)
-        prepare_w1(1, 1, "g1", False)
-        driving_force(0, 1)
-        open_fraction(1, 0, 512, "o2", "vector")
-        current(0, 512, 512, "g1")
-        driving_force(1, 0)
-        prepare_wc(0, "g0", False)
-        open_fraction(1, 512, 512, "o0", "vector")
-        prepare_wc(1, "r0", False)
-        current(1, 0, 512, "r1")
-        driving_force(1, 1)
-        second_stage(0)
-        current(1, 512, 256, "g0")
-        current(1, 768, 256, "g1")
-        second_stage(1)
-        second_stage(2)
+        nc.vector.memset(warm[:], 0.0)
+        nc.scalar.activation(out=warm[:, 4:8], in_=warm[:, 0:4], func=ACT.Sigmoid)
+        for tile in (v_table_planes, v2_table_plane, w2_raw_plane):
+            nc.vector.memset(tile[:].bitcast(I32), 0)
 
-        for q in range(4):
-            queue = nc.sync if q % 2 == 0 else nc.scalar
-            queue.dma_start(
-                out=out_2[0, 4 * q : 4 * q + 4, :].bitcast(I32), in_=y_plane[32 * q : 32 * q + 4, :].bitcast(I32)
-            )
+        nc.sync.dma_start(idx[:], offs)
+        load_words(v_table[0], tab_words[0])
+        load_two_planes(v_table_planes, tab_scales)
+        nc.sync.dma_start(idx2[:], offs2)
+        load_plane(v2_table_plane, tab2_scales[0])
+        load_w1(0, 0)
+        load_w1(1, 0)
+        load_words(v_table[1], tab_words[1])
+        nc.sync.dma_start(out=w2_raw[:].bitcast(I32), in_=w2_words[0].bitcast(I32))
+        load_plane(w2_raw_plane, w2_scales[0])
+        nc.sync.dma_start(out=gain[:], in_=gmax.rearrange("(b p t) -> p b t", b=2, t=PACK))
+        load_words(v2_table, tab2_words[0])
+        load_vm(0, 0)
+        load_vm(0, 1)
+        load_w1(0, 1)
+        load_w1(1, 1)
+        load_vm(1, 0)
+        load_wc(0)
+        load_wc(1)
+        load_vm(1, 1)
+        nc.sync.dma_start(out=inv_cap[:], in_=cinv.rearrange("(p t) -> p t", t=PACK))
+
+        gather(v_codes[0][:], v_table[0][:].bitcast(U32), idx[:])
+        gather(v_planes[:], v_table_planes[:], idx[:])
+        gather(v2_plane[:], v2_table_plane[:], idx2[:])
+        nc.vector.tensor_copy(
+            out=w2_codes[:].bitcast(U16).rearrange("p (b t m) -> p b m t", b=2, t=PACK),
+            in_=w2_raw[:].bitcast(U16).rearrange("p (b m t) -> p b m t", b=2, t=PACK),
+        )
+        nc.vector.tensor_copy(
+            out=w2_plane[:].rearrange("p (b t m) -> p b m t", b=2, t=PACK),
+            in_=w2_raw_plane[:].rearrange("p (b m t) -> p b m t", b=2, t=PACK),
+        )
+
+        quantize_w1(0, 0, "bf16_a")
+        quantize_w1(1, 0, "bf16_b")
+        for h in range(2):
+            gather(v_codes[1][:, half(h)], v_table[1][:].bitcast(U32), entries(idx, h))
+        make_conductance(0, 0, "f32_a")
+        for h in range(2):
+            gather(v2_codes[h][:], v2_table[:].bitcast(U32), entries(idx2, h))
+        make_force(0, 0)
+        make_conductance(0, 1, "f32_b")
+        make_current(0, 0, HALF, "bf16_c")
+        quantize_w1(0, 1, "bf16_a")
+        quantize_w1(1, 1, "bf16_b")
+        make_force(0, 1)
+        make_conductance(1, 0, "f32_c")
+        make_current(0, HALF, QUARTER, "bf16_d")
+        make_current(0, HALF + QUARTER, QUARTER, "bf16_b")
+
+        make_force(1, 0)
+        quantize_wc(0, "bf16_a")
+        make_conductance(1, 1, "f32_a")
+        quantize_wc(1, "bf16_c")
+        make_current(1, 0, HALF, "bf16_d")
+        make_force(1, 1)
+        make_output(0)
+        make_current(1, HALF, QUARTER, "bf16_a")
+        make_current(1, HALF + QUARTER, QUARTER, "bf16_b")
+        make_output(1)
+        make_output(2)
+
+        out_rows = out_2[0].rearrange("(q r) m -> r q m", r=4)
+        for r in range(4):
+            queue = nc.sync if r % 2 == 0 else nc.scalar
+            queue.dma_start(out=out_rows[r].bitcast(I32), in_=y_plane[r:P:QUADRANT, :].bitcast(I32))

@@ -65,7 +65,6 @@ def tile_list_coupled_ionic_current_kernel(
         v2_plane = held("v2_plane", [P, S], U8)
         gain = held("gain", [P, 2, PACK], F32)
         inv_cap = held("inv_cap", [P, PACK], F32)
-        warm = held("warm", [P, 8], F32)
         w1_raw = {(a, b): float_rows("w1_raw%d%d" % (a, b), PASS) for b in range(2) for a in range(2)}
         wc_raw = [held("wc_raw%d" % b, [P, PACK, N], F32) for b in range(2)]
         w1_codes = {ab: held("w1_codes%d%d" % ab, [P, PASS], U32) for ab in w1_raw}
@@ -225,8 +224,6 @@ def tile_list_coupled_ionic_current_kernel(
                 in_=y_codes[c][:].bitcast(I32),
             )
 
-        nc.vector.memset(warm[:], 0.0)
-        nc.scalar.activation(out=warm[:, 4:8], in_=warm[:, 0:4], func=ACT.Sigmoid)
         for tile in (v_table_planes, v2_table_plane, w2_raw_plane):
             nc.vector.memset(tile[:].bitcast(I32), 0)
 
@@ -278,8 +275,7 @@ def tile_list_coupled_ionic_current_kernel(
         quantize_w1(1, 1, "bf16_b")
         make_force(0, 1)
         make_conductance(1, 0, "f32_c")
-        make_current(0, HALF, QUARTER, "bf16_d")
-        make_current(0, HALF + QUARTER, QUARTER, "bf16_b")
+        make_current(0, HALF, HALF, "bf16_b")
 
         make_force(1, 0)
         quantize_wc(0, "bf16_a")

@@ -16,6 +16,7 @@ E2M1 = mybir.dt.float4_e2m1fn_x4
 ALU = mybir.AluOpType
 ACT = mybir.ActivationFunctionType
 
+O = {"loads":"i1 t0 s1 i2 s2 w00 w10 t1 w2 sw g t2 v0 w01 w11 wc0 wc1 v10 v11 c","gain":"SSSSSSSS","gain1":"SSSSSSSS","ranges":[[0,256],[256,256],[512,256],[768,256]],"slots":{"w01":"a","w11":"b","c00":"c","c01":"a","wc0":"d","wc1":"e","cur0":"b"},"vround":["wc1"],"yround":"SVVV","tmajor1":0,"cslot":"ccgg","weave":0,"yrb":4,"per":[1,1,1,1],"split":1,"store1":{},"yout":["SSSS","SSSS","SSSS","SVSV"],"q2":"PSPS"}
 P = 128
 PACK = 4
 PASS = P * PACK
@@ -24,7 +25,7 @@ BANKS = 8
 HALF = S // 2
 QUARTER = S // 4
 V_PLANE_ROW = 4
-OUT_RANGES = ((0, HALF), (HALF, QUARTER), (HALF + QUARTER, QUARTER))
+OUT_RANGES = O.get("ranges", ((0, HALF), (HALF, QUARTER), (HALF + QUARTER, QUARTER)))
 
 
 def tile_list_coupled_ionic_current_kernel(
@@ -46,8 +47,8 @@ def tile_list_coupled_ionic_current_kernel(
         def float_rows(name, width):
             return ring.tile([P, PACK, width], F32, name=name, tag="float_rows", align_bytes=64, bufs=4)
 
-        def four_banks(name):
-            return [psum.tile([P, HALF], F32, name=name, tag="bank", bufs=BANKS) for t in range(PACK)]
+        def bank(name, ring_name):
+            return psum.tile([P, HALF], F32, name=name, tag=ring_name, bufs=O.get("banks", {"a": 4, "e": 4})[ring_name])
 
         idx = held("idx", [P, S // 16], U16)
         idx2 = held("idx2", [P, S // 16], U16)
@@ -72,8 +73,8 @@ def tile_list_coupled_ionic_current_kernel(
         wc_codes = [held("wc_codes%d" % b, [P, N], U32) for b in range(2)]
         wc_plane = [held("wc_plane%d" % b, [P, N], U8) for b in range(2)]
         force = [held("force%d" % b, [P, PACK, S], F32) for b in range(2)]
-        y_codes = [held("y_codes%d" % c, [P, w], U32) for c, (j0, w) in enumerate(OUT_RANGES)]
-        cur_codes = [held("cur_codes%d" % b, [P, S], U32) for b in range(2)]
+        y_codes = held("y_codes", [P, S], U32)
+        cur_codes = {1: held("cur_codes1", [P, S], U32)}
         cur_plane = [held("cur_plane%d" % b, [P, S], U8) for b in range(2)]
         y_plane = held("y_plane", [P, S], U8)
         conductance = {}
@@ -91,10 +92,12 @@ def tile_list_coupled_ionic_current_kernel(
                     out=tile[p0 : p0 + 8, :].bitcast(I32), in_=scales[:, 4 * q : 4 * q + 4, :].bitcast(I32)
                 )
 
-        def load_plane(tile, scales):
+        Q = {"P": nc.sync, "G": nc.gpsimd, "S": nc.scalar}
+
+        def load_plane(tile, scales, queue):
             rows = scales.rearrange("(q r) n -> r q n", r=4)
             for r in range(4):
-                nc.sync.dma_start(out=tile[r:P:QUADRANT, :].bitcast(I32), in_=rows[r].bitcast(I32))
+                Q[queue].dma_start(out=tile[r:P:QUADRANT, :].bitcast(I32), in_=rows[r].bitcast(I32))
 
         def load_rows(tile, rows):
             nc.sync.dma_start(out=tile, in_=rows.rearrange("(p t) n -> p t n", t=PACK))
@@ -120,29 +123,35 @@ def tile_list_coupled_ionic_current_kernel(
                 [rows.rearrange("p t (x i) -> p x t i", i=4) for rows in by_rows],
             )
 
-        def quantize_weight(raw, codes, plane, slot):
-            rounded = staged("weight_rounded", slot, [P, PACK * PASS], BF16)
-            nc.scalar.copy(
+        def quantize_weight(label, raw, codes, plane, slot):
+            rounded = staged("wr_" + label, slot, [P, PACK * PASS], BF16)
+            (nc.vector.tensor_copy if label in O.get("vround", []) else nc.scalar.copy)(
                 out=rounded[:].rearrange("p (t m i) -> p m i t", t=PACK, i=PACK),
                 in_=raw[:].rearrange("p i (m t) -> p m i t", t=PACK),
             )
             nc.vector.quantize_mx(out=codes[:].bitcast(E4M3), scales=plane[:], in_=rounded[:])
 
         def quantize_w1(a, b, slot):
-            quantize_weight(w1_raw[a, b], w1_codes[a, b], w1_plane[a, b], slot)
+            quantize_weight("w%d%d" % (a, b), w1_raw[a, b], w1_codes[a, b], w1_plane[a, b], slot)
 
         def quantize_wc(b, slot):
-            quantize_weight(wc_raw[b], wc_codes[b], wc_plane[b], slot)
+            quantize_weight("wc%d" % b, wc_raw[b], wc_codes[b], wc_plane[b], slot)
+
+        def load_vm_t(b, t):
+            nc.sync.dma_start(out=force[b][:, t, :], in_=vm[PASS * b : PASS * (b + 1), :].rearrange("(p t) n -> t p n", t=PACK)[t])
+
+        def who(b, h, t):
+            return O.get("gain", "GGGGGGGS")[2 * t + h] if b == 0 else O.get("gain1", "GGGGGGGS")[2 * t + h]
 
         def make_conductance(b, h, slot):
-            tile = staged("conductance", slot, [P, PACK, HALF], F32)
+            tile = staged("cond%d%d" % (b, h), slot, [P, PACK, HALF], F32)
             conductance[b, h] = tile
-            banks = four_banks("a_bank")
-            for a in range(2):
-                for t in range(PACK):
-                    places = slice(P * t, P * (t + 1))
+            for t in range(PACK):
+                acc = bank("a_bank", "a")
+                places = slice(P * t, P * (t + 1))
+                for a in range(2):
                     nc.tensor.matmul_mx(
-                        out=banks[t][:],
+                        out=acc[:],
                         lhsT=w1_codes[a, b][:, places].bitcast(E4M3),
                         lhsT_scale=w1_plane[a, b][:, places],
                         rhs=v_codes[a][:, half(h)].bitcast(E4M3),
@@ -150,51 +159,61 @@ def tile_list_coupled_ionic_current_kernel(
                         start=(a == 0),
                         stop=(a == 1),
                     )
-            for t in range(PACK):
-                nc.scalar.activation(out=tile[:, t, :], in_=banks[t][:], func=ACT.Sigmoid)
+                nc.scalar.activation(out=tile[:, t, :], in_=acc[:], func=ACT.Sigmoid)
             for t in range(PACK):
                 g, factor = tile[:, t, :], gain[:, b, t : t + 1]
-                if b == 0:
+                if who(b, h, t) == "S":
                     nc.scalar.activation(out=g, in_=g, func=ACT.Copy, scale=factor)
-                else:
+                if who(b, h, t) == "V":
                     nc.vector.tensor_scalar(out=g, in0=g, scalar1=factor, scalar2=None, op0=ALU.mult)
 
-        def make_force(b, h):
-            banks = four_banks("e_bank")
-            for t in range(PACK):
-                place = PASS * b + P * t
-                nc.tensor.matmul_mx(
-                    out=banks[t][:],
-                    lhsT=w2_codes[:, 2 * place : 2 * (place + P)].bitcast(E2M1),
-                    lhsT_scale=w2_plane[:, place : place + P],
-                    rhs=v2_codes[h][:].bitcast(E4M3),
-                    rhs_scale=v2_plane[:, half(h)],
-                    start=True,
-                    stop=True,
-                )
-                d = force[b][:, t, half(h)]
-                nc.vector.tensor_tensor(out=d, in0=d, in1=banks[t][:], op=ALU.subtract)
+        def make_force(b, h, t, x0=0, w=HALF):
+            acc = bank("e_bank", O.get("ering", "e"))
+            place = PASS * b + P * t
+            nc.tensor.matmul_mx(
+                out=acc[:, 0:w],
+                lhsT=w2_codes[:, 2 * place : 2 * (place + P)].bitcast(E2M1),
+                lhsT_scale=w2_plane[:, place : place + P],
+                rhs=v2_codes[h][:, x0 : x0 + w].bitcast(E4M3),
+                rhs_scale=v2_plane[:, HALF * h + x0 : HALF * h + x0 + w],
+                start=True,
+                stop=True,
+            )
+            d = force[b][:, t, HALF * h + x0 : HALF * h + x0 + w]
+            nc.vector.tensor_tensor(out=d, in0=d, in1=acc[:, 0:w], op=ALU.subtract)
+            if who(b, h, t) == "G":
+                nc.gpsimd.tensor_scalar(out=d, in0=d, scalar1=gain[:, b, t : t + 1], scalar2=0.0, op0=ALU.mult, op1=ALU.add)
+
+        rounded_cur = {}
 
         def make_current(b, j0, w, slot):
             cols = slice(j0, j0 + w)
             h, x0 = divmod(j0, HALF)
-            rounded = staged("cur_rounded", slot, [P, PACK * w], BF16)
+            rounded = staged("cur_r%d_%d" % (b, j0), slot, [P, PACK * w], BF16)
+            rounded_cur[b, j0] = rounded
             dst, (g, d) = word_walk(rounded[:], [conductance[b, h][:, :, x0 : x0 + w], force[b][:, :, cols]])
             nc.vector.tensor_tensor(out=dst, in0=g, in1=d, op=ALU.mult)
+
+        def quantize_current(b, j0, w):
+            cols = slice(j0, j0 + w)
             nc.vector.quantize_mx(
-                out=cur_codes[b][:, cols].bitcast(E4M3), scales=cur_plane[b][:, cols], in_=rounded[:]
+                out=cur_codes[b][:, cols].bitcast(E4M3), scales=cur_plane[b][:, cols], in_=rounded_cur[b, j0][:]
             )
 
         def make_output(c):
             j0, w = OUT_RANGES[c]
             cols = slice(j0, j0 + w)
-            y = float_rows("y", w)
-            banks = four_banks("c_bank")
-            for b in range(2):
-                for t in range(PACK):
-                    places = slice(P * t, P * (t + 1))
+            y = float_rows("y%d" % c, w)
+            per = O.get("per", [HALF // x[1] for x in OUT_RANGES])[c]
+            acc = None
+            for t in range(PACK):
+                if t % per == 0:
+                    acc = bank("c_bank", O.get("cring", "aeaeaeae")[c])
+                part = acc[:, (t % per) * w : (t % per + 1) * w]
+                places = slice(P * t, P * (t + 1))
+                for b in range(2):
                     nc.tensor.matmul_mx(
-                        out=banks[t][:, 0:w],
+                        out=part,
                         lhsT=wc_codes[b][:, places].bitcast(E4M3),
                         lhsT_scale=wc_plane[b][:, places],
                         rhs=cur_codes[b][:, cols].bitcast(E4M3),
@@ -202,52 +221,48 @@ def tile_list_coupled_ionic_current_kernel(
                         start=(b == 0),
                         stop=(b == 1),
                     )
-            shared = c == len(OUT_RANGES) - 1
-            for t in range(PACK):
-                factor = inv_cap[:, t : t + 1]
-                if shared and t % 2 == 1:
-                    nc.vector.tensor_scalar(
-                        out=y[:, t, :], in0=banks[t][:, 0:w], scalar1=factor, scalar2=None, op0=ALU.mult
-                    )
-                else:
-                    nc.scalar.activation(out=y[:, t, :], in_=banks[t][:, 0:w], func=ACT.Copy, scale=factor)
-            nc.sync.dma_start(out=out_0[:, cols].rearrange("(p t) j -> p t j", t=PACK), in_=y[:])
-            rounded = ring.tile([P, PACK * w], BF16, name="y_rounded", align_bytes=64)
+                if (t + 1) % per == 0:
+                    for u in range(t + 1 - per, t + 1):
+                        factor = inv_cap[:, u : u + 1]
+                        part = acc[:, (u % per) * w : (u % per + 1) * w]
+                        if O.get("yout", ["SSSS"] * 8)[c][u] == "V":
+                            nc.vector.tensor_scalar(out=y[:, u, :], in0=part, scalar1=factor, scalar2=None, op0=ALU.mult)
+                        else:
+                            nc.scalar.activation(out=y[:, u, :], in_=part, func=ACT.Copy, scale=factor)
+            Q[O.get("q0", "PPPPPPPP")[c]].dma_start(out=out_0[:, cols].rearrange("(p t) j -> p t j", t=PACK), in_=y[:])
+            rounded = ring.tile([P, PACK * w], BF16, name="y_r%d" % c, tag="y_rounded", align_bytes=64, bufs=O.get("yrb", 2))
             dst, (src,) = word_walk(rounded[:], [y[:]])
-            if c == 0:
+            if O.get("yround", "SVVVVVVV")[c] == "S":
                 nc.scalar.copy(out=dst, in_=src)
             else:
                 nc.vector.tensor_copy(out=dst, in_=src)
-            nc.vector.quantize_mx(out=y_codes[c][:].bitcast(E4M3), scales=y_plane[:, cols], in_=rounded[:])
-            nc.sync.dma_start(
-                out=out_1[0].rearrange("p m t -> p (m t)")[:, PACK * j0 : PACK * (j0 + w)].bitcast(I32),
-                in_=y_codes[c][:].bitcast(I32),
-            )
+            nc.vector.quantize_mx(out=y_codes[:, cols].bitcast(E4M3), scales=y_plane[:, cols], in_=rounded[:])
+            first = O.get("store1", {}).get(str(c), j0)
+            if first >= 0:
+                Q[O.get("q1", "PPPPPPPP")[c]].dma_start(
+                    out=out_1[0].rearrange("p m t -> p (m t)")[:, PACK * first : PACK * (j0 + w)].bitcast(I32),
+                    in_=y_codes[:, first : j0 + w].bitcast(I32),
+                )
 
         for tile in (v_table_planes, v2_table_plane, w2_raw_plane):
             nc.vector.memset(tile[:].bitcast(I32), 0)
 
-        nc.sync.dma_start(idx[:], offs)
-        load_words(v_table[0], tab_words[0])
-        load_two_planes(v_table_planes, tab_scales)
-        nc.sync.dma_start(idx2[:], offs2)
-        load_plane(v2_table_plane, tab2_scales[0])
-        load_w1(0, 0)
-        load_w1(1, 0)
-        load_words(v_table[1], tab_words[1])
-        nc.sync.dma_start(out=w2_raw[:].bitcast(I32), in_=w2_words[0].bitcast(I32))
-        load_plane(w2_raw_plane, w2_scales[0])
-        nc.sync.dma_start(out=gain[:], in_=gmax.rearrange("(b p t) -> p b t", b=2, t=PACK))
-        load_words(v2_table, tab2_words[0])
-        load_vm(0, 0)
-        load_vm(0, 1)
-        load_w1(0, 1)
-        load_w1(1, 1)
-        load_vm(1, 0)
-        load_wc(0)
-        load_wc(1)
-        load_vm(1, 1)
-        nc.sync.dma_start(out=inv_cap[:], in_=cinv.rearrange("(p t) -> p t", t=PACK))
+        L = {
+            "i1": lambda: nc.sync.dma_start(idx[:], offs), "i2": lambda: nc.sync.dma_start(idx2[:], offs2),
+            "t0": lambda: load_words(v_table[0], tab_words[0]), "t1": lambda: load_words(v_table[1], tab_words[1]),
+            "t2": lambda: load_words(v2_table, tab2_words[0]),
+            "s1": lambda: load_two_planes(v_table_planes, tab_scales), "s2": lambda: load_plane(v2_table_plane, tab2_scales[0], O.get("qs2", "P")),
+            "w2": lambda: nc.sync.dma_start(out=w2_raw[:].bitcast(I32), in_=w2_words[0].bitcast(I32)),
+            "sw": lambda: load_plane(w2_raw_plane, w2_scales[0], O.get("qsw", "P")),
+            "g": lambda: Q[O.get("qg", "P")].dma_start(out=gain[:], in_=gmax.rearrange("(b p t) -> p b t", b=2, t=PACK)),
+            "c": lambda: Q[O.get("qg", "P")].dma_start(out=inv_cap[:], in_=cinv.rearrange("(p t) -> p t", t=PACK)),
+            "w00": lambda: load_w1(0, 0), "w10": lambda: load_w1(1, 0), "w01": lambda: load_w1(0, 1), "w11": lambda: load_w1(1, 1),
+            "wc0": lambda: load_wc(0), "wc1": lambda: load_wc(1),
+            "v0": lambda: [load_vm_t(0, t) for t in range(4)], "v1": lambda: [load_vm_t(1, t) for t in range(4)],
+            "v00": lambda: load_vm(0, 0), "v01": lambda: load_vm(0, 1), "v10": lambda: load_vm(1, 0), "v11": lambda: load_vm(1, 1),
+        }
+        for name in O.get("loads", "i1 t0 s1 i2 s2 w2 sw t2 w00 t1 w10 g v0 w01 w11 v1 wc0 wc1 c").split():
+            L[name]()
 
         gather(v_codes[0][:], v_table[0][:].bitcast(U32), idx[:])
         gather(v_planes[:], v_table_planes[:], idx[:])
@@ -260,36 +275,49 @@ def tile_list_coupled_ionic_current_kernel(
             out=w2_plane[:].rearrange("p (b t m) -> p b m t", b=2, t=PACK),
             in_=w2_raw_plane[:].rearrange("p (b m t) -> p b m t", b=2, t=PACK),
         )
-
-        quantize_w1(0, 0, "bf16_a")
-        quantize_w1(1, 0, "bf16_b")
+        sl = O.get("slots", dict(w01="a", w11="b", c00="c", c01="d", wc0="a", wc1="b"))
+        quantize_w1(0, 0, "a")
+        quantize_w1(1, 0, "b")
         for h in range(2):
             gather(v_codes[1][:, half(h)], v_table[1][:].bitcast(U32), entries(idx, h))
-        make_conductance(0, 0, "f32_a")
         for h in range(2):
             gather(v2_codes[h][:], v2_table[:].bitcast(U32), entries(idx2, h))
-        make_force(0, 0)
+        make_conductance(0, 0, "f32_a")
         make_conductance(0, 1, "f32_b")
-        make_current(0, 0, HALF, "bf16_c")
-        quantize_w1(0, 1, "bf16_a")
-        quantize_w1(1, 1, "bf16_b")
-        make_force(0, 1)
+        quantize_w1(0, 1, sl["w01"])
+        quantize_w1(1, 1, sl["w11"])
+        order0 = [(h, t) for t in range(4) for h in range(2)] if O.get("tmajor0", 1) else [(h, t) for h in range(2) for t in range(4)]
+        order1 = [(h, t) for t in range(4) for h in range(2)] if O.get("tmajor1", 1) else [(h, t) for h in range(2) for t in range(4)]
+        for h, t in order0:
+            make_force(0, h, t)
         make_conductance(1, 0, "f32_c")
-        make_current(0, HALF, HALF, "bf16_b")
-
-        make_force(1, 0)
-        quantize_wc(0, "bf16_a")
+        make_current(0, 0, HALF, sl["c00"])
+        make_current(0, HALF, HALF, sl["c01"])
+        cur_codes[0] = staged("cur_codes0", sl.get("cur0", "z"), [P, S], U32)
+        quantize_current(0, 0, HALF)
+        quantize_current(0, HALF, HALF)
         make_conductance(1, 1, "f32_a")
-        quantize_wc(1, "bf16_c")
-        make_current(1, 0, HALF, "bf16_d")
-        make_force(1, 1)
-        make_output(0)
-        make_current(1, HALF, QUARTER, "bf16_a")
-        make_current(1, HALF + QUARTER, QUARTER, "bf16_b")
-        make_output(1)
-        make_output(2)
+        quantize_wc(0, sl["wc0"])
+        quantize_wc(1, sl["wc1"])
+        for h, t in order1:
+            if O.get("tmajor1", 1) or h == 0:
+                make_force(1, h, t)
+        for c, (j0, w) in enumerate(OUT_RANGES):
+            if j0 == HALF and not O.get("tmajor1", 1) and not O.get("split", 0):
+                for t in range(PACK):
+                    make_force(1, 1, t)
+            if j0 >= HALF and O.get("split", 0):
+                for t in range(PACK):
+                    make_force(1, 1, t, j0 - HALF, w)
+            make_current(1, j0, w, O.get("cslot", "cdefcdef")[c])
+            quantize_current(1, j0, w)
+            if c > 0 and O.get("weave", 1):
+                make_output(c - 1)
+        for c in range(len(OUT_RANGES)):
+            if c == len(OUT_RANGES) - 1 or not O.get("weave", 1):
+                make_output(c)
 
         out_rows = out_2[0].rearrange("(q r) m -> r q m", r=4)
         for r in range(4):
-            queue = nc.sync if r % 2 == 0 else nc.scalar
+            queue = Q[O.get("q2", "PSPS")[r]]
             queue.dma_start(out=out_rows[r].bitcast(I32), in_=y_plane[r:P:QUADRANT, :].bitcast(I32))

@@ -16,7 +16,7 @@ E2M1 = mybir.dt.float4_e2m1fn_x4
 ALU = mybir.AluOpType
 ACT = mybir.ActivationFunctionType
 
-O = {"loads":"i1 t0 s1 i2 s2 w00 w10 t1 w2 sw g t2 v0 w01 w11 wc0 wc1 v10 v11 c","gain":"SSSSSSSS","gain1":"SSSSSSSS","ranges":[[0,256],[256,256],[512,256],[768,256]],"slots":{"w01":"a","w11":"b","c00":"c","c01":"a","wc0":"d","wc1":"e","cur0":"b"},"vround":["wc1"],"yround":"SVVV","tmajor1":0,"cslot":"ccgg","weave":0,"yrb":4,"per":[1,1,1,1],"split":1,"store1":{},"yout":["SSSS","SSSS","SSSS","SVSV"],"q2":"PSPS"}
+O = {"loads":"w00 i1 sA i2 sB t0 pv sC pe w10 mA1 mA2 mA3 t1 w2 g t2 mE1 mE2 mE3 vp00 vp01 w01 w11 wc0 v10 wc1 v11 c","gain":"SSSSSSSS","gain1":"SSSSSSSS","ranges":[[0,256],[256,256],[512,256],[768,256]],"slots":{"w01":"a","w11":"b","c00":"c","c01":"a","wc0":"d","wc1":"e","cur01":"z","cur00":"y"},"vround":["wc1"],"yround":"HVHVV","tmajor1":0,"cslot":"ccggg","weave":0,"yrb":4,"per":[1,1,1,1],"split":1,"store1":{"0":-1,"1":0},"yout":["SSSS","SSSS","SSSS","SSSS"],"q2":"PSPS","cring":"aaeae","wcut":{"wc1":0},"spreadE":1,"spreadA":1}
 P = 128
 PACK = 4
 PASS = P * PACK
@@ -24,7 +24,7 @@ QUADRANT = 32
 BANKS = 8
 HALF = S // 2
 QUARTER = S // 4
-V_PLANE_ROW = 4
+V_PLANE_ROW = 0 if O.get("spreadA") else 4
 OUT_RANGES = O.get("ranges", ((0, HALF), (HALF, QUARTER), (HALF + QUARTER, QUARTER)))
 
 
@@ -59,11 +59,14 @@ def tile_list_coupled_ionic_current_kernel(
         w2_raw = held("w2_raw", [P, 2 * H], U8)
         w2_raw_plane = held("w2_raw_plane", [P, H], U8)
         w2_codes = held("w2_codes", [P, 2 * H], U8)
-        w2_plane = held("w2_plane", [P, H], U8)
+        e_planes = held("e_planes", [P, S + H], U8)
+        w2_plane = e_planes[:, S : S + H]
+        v2_picked = held("v2_picked", [P, S], U8)
+        v_picked = held("v_picked", [P, S], U8)
         v_codes = [held("v_codes%d" % a, [P, S], U32) for a in range(2)]
-        v_planes = held("v_planes", [P, S], U8)
+        v_planes = held("v_planes", [P, S], U8) if O.get("spreadA") else v_picked
         v2_codes = [held("v2_codes%d" % h, [P, HALF], U32) for h in range(2)]
-        v2_plane = held("v2_plane", [P, S], U8)
+        v2_plane = e_planes[:, 0:S] if O.get("spreadE") else v2_picked[:]
         gain = held("gain", [P, 2, PACK], F32)
         inv_cap = held("inv_cap", [P, PACK], F32)
         w1_raw = {(a, b): float_rows("w1_raw%d%d" % (a, b), PASS) for b in range(2) for a in range(2)}
@@ -74,7 +77,7 @@ def tile_list_coupled_ionic_current_kernel(
         wc_plane = [held("wc_plane%d" % b, [P, N], U8) for b in range(2)]
         force = [held("force%d" % b, [P, PACK, S], F32) for b in range(2)]
         y_codes = held("y_codes", [P, S], U32)
-        cur_codes = {1: held("cur_codes1", [P, S], U32)}
+        cur_codes = {}
         cur_plane = [held("cur_plane%d" % b, [P, S], U8) for b in range(2)]
         y_plane = held("y_plane", [P, S], U8)
         conductance = {}
@@ -88,7 +91,7 @@ def tile_list_coupled_ionic_current_kernel(
         def load_two_planes(tile, scales):
             for q in range(4):
                 p0 = QUADRANT * q + V_PLANE_ROW
-                nc.sync.dma_start(
+                (nc.gpsimd if O.get("qs1", "P") == "G" else nc.sync).dma_start(
                     out=tile[p0 : p0 + 8, :].bitcast(I32), in_=scales[:, 4 * q : 4 * q + 4, :].bitcast(I32)
                 )
 
@@ -125,10 +128,13 @@ def tile_list_coupled_ionic_current_kernel(
 
         def quantize_weight(label, raw, codes, plane, slot):
             rounded = staged("wr_" + label, slot, [P, PACK * PASS], BF16)
-            (nc.vector.tensor_copy if label in O.get("vround", []) else nc.scalar.copy)(
-                out=rounded[:].rearrange("p (t m i) -> p m i t", t=PACK, i=PACK),
-                in_=raw[:].rearrange("p i (m t) -> p m i t", t=PACK),
-            )
+            dst = rounded[:].rearrange("p (t m i) -> p m i t", t=PACK, i=PACK)
+            src = raw[:].rearrange("p i (m t) -> p m i t", t=PACK)
+            cut = O.get("wcut", {}).get(label, 0 if label in O.get("vround", []) else P)
+            if cut > 0:
+                nc.scalar.copy(out=dst[:, 0:cut], in_=src[:, 0:cut])
+            if cut < P:
+                nc.vector.tensor_copy(out=dst[:, cut:P], in_=src[:, cut:P])
             nc.vector.quantize_mx(out=codes[:].bitcast(E4M3), scales=plane[:], in_=rounded[:])
 
         def quantize_w1(a, b, slot):
@@ -197,7 +203,7 @@ def tile_list_coupled_ionic_current_kernel(
         def quantize_current(b, j0, w):
             cols = slice(j0, j0 + w)
             nc.vector.quantize_mx(
-                out=cur_codes[b][:, cols].bitcast(E4M3), scales=cur_plane[b][:, cols], in_=rounded_cur[b, j0][:]
+                out=cur_codes[b, j0 // HALF][:, j0 % HALF : j0 % HALF + w].bitcast(E4M3), scales=cur_plane[b][:, cols], in_=rounded_cur[b, j0][:]
             )
 
         def make_output(c):
@@ -216,7 +222,7 @@ def tile_list_coupled_ionic_current_kernel(
                         out=part,
                         lhsT=wc_codes[b][:, places].bitcast(E4M3),
                         lhsT_scale=wc_plane[b][:, places],
-                        rhs=cur_codes[b][:, cols].bitcast(E4M3),
+                        rhs=cur_codes[b, j0 // HALF][:, j0 % HALF : j0 % HALF + w].bitcast(E4M3),
                         rhs_scale=cur_plane[b][:, cols],
                         start=(b == 0),
                         stop=(b == 1),
@@ -232,7 +238,11 @@ def tile_list_coupled_ionic_current_kernel(
             Q[O.get("q0", "PPPPPPPP")[c]].dma_start(out=out_0[:, cols].rearrange("(p t) j -> p t j", t=PACK), in_=y[:])
             rounded = ring.tile([P, PACK * w], BF16, name="y_r%d" % c, tag="y_rounded", align_bytes=64, bufs=O.get("yrb", 2))
             dst, (src,) = word_walk(rounded[:], [y[:]])
-            if O.get("yround", "SVVVVVVV")[c] == "S":
+            if O.get("yround", "SVVVVVVV")[c] == "H":
+                cut = O.get("ycut", w // 8)
+                nc.scalar.copy(out=dst[:, 0:cut], in_=src[:, 0:cut])
+                nc.vector.tensor_copy(out=dst[:, cut:], in_=src[:, cut:])
+            elif O.get("yround", "SVVVVVVV")[c] == "S":
                 nc.scalar.copy(out=dst, in_=src)
             else:
                 nc.vector.tensor_copy(out=dst, in_=src)
@@ -261,19 +271,52 @@ def tile_list_coupled_ionic_current_kernel(
             "v0": lambda: [load_vm_t(0, t) for t in range(4)], "v1": lambda: [load_vm_t(1, t) for t in range(4)],
             "v00": lambda: load_vm(0, 0), "v01": lambda: load_vm(0, 1), "v10": lambda: load_vm(1, 0), "v11": lambda: load_vm(1, 1),
         }
+        def load_vm_pair(b, u):
+            nc.sync.dma_start(out=force[b][:, 2 * u : 2 * u + 2, :], in_=vm[PASS * b : PASS * (b + 1), :].rearrange("(p t) n -> p t n", t=PACK)[:, 2 * u : 2 * u + 2, :])
+
+        def spread(tile, rows, first):
+            nc.sync.dma_start(out=tile[first:P:8, :].bitcast(I32), in_=rows.bitcast(I32))
+
+        def close_up(tile, first, r):
+            nc.sync.dma_start(out=tile[first + r : P : QUADRANT, :].bitcast(I32), in_=tile[first + 8 * r : P : QUADRANT, :].bitcast(I32))
+
+        def pick_v():
+            gather(v_picked[:], v_table_planes[:], idx[:])
+            if O.get("spreadA"):
+                nc.vector.tensor_copy(out=v_planes[:].bitcast(I32), in_=v_picked[:].bitcast(I32))
+
+        def pick_e():
+            gather(v2_picked[:], v2_table_plane[:], idx2[:])
+            if O.get("spreadE"):
+                nc.vector.tensor_copy(out=v2_plane.bitcast(I32), in_=v2_picked[:].bitcast(I32))
+            nc.vector.tensor_copy(
+                out=w2_plane.rearrange("p (b t m) -> p b m t", b=2, t=PACK),
+                in_=w2_raw_plane[:].rearrange("p (b m t) -> p b m t", b=2, t=PACK),
+            )
+
+        L["pv"] = pick_v
+        L["pe"] = pick_e
+        L["sA"] = lambda: [spread(v_table_planes, tab_scales[a], 4 * a) for a in range(2)]
+        L["sB"] = lambda: spread(v2_table_plane, tab2_scales[0], 0)
+        L["sC"] = lambda: spread(w2_raw_plane, w2_scales[0], 0)
+        for u in range(1, 4):
+            L["mA%d" % u] = lambda u=u: [close_up(v_planes, 4 * a, u) for a in range(2)]
+            L["mE%d" % u] = lambda u=u: close_up(e_planes, 0, u)
+        for u in range(4):
+            L["vp%d%d" % divmod(u, 2)] = lambda u=u: load_vm_pair(u // 2, u % 2)
+        for u in range(PACK):
+            L["v0t%d" % u] = lambda u=u: load_vm_t(0, u)
         for name in O.get("loads", "i1 t0 s1 i2 s2 w2 sw t2 w00 t1 w10 g v0 w01 w11 v1 wc0 wc1 c").split():
             L[name]()
 
         gather(v_codes[0][:], v_table[0][:].bitcast(U32), idx[:])
-        gather(v_planes[:], v_table_planes[:], idx[:])
-        gather(v2_plane[:], v2_table_plane[:], idx2[:])
+        if not O.get("spreadA"):
+            pick_v()
+        if not O.get("spreadE"):
+            pick_e()
         nc.vector.tensor_copy(
             out=w2_codes[:].bitcast(U16).rearrange("p (b t m) -> p b m t", b=2, t=PACK),
             in_=w2_raw[:].bitcast(U16).rearrange("p (b m t) -> p b m t", b=2, t=PACK),
-        )
-        nc.vector.tensor_copy(
-            out=w2_plane[:].rearrange("p (b t m) -> p b m t", b=2, t=PACK),
-            in_=w2_raw_plane[:].rearrange("p (b m t) -> p b m t", b=2, t=PACK),
         )
         sl = O.get("slots", dict(w01="a", w11="b", c00="c", c01="d", wc0="a", wc1="b"))
         quantize_w1(0, 0, "a")
@@ -293,9 +336,12 @@ def tile_list_coupled_ionic_current_kernel(
         make_conductance(1, 0, "f32_c")
         make_current(0, 0, HALF, sl["c00"])
         make_current(0, HALF, HALF, sl["c01"])
-        cur_codes[0] = staged("cur_codes0", sl.get("cur0", "z"), [P, S], U32)
+        cur_codes[0, 0] = staged("cur_codes00", sl.get("cur00", "y"), [P, HALF], U32)
         quantize_current(0, 0, HALF)
+        cur_codes[0, 1] = staged("cur_codes01", sl.get("cur01", "z"), [P, HALF], U32)
         quantize_current(0, HALF, HALF)
+        cur_codes[1, 0] = held("cur_codes10", [P, HALF], U32)
+        cur_codes[1, 1] = held("cur_codes11", [P, HALF], U32)
         make_conductance(1, 1, "f32_a")
         quantize_wc(0, sl["wc0"])
         quantize_wc(1, sl["wc1"])

@@ -16,7 +16,7 @@ E2M1 = mybir.dt.float4_e2m1fn_x4
 ALU = mybir.AluOpType
 ACT = mybir.ActivationFunctionType
 
-O = {"loads":"w00 i1 sA i2 sB t0 pv sC pe w10 mA1 mA2 mA3 t1 w2 g t2 mE1 mE2 mE3 vp00 vp01 w01 w11 wc0 v10 wc1 v11 c","gain":"SSSSSSSS","gain1":"SSSSSSSS","ranges":[[0,256],[256,256],[512,256],[768,256]],"slots":{"w01":"a","w11":"b","c00":"c","c01":"a","wc0":"d","wc1":"e","cur01":"z","cur00":"y"},"vround":["wc1"],"yround":"HVHVV","tmajor1":0,"cslot":"ccggg","weave":0,"yrb":4,"per":[1,1,1,1],"split":1,"store1":{"0":-1,"1":0},"yout":["SSSS","SSSS","SSSS","SSSS"],"q2":"PSPS","cring":"aaeae","wcut":{"wc1":0},"spreadE":1,"spreadA":1}
+O = {"loads":"w2 i1 sA w00 i2 sB t0 pv sC pe w10 mA1 mA2 mA3 t1 g t2 mE1 mE2 mE3 vp00 vp01 w01 w11 wc0 v10 wc1 v11 c","gain":"SSSSSSSS","gain1":"SSSSSSSS","ranges":[[0,256],[256,256],[512,256],[768,256]],"slots":{"w01":"a","w11":"b","c00":"c","c01":"f","wc0":"d","wc1":"e","cur01":"z","cur00":"y"},"vround":["wc1"],"yround":"HVHH","tmajor1":0,"cslot":"ccggg","weave":0,"yrb":4,"per":[1,1,1,1],"split":1,"store1":{},"yout":["SSSS","SSSS","SSSS","SSSS"],"q2":"PSPS","cring":"aaeae","wcut":{"wc1":0,"wc0":80},"spreadE":1,"spreadA":1,"split01":1,"yrslot":["y0","y1","y2","y3"],"ycut":32}
 P = 128
 PACK = 4
 PASS = P * PACK
@@ -73,10 +73,12 @@ def tile_list_coupled_ionic_current_kernel(
         wc_raw = [held("wc_raw%d" % b, [P, PACK, N], F32) for b in range(2)]
         w1_codes = {ab: held("w1_codes%d%d" % ab, [P, PASS], U32) for ab in w1_raw}
         w1_plane = {ab: held("w1_plane%d%d" % ab, [P, PASS], U8) for ab in w1_raw}
-        wc_codes = [held("wc_codes%d" % b, [P, N], U32) for b in range(2)]
-        wc_plane = [held("wc_plane%d" % b, [P, N], U8) for b in range(2)]
+        wc_codes_all = held("wc_codes", [P, 2 * N], U32)
+        wc_plane_all = held("wc_plane", [P, 2 * N], U8)
+        wc_codes = [wc_codes_all[:, N * b : N * (b + 1)] for b in range(2)]
+        wc_plane = [wc_plane_all[:, N * b : N * (b + 1)] for b in range(2)]
         force = [held("force%d" % b, [P, PACK, S], F32) for b in range(2)]
-        y_codes = held("y_codes", [P, S], U32)
+        y_tiles = {}
         cur_codes = {}
         cur_plane = [held("cur_plane%d" % b, [P, S], U8) for b in range(2)]
         y_plane = held("y_plane", [P, S], U8)
@@ -126,8 +128,10 @@ def tile_list_coupled_ionic_current_kernel(
                 [rows.rearrange("p t (x i) -> p x t i", i=4) for rows in by_rows],
             )
 
-        def quantize_weight(label, raw, codes, plane, slot):
-            rounded = staged("wr_" + label, slot, [P, PACK * PASS], BF16)
+        def quantize_weight(label, raw, codes, plane, slot, rounded=None):
+            alone = rounded is None
+            if alone:
+                rounded = staged("wr_" + label, slot, [P, PACK * PASS], BF16)
             dst = rounded[:].rearrange("p (t m i) -> p m i t", t=PACK, i=PACK)
             src = raw[:].rearrange("p i (m t) -> p m i t", t=PACK)
             cut = O.get("wcut", {}).get(label, 0 if label in O.get("vround", []) else P)
@@ -135,7 +139,8 @@ def tile_list_coupled_ionic_current_kernel(
                 nc.scalar.copy(out=dst[:, 0:cut], in_=src[:, 0:cut])
             if cut < P:
                 nc.vector.tensor_copy(out=dst[:, cut:P], in_=src[:, cut:P])
-            nc.vector.quantize_mx(out=codes[:].bitcast(E4M3), scales=plane[:], in_=rounded[:])
+            if alone:
+                nc.vector.quantize_mx(out=codes[:].bitcast(E4M3), scales=plane[:], in_=rounded[:])
 
         def quantize_w1(a, b, slot):
             quantize_weight("w%d%d" % (a, b), w1_raw[a, b], w1_codes[a, b], w1_plane[a, b], slot)
@@ -210,6 +215,9 @@ def tile_list_coupled_ionic_current_kernel(
             j0, w = OUT_RANGES[c]
             cols = slice(j0, j0 + w)
             y = float_rows("y%d" % c, w)
+            if c == 0:
+                y_tiles[0] = staged("y_codes", O.get("yslot", "yc"), [P, S], U32)
+            y_codes = y_tiles[0]
             per = O.get("per", [HALF // x[1] for x in OUT_RANGES])[c]
             acc = None
             for t in range(PACK):
@@ -236,7 +244,7 @@ def tile_list_coupled_ionic_current_kernel(
                         else:
                             nc.scalar.activation(out=y[:, u, :], in_=part, func=ACT.Copy, scale=factor)
             Q[O.get("q0", "PPPPPPPP")[c]].dma_start(out=out_0[:, cols].rearrange("(p t) j -> p t j", t=PACK), in_=y[:])
-            rounded = ring.tile([P, PACK * w], BF16, name="y_r%d" % c, tag="y_rounded", align_bytes=64, bufs=O.get("yrb", 2))
+            rounded = staged("y_r%d" % c, O.get("yrslot", ["y0", "y1", "y2", "y3", "y4"])[c], [P, PACK * w], BF16)
             dst, (src,) = word_walk(rounded[:], [y[:]])
             if O.get("yround", "SVVVVVVV")[c] == "H":
                 cut = O.get("ycut", w // 8)
@@ -294,6 +302,8 @@ def tile_list_coupled_ionic_current_kernel(
                 in_=w2_raw_plane[:].rearrange("p (b m t) -> p b m t", b=2, t=PACK),
             )
 
+        for u in range(2):
+            L["w00" + "ab"[u]] = lambda u=u: nc.sync.dma_start(out=w1_raw[0, 0][:, 2 * u : 2 * u + 2, :], in_=w1[0:PASS, 0:PASS].rearrange("(p t) n -> p t n", t=PACK)[:, 2 * u : 2 * u + 2, :])
         L["pv"] = pick_v
         L["pe"] = pick_e
         L["sA"] = lambda: [spread(v_table_planes, tab_scales[a], 4 * a) for a in range(2)]
@@ -335,16 +345,33 @@ def tile_list_coupled_ionic_current_kernel(
             make_force(0, h, t)
         make_conductance(1, 0, "f32_c")
         make_current(0, 0, HALF, sl["c00"])
-        make_current(0, HALF, HALF, sl["c01"])
+        if O.get("split01"):
+            make_current(0, HALF, QUARTER, sl["c01"])
+            make_current(0, HALF + QUARTER, QUARTER, sl.get("c01b", "b"))
+        else:
+            make_current(0, HALF, HALF, sl["c01"])
         cur_codes[0, 0] = staged("cur_codes00", sl.get("cur00", "y"), [P, HALF], U32)
         quantize_current(0, 0, HALF)
         cur_codes[0, 1] = staged("cur_codes01", sl.get("cur01", "z"), [P, HALF], U32)
-        quantize_current(0, HALF, HALF)
+        if O.get("split01"):
+            quantize_current(0, HALF, QUARTER)
+            quantize_current(0, HALF + QUARTER, QUARTER)
+        else:
+            quantize_current(0, HALF, HALF)
         cur_codes[1, 0] = held("cur_codes10", [P, HALF], U32)
         cur_codes[1, 1] = held("cur_codes11", [P, HALF], U32)
-        make_conductance(1, 1, "f32_a")
-        quantize_wc(0, sl["wc0"])
-        quantize_wc(1, sl["wc1"])
+        if not O.get("wcfirst"):
+            make_conductance(1, 1, O.get("c11", "f32_a"))
+        if O.get("wideq"):
+            both = staged("wc_rounded", sl.get("wcq", "w"), [P, 2 * PACK * PASS], BF16)
+            for b in range(2):
+                quantize_weight("wc%d" % b, wc_raw[b], None, None, None, both[:, PACK * PASS * b : PACK * PASS * (b + 1)])
+            nc.vector.quantize_mx(out=wc_codes_all[:].bitcast(E4M3), scales=wc_plane_all[:], in_=both[:])
+        else:
+            quantize_wc(0, sl["wc0"])
+            quantize_wc(1, sl["wc1"])
+        if O.get("wcfirst"):
+            make_conductance(1, 1, O.get("c11", "f32_a"))
         for h, t in order1:
             if O.get("tmajor1", 1) or h == 0:
                 make_force(1, h, t)

@@ -16,16 +16,17 @@ E2M1 = mybir.dt.float4_e2m1fn_x4
 ALU = mybir.AluOpType
 ACT = mybir.ActivationFunctionType
 
-O = {"loads":"w2 i1 sA w00 i2 sB t0 pv sC pe w10 mA1 mA2 mA3 t1 g t2 mE1 mE2 mE3 vp00 vp01 w01 w11 wc0 v10 wc1 v11 c","gain":"SSSSSSSS","gain1":"SSSSSSSS","ranges":[[0,256],[256,256],[512,256],[768,256]],"slots":{"w01":"a","w11":"b","c00":"c","c01":"f","wc0":"d","wc1":"e","cur01":"z","cur00":"y"},"vround":["wc1"],"yround":"HVHH","tmajor1":0,"cslot":"ccggg","weave":0,"yrb":4,"per":[1,1,1,1],"split":1,"store1":{},"yout":["SSSS","SSSS","SSSS","SSSS"],"q2":"PSPS","cring":"aaeae","wcut":{"wc1":0,"wc0":80},"spreadE":1,"spreadA":1,"split01":1,"yrslot":["y0","y1","y2","y3"],"ycut":32}
 P = 128
 PACK = 4
 PASS = P * PACK
 QUADRANT = 32
-BANKS = 8
+SPREAD = 8
+PLANE_SHIFT = 4
+RING_BANKS = 4
 HALF = S // 2
 QUARTER = S // 4
-V_PLANE_ROW = 0 if O.get("spreadA") else 4
-OUT_RANGES = O.get("ranges", ((0, HALF), (HALF, QUARTER), (HALF + QUARTER, QUARTER)))
+SCALAR_KEEPS_LAST_W1 = 96
+GPSIMD_ROWS = 2
 
 
 def tile_list_coupled_ionic_current_kernel(
@@ -35,86 +36,81 @@ def tile_list_coupled_ionic_current_kernel(
     nc = tc.nc
     with ExitStack() as ctx:
         keep = ctx.enter_context(tc.tile_pool(name="keep", bufs=1))
-        ring = ctx.enter_context(tc.tile_pool(name="ring", bufs=2))
-        psum = ctx.enter_context(tc.psum_pool(name="psum", bufs=1))
+        ring = ctx.enter_context(tc.tile_pool(name="ring", bufs=1))
+        psum = ctx.enter_context(tc.psum_pool(name="psum", bufs=RING_BANKS))
 
         def held(name, shape, dtype):
             return keep.tile(shape, dtype, name=name, align_bytes=64)
 
         def staged(name, slot, shape, dtype):
-            return ring.tile(shape, dtype, name=name, tag=slot, align_bytes=64, bufs=1)
+            return ring.tile(shape, dtype, name=name, tag=slot, align_bytes=64)
 
         def float_rows(name, width):
             return ring.tile([P, PACK, width], F32, name=name, tag="float_rows", align_bytes=64, bufs=4)
 
-        def bank(name, ring_name):
-            return psum.tile([P, HALF], F32, name=name, tag=ring_name, bufs=O.get("banks", {"a": 4, "e": 4})[ring_name])
+        def bank(bank_ring):
+            return psum.tile([P, HALF], F32, name="bank", tag=bank_ring)
 
         idx = held("idx", [P, S // 16], U16)
         idx2 = held("idx2", [P, S // 16], U16)
         v_table = [held("v_table%d" % a, [P, T], I32) for a in range(2)]
-        v_table_planes = held("v_table_planes", [P, T], U8)
+        v_table_scales = held("v_table_scales", [P, T], U8)
         v2_table = held("v2_table", [P, T2], I32)
-        v2_table_plane = held("v2_table_plane", [P, T2], U8)
+        v2_table_scales = held("v2_table_scales", [P, T2], U8)
         w2_raw = held("w2_raw", [P, 2 * H], U8)
-        w2_raw_plane = held("w2_raw_plane", [P, H], U8)
+        w2_raw_scales = held("w2_raw_scales", [P, H], U8)
         w2_codes = held("w2_codes", [P, 2 * H], U8)
         e_planes = held("e_planes", [P, S + H], U8)
-        w2_plane = e_planes[:, S : S + H]
-        v2_picked = held("v2_picked", [P, S], U8)
-        v_picked = held("v_picked", [P, S], U8)
+        v2_plane, w2_plane = e_planes[:, 0:S], e_planes[:, S : S + H]
+        v2_picked_scales = held("v2_picked_scales", [P, S], U8)
+        v_picked_scales = held("v_picked_scales", [P, S], U8)
         v_codes = [held("v_codes%d" % a, [P, S], U32) for a in range(2)]
-        v_planes = held("v_planes", [P, S], U8) if O.get("spreadA") else v_picked
+        v_planes = held("v_planes", [P, S], U8)
         v2_codes = [held("v2_codes%d" % h, [P, HALF], U32) for h in range(2)]
-        v2_plane = e_planes[:, 0:S] if O.get("spreadE") else v2_picked[:]
         gain = held("gain", [P, 2, PACK], F32)
         inv_cap = held("inv_cap", [P, PACK], F32)
         w1_raw = {(a, b): float_rows("w1_raw%d%d" % (a, b), PASS) for b in range(2) for a in range(2)}
         wc_raw = [held("wc_raw%d" % b, [P, PACK, N], F32) for b in range(2)]
         w1_codes = {ab: held("w1_codes%d%d" % ab, [P, PASS], U32) for ab in w1_raw}
         w1_plane = {ab: held("w1_plane%d%d" % ab, [P, PASS], U8) for ab in w1_raw}
-        wc_codes_all = held("wc_codes", [P, 2 * N], U32)
-        wc_plane_all = held("wc_plane", [P, 2 * N], U8)
-        wc_codes = [wc_codes_all[:, N * b : N * (b + 1)] for b in range(2)]
-        wc_plane = [wc_plane_all[:, N * b : N * (b + 1)] for b in range(2)]
+        wc_codes = held("wc_codes", [P, 2, N], U32)
+        wc_plane = held("wc_plane", [P, 2, N], U8)
         force = [held("force%d" % b, [P, PACK, S], F32) for b in range(2)]
-        y_tiles = {}
-        cur_codes = {}
         cur_plane = [held("cur_plane%d" % b, [P, S], U8) for b in range(2)]
         y_plane = held("y_plane", [P, S], U8)
         conductance = {}
+        cur_codes = {}
+        cur_rounded = {}
 
         def half(h):
             return slice(HALF * h, HALF * (h + 1))
 
+        def dealt_rows(rows):
+            return rows.rearrange("(p t) n -> p t n", t=PACK)
+
+        def move_bytes(dst, src):
+            nc.sync.dma_start(out=dst.bitcast(I32), in_=src.bitcast(I32))
+
         def load_words(tile, words):
             nc.sync.dma_start(out=tile[:], in_=words.rearrange("p t i -> p (t i)").bitcast(I32))
 
-        def load_two_planes(tile, scales):
-            for q in range(4):
-                p0 = QUADRANT * q + V_PLANE_ROW
-                (nc.gpsimd if O.get("qs1", "P") == "G" else nc.sync).dma_start(
-                    out=tile[p0 : p0 + 8, :].bitcast(I32), in_=scales[:, 4 * q : 4 * q + 4, :].bitcast(I32)
-                )
+        def load_spread(tile, rows, shift):
+            move_bytes(tile[shift:P:SPREAD, :], rows)
 
-        Q = {"P": nc.sync, "G": nc.gpsimd, "S": nc.scalar}
-
-        def load_plane(tile, scales, queue):
-            rows = scales.rearrange("(q r) n -> r q n", r=4)
-            for r in range(4):
-                Q[queue].dma_start(out=tile[r:P:QUADRANT, :].bitcast(I32), in_=rows[r].bitcast(I32))
-
-        def load_rows(tile, rows):
-            nc.sync.dma_start(out=tile, in_=rows.rearrange("(p t) n -> p t n", t=PACK))
+        def close_up(tile, shifts):
+            for r in range(1, 4):
+                for shift in shifts:
+                    move_bytes(tile[shift + r : P : QUADRANT, :], tile[shift + SPREAD * r : P : QUADRANT, :])
 
         def load_w1(a, b):
-            load_rows(w1_raw[a, b][:], w1[PASS * a : PASS * (a + 1), PASS * b : PASS * (b + 1)])
+            block = w1[PASS * a : PASS * (a + 1), PASS * b : PASS * (b + 1)]
+            nc.sync.dma_start(out=w1_raw[a, b][:], in_=dealt_rows(block))
 
         def load_wc(b):
-            load_rows(wc_raw[b][:], wc[PASS * b : PASS * (b + 1), :])
+            nc.sync.dma_start(out=wc_raw[b][:], in_=dealt_rows(wc[PASS * b : PASS * (b + 1), :]))
 
-        def load_vm(b, h):
-            load_rows(force[b][:, :, half(h)], vm[PASS * b : PASS * (b + 1), half(h)])
+        def load_vm(b, rows, cols):
+            nc.sync.dma_start(out=force[b][:, rows, cols], in_=dealt_rows(vm[PASS * b : PASS * (b + 1), :])[:, rows, cols])
 
         def gather(dst, table, offsets):
             nc.vector.tensor_copy(out=dst, in_=table.indirect(offsets))
@@ -122,275 +118,207 @@ def tile_list_coupled_ionic_current_kernel(
         def entries(offsets, h):
             return offsets[:, h * HALF // 16 : (h + 1) * HALF // 16]
 
+        def copy_bytes(dst, src):
+            nc.vector.tensor_copy(out=dst.bitcast(I32), in_=src.bitcast(I32))
+
+        def deal(dst, src):
+            nc.vector.tensor_copy(
+                out=dst.rearrange("p (b t m) -> p b m t", b=2, t=PACK),
+                in_=src.rearrange("p (b m t) -> p b m t", b=2, t=PACK),
+            )
+
+        def shared_copy(dst, src, cut):
+            if cut > 0:
+                nc.scalar.copy(out=dst[:, 0:cut], in_=src[:, 0:cut])
+            if cut < dst.shape[1]:
+                nc.vector.tensor_copy(out=dst[:, cut:], in_=src[:, cut:])
+
         def word_walk(side_by_side, by_rows):
             return (
                 side_by_side.rearrange("p (x i t) -> p x t i", t=PACK, i=4),
                 [rows.rearrange("p t (x i) -> p x t i", i=4) for rows in by_rows],
             )
 
-        def quantize_weight(label, raw, codes, plane, slot, rounded=None):
-            alone = rounded is None
-            if alone:
-                rounded = staged("wr_" + label, slot, [P, PACK * PASS], BF16)
-            dst = rounded[:].rearrange("p (t m i) -> p m i t", t=PACK, i=PACK)
-            src = raw[:].rearrange("p i (m t) -> p m i t", t=PACK)
-            cut = O.get("wcut", {}).get(label, 0 if label in O.get("vround", []) else P)
-            if cut > 0:
-                nc.scalar.copy(out=dst[:, 0:cut], in_=src[:, 0:cut])
-            if cut < P:
-                nc.vector.tensor_copy(out=dst[:, cut:P], in_=src[:, cut:P])
-            if alone:
-                nc.vector.quantize_mx(out=codes[:].bitcast(E4M3), scales=plane[:], in_=rounded[:])
+        def quantize_weight(raw, codes, plane, rounded, scalar_keeps):
+            shared_copy(
+                rounded[:].rearrange("p (t m i) -> p m i t", t=PACK, i=PACK),
+                raw[:].rearrange("p i (m t) -> p m i t", t=PACK),
+                scalar_keeps,
+            )
+            nc.vector.quantize_mx(out=codes.bitcast(E4M3), scales=plane, in_=rounded[:])
 
-        def quantize_w1(a, b, slot):
-            quantize_weight("w%d%d" % (a, b), w1_raw[a, b], w1_codes[a, b], w1_plane[a, b], slot)
+        def quantize_w1(a, b, scalar_keeps):
+            rounded = staged("w1_rounded", "w1_pass%d" % a, [P, PACK * PASS], BF16)
+            quantize_weight(w1_raw[a, b], w1_codes[a, b][:], w1_plane[a, b][:], rounded, scalar_keeps)
 
-        def quantize_wc(b, slot):
-            quantize_weight("wc%d" % b, wc_raw[b], wc_codes[b], wc_plane[b], slot)
+        def quantize_wc(b):
+            rounded = staged("wc_rounded", "wc%d" % b, [P, PACK * N], BF16)
+            quantize_weight(wc_raw[b], wc_codes[:, b, :], wc_plane[:, b, :], rounded, P if b == 0 else 0)
 
-        def load_vm_t(b, t):
-            nc.sync.dma_start(out=force[b][:, t, :], in_=vm[PASS * b : PASS * (b + 1), :].rearrange("(p t) n -> t p n", t=PACK)[t])
-
-        def who(b, h, t):
-            return O.get("gain", "GGGGGGGS")[2 * t + h] if b == 0 else O.get("gain1", "GGGGGGGS")[2 * t + h]
+        def gain_on_force(b, h, t):
+            return t < GPSIMD_ROWS and (b, h) != (1, 1)
 
         def make_conductance(b, h, slot):
-            tile = staged("cond%d%d" % (b, h), slot, [P, PACK, HALF], F32)
+            tile = staged("conductance", slot, [P, PACK, HALF], F32)
             conductance[b, h] = tile
             for t in range(PACK):
-                acc = bank("a_bank", "a")
+                sums = bank("drive")
                 places = slice(P * t, P * (t + 1))
                 for a in range(2):
                     nc.tensor.matmul_mx(
-                        out=acc[:],
+                        out=sums[:],
                         lhsT=w1_codes[a, b][:, places].bitcast(E4M3),
                         lhsT_scale=w1_plane[a, b][:, places],
                         rhs=v_codes[a][:, half(h)].bitcast(E4M3),
-                        rhs_scale=v_planes[V_PLANE_ROW + 4 * a : P, half(h)],
+                        rhs_scale=v_planes[PLANE_SHIFT * a : P, half(h)],
                         start=(a == 0),
                         stop=(a == 1),
                     )
-                nc.scalar.activation(out=tile[:, t, :], in_=acc[:], func=ACT.Sigmoid)
+                nc.scalar.activation(out=tile[:, t, :], in_=sums[:], func=ACT.Sigmoid)
             for t in range(PACK):
-                g, factor = tile[:, t, :], gain[:, b, t : t + 1]
-                if who(b, h, t) == "S":
-                    nc.scalar.activation(out=g, in_=g, func=ACT.Copy, scale=factor)
-                if who(b, h, t) == "V":
-                    nc.vector.tensor_scalar(out=g, in0=g, scalar1=factor, scalar2=None, op0=ALU.mult)
+                if not gain_on_force(b, h, t):
+                    g = tile[:, t, :]
+                    nc.scalar.activation(out=g, in_=g, func=ACT.Copy, scale=gain[:, b, t : t + 1])
 
-        def make_force(b, h, t, x0=0, w=HALF):
-            acc = bank("e_bank", O.get("ering", "e"))
+        def make_force(b, t, j0, w):
+            h, x0 = divmod(j0, HALF)
+            sums = bank("reversal")
             place = PASS * b + P * t
             nc.tensor.matmul_mx(
-                out=acc[:, 0:w],
+                out=sums[:, 0:w],
                 lhsT=w2_codes[:, 2 * place : 2 * (place + P)].bitcast(E2M1),
                 lhsT_scale=w2_plane[:, place : place + P],
                 rhs=v2_codes[h][:, x0 : x0 + w].bitcast(E4M3),
-                rhs_scale=v2_plane[:, HALF * h + x0 : HALF * h + x0 + w],
+                rhs_scale=v2_plane[:, j0 : j0 + w],
                 start=True,
                 stop=True,
             )
-            d = force[b][:, t, HALF * h + x0 : HALF * h + x0 + w]
-            nc.vector.tensor_tensor(out=d, in0=d, in1=acc[:, 0:w], op=ALU.subtract)
-            if who(b, h, t) == "G":
-                nc.gpsimd.tensor_scalar(out=d, in0=d, scalar1=gain[:, b, t : t + 1], scalar2=0.0, op0=ALU.mult, op1=ALU.add)
-
-        rounded_cur = {}
+            d = force[b][:, t, j0 : j0 + w]
+            nc.vector.tensor_tensor(out=d, in0=d, in1=sums[:, 0:w], op=ALU.subtract)
+            if gain_on_force(b, h, t):
+                nc.gpsimd.tensor_scalar(
+                    out=d, in0=d, scalar1=gain[:, b, t : t + 1], scalar2=0.0, op0=ALU.mult, op1=ALU.add
+                )
 
         def make_current(b, j0, w, slot):
-            cols = slice(j0, j0 + w)
             h, x0 = divmod(j0, HALF)
-            rounded = staged("cur_r%d_%d" % (b, j0), slot, [P, PACK * w], BF16)
-            rounded_cur[b, j0] = rounded
-            dst, (g, d) = word_walk(rounded[:], [conductance[b, h][:, :, x0 : x0 + w], force[b][:, :, cols]])
+            rounded = staged("cur_rounded", slot, [P, PACK * w], BF16)
+            cur_rounded[b, j0] = rounded
+            dst, (g, d) = word_walk(rounded[:], [conductance[b, h][:, :, x0 : x0 + w], force[b][:, :, j0 : j0 + w]])
             nc.vector.tensor_tensor(out=dst, in0=g, in1=d, op=ALU.mult)
 
         def quantize_current(b, j0, w):
-            cols = slice(j0, j0 + w)
+            h, x0 = divmod(j0, HALF)
             nc.vector.quantize_mx(
-                out=cur_codes[b, j0 // HALF][:, j0 % HALF : j0 % HALF + w].bitcast(E4M3), scales=cur_plane[b][:, cols], in_=rounded_cur[b, j0][:]
+                out=cur_codes[b, h][:, x0 : x0 + w].bitcast(E4M3),
+                scales=cur_plane[b][:, j0 : j0 + w],
+                in_=cur_rounded[b, j0][:],
             )
 
-        def make_output(c):
-            j0, w = OUT_RANGES[c]
-            cols = slice(j0, j0 + w)
-            y = float_rows("y%d" % c, w)
-            if c == 0:
-                y_tiles[0] = staged("y_codes", O.get("yslot", "yc"), [P, S], U32)
-            y_codes = y_tiles[0]
-            per = O.get("per", [HALF // x[1] for x in OUT_RANGES])[c]
-            acc = None
+        def make_output(c, bank_ring, scalar_rounds):
+            cols = slice(QUARTER * c, QUARTER * (c + 1))
+            h, x0 = divmod(QUARTER * c, HALF)
+            y = float_rows("y", QUARTER)
             for t in range(PACK):
-                if t % per == 0:
-                    acc = bank("c_bank", O.get("cring", "aeaeaeae")[c])
-                part = acc[:, (t % per) * w : (t % per + 1) * w]
+                sums = bank(bank_ring)[:, 0:QUARTER]
                 places = slice(P * t, P * (t + 1))
                 for b in range(2):
                     nc.tensor.matmul_mx(
-                        out=part,
-                        lhsT=wc_codes[b][:, places].bitcast(E4M3),
-                        lhsT_scale=wc_plane[b][:, places],
-                        rhs=cur_codes[b, j0 // HALF][:, j0 % HALF : j0 % HALF + w].bitcast(E4M3),
+                        out=sums,
+                        lhsT=wc_codes[:, b, places].bitcast(E4M3),
+                        lhsT_scale=wc_plane[:, b, places],
+                        rhs=cur_codes[b, h][:, x0 : x0 + QUARTER].bitcast(E4M3),
                         rhs_scale=cur_plane[b][:, cols],
                         start=(b == 0),
                         stop=(b == 1),
                     )
-                if (t + 1) % per == 0:
-                    for u in range(t + 1 - per, t + 1):
-                        factor = inv_cap[:, u : u + 1]
-                        part = acc[:, (u % per) * w : (u % per + 1) * w]
-                        if O.get("yout", ["SSSS"] * 8)[c][u] == "V":
-                            nc.vector.tensor_scalar(out=y[:, u, :], in0=part, scalar1=factor, scalar2=None, op0=ALU.mult)
-                        else:
-                            nc.scalar.activation(out=y[:, u, :], in_=part, func=ACT.Copy, scale=factor)
-            Q[O.get("q0", "PPPPPPPP")[c]].dma_start(out=out_0[:, cols].rearrange("(p t) j -> p t j", t=PACK), in_=y[:])
-            rounded = staged("y_r%d" % c, O.get("yrslot", ["y0", "y1", "y2", "y3", "y4"])[c], [P, PACK * w], BF16)
+                nc.scalar.activation(out=y[:, t, :], in_=sums, func=ACT.Copy, scale=inv_cap[:, t : t + 1])
+            nc.sync.dma_start(out=dealt_rows(out_0[:, cols]), in_=y[:])
+            rounded = staged("y_rounded", "y%d" % c, [P, PACK * QUARTER], BF16)
             dst, (src,) = word_walk(rounded[:], [y[:]])
-            if O.get("yround", "SVVVVVVV")[c] == "H":
-                cut = O.get("ycut", w // 8)
-                nc.scalar.copy(out=dst[:, 0:cut], in_=src[:, 0:cut])
-                nc.vector.tensor_copy(out=dst[:, cut:], in_=src[:, cut:])
-            elif O.get("yround", "SVVVVVVV")[c] == "S":
-                nc.scalar.copy(out=dst, in_=src)
-            else:
-                nc.vector.tensor_copy(out=dst, in_=src)
+            shared_copy(dst, src, scalar_rounds // 4)
             nc.vector.quantize_mx(out=y_codes[:, cols].bitcast(E4M3), scales=y_plane[:, cols], in_=rounded[:])
-            first = O.get("store1", {}).get(str(c), j0)
-            if first >= 0:
-                Q[O.get("q1", "PPPPPPPP")[c]].dma_start(
-                    out=out_1[0].rearrange("p m t -> p (m t)")[:, PACK * first : PACK * (j0 + w)].bitcast(I32),
-                    in_=y_codes[:, first : j0 + w].bitcast(I32),
-                )
+            words = out_1[0].rearrange("p m t -> p (m t)")
+            move_bytes(words[:, PACK * QUARTER * c : PACK * QUARTER * (c + 1)], y_codes[:, cols])
 
-        for tile in (v_table_planes, v2_table_plane, w2_raw_plane):
+        for tile in (v_table_scales, v2_table_scales, w2_raw_scales):
             nc.vector.memset(tile[:].bitcast(I32), 0)
 
-        L = {
-            "i1": lambda: nc.sync.dma_start(idx[:], offs), "i2": lambda: nc.sync.dma_start(idx2[:], offs2),
-            "t0": lambda: load_words(v_table[0], tab_words[0]), "t1": lambda: load_words(v_table[1], tab_words[1]),
-            "t2": lambda: load_words(v2_table, tab2_words[0]),
-            "s1": lambda: load_two_planes(v_table_planes, tab_scales), "s2": lambda: load_plane(v2_table_plane, tab2_scales[0], O.get("qs2", "P")),
-            "w2": lambda: nc.sync.dma_start(out=w2_raw[:].bitcast(I32), in_=w2_words[0].bitcast(I32)),
-            "sw": lambda: load_plane(w2_raw_plane, w2_scales[0], O.get("qsw", "P")),
-            "g": lambda: Q[O.get("qg", "P")].dma_start(out=gain[:], in_=gmax.rearrange("(b p t) -> p b t", b=2, t=PACK)),
-            "c": lambda: Q[O.get("qg", "P")].dma_start(out=inv_cap[:], in_=cinv.rearrange("(p t) -> p t", t=PACK)),
-            "w00": lambda: load_w1(0, 0), "w10": lambda: load_w1(1, 0), "w01": lambda: load_w1(0, 1), "w11": lambda: load_w1(1, 1),
-            "wc0": lambda: load_wc(0), "wc1": lambda: load_wc(1),
-            "v0": lambda: [load_vm_t(0, t) for t in range(4)], "v1": lambda: [load_vm_t(1, t) for t in range(4)],
-            "v00": lambda: load_vm(0, 0), "v01": lambda: load_vm(0, 1), "v10": lambda: load_vm(1, 0), "v11": lambda: load_vm(1, 1),
-        }
-        def load_vm_pair(b, u):
-            nc.sync.dma_start(out=force[b][:, 2 * u : 2 * u + 2, :], in_=vm[PASS * b : PASS * (b + 1), :].rearrange("(p t) n -> p t n", t=PACK)[:, 2 * u : 2 * u + 2, :])
-
-        def spread(tile, rows, first):
-            nc.sync.dma_start(out=tile[first:P:8, :].bitcast(I32), in_=rows.bitcast(I32))
-
-        def close_up(tile, first, r):
-            nc.sync.dma_start(out=tile[first + r : P : QUADRANT, :].bitcast(I32), in_=tile[first + 8 * r : P : QUADRANT, :].bitcast(I32))
-
-        def pick_v():
-            gather(v_picked[:], v_table_planes[:], idx[:])
-            if O.get("spreadA"):
-                nc.vector.tensor_copy(out=v_planes[:].bitcast(I32), in_=v_picked[:].bitcast(I32))
-
-        def pick_e():
-            gather(v2_picked[:], v2_table_plane[:], idx2[:])
-            if O.get("spreadE"):
-                nc.vector.tensor_copy(out=v2_plane.bitcast(I32), in_=v2_picked[:].bitcast(I32))
-            nc.vector.tensor_copy(
-                out=w2_plane.rearrange("p (b t m) -> p b m t", b=2, t=PACK),
-                in_=w2_raw_plane[:].rearrange("p (b m t) -> p b m t", b=2, t=PACK),
-            )
-
-        for u in range(2):
-            L["w00" + "ab"[u]] = lambda u=u: nc.sync.dma_start(out=w1_raw[0, 0][:, 2 * u : 2 * u + 2, :], in_=w1[0:PASS, 0:PASS].rearrange("(p t) n -> p t n", t=PACK)[:, 2 * u : 2 * u + 2, :])
-        L["pv"] = pick_v
-        L["pe"] = pick_e
-        L["sA"] = lambda: [spread(v_table_planes, tab_scales[a], 4 * a) for a in range(2)]
-        L["sB"] = lambda: spread(v2_table_plane, tab2_scales[0], 0)
-        L["sC"] = lambda: spread(w2_raw_plane, w2_scales[0], 0)
-        for u in range(1, 4):
-            L["mA%d" % u] = lambda u=u: [close_up(v_planes, 4 * a, u) for a in range(2)]
-            L["mE%d" % u] = lambda u=u: close_up(e_planes, 0, u)
-        for u in range(4):
-            L["vp%d%d" % divmod(u, 2)] = lambda u=u: load_vm_pair(u // 2, u % 2)
-        for u in range(PACK):
-            L["v0t%d" % u] = lambda u=u: load_vm_t(0, u)
-        for name in O.get("loads", "i1 t0 s1 i2 s2 w2 sw t2 w00 t1 w10 g v0 w01 w11 v1 wc0 wc1 c").split():
-            L[name]()
+        everything = slice(None)
+        move_bytes(w2_raw[:], w2_words[0])
+        nc.sync.dma_start(idx[:], offs)
+        for a in range(2):
+            load_spread(v_table_scales, tab_scales[a], PLANE_SHIFT * a)
+        load_w1(0, 0)
+        nc.sync.dma_start(idx2[:], offs2)
+        load_spread(v2_table_scales, tab2_scales[0], 0)
+        load_words(v_table[0], tab_words[0])
+        gather(v_picked_scales[:], v_table_scales[:], idx[:])
+        copy_bytes(v_planes[:], v_picked_scales[:])
+        load_spread(w2_raw_scales, w2_scales[0], 0)
+        gather(v2_picked_scales[:], v2_table_scales[:], idx2[:])
+        copy_bytes(v2_plane, v2_picked_scales[:])
+        deal(w2_plane, w2_raw_scales[:])
+        load_w1(1, 0)
+        close_up(v_planes, (0, PLANE_SHIFT))
+        load_words(v_table[1], tab_words[1])
+        nc.sync.dma_start(out=gain[:], in_=gmax.rearrange("(b p t) -> p b t", b=2, t=PACK))
+        load_words(v2_table, tab2_words[0])
+        close_up(e_planes, (0,))
+        load_vm(0, slice(0, 2), everything)
+        load_vm(0, slice(2, 4), everything)
+        load_w1(0, 1)
+        load_w1(1, 1)
+        for bh in range(2):
+            load_wc(bh)
+            load_vm(1, everything, half(bh))
+        nc.sync.dma_start(out=inv_cap[:], in_=cinv.rearrange("(p t) -> p t", t=PACK))
 
         gather(v_codes[0][:], v_table[0][:].bitcast(U32), idx[:])
-        if not O.get("spreadA"):
-            pick_v()
-        if not O.get("spreadE"):
-            pick_e()
-        nc.vector.tensor_copy(
-            out=w2_codes[:].bitcast(U16).rearrange("p (b t m) -> p b m t", b=2, t=PACK),
-            in_=w2_raw[:].bitcast(U16).rearrange("p (b m t) -> p b m t", b=2, t=PACK),
-        )
-        sl = O.get("slots", dict(w01="a", w11="b", c00="c", c01="d", wc0="a", wc1="b"))
-        quantize_w1(0, 0, "a")
-        quantize_w1(1, 0, "b")
+        deal(w2_codes[:].bitcast(U16), w2_raw[:].bitcast(U16))
+        for a in range(2):
+            quantize_w1(a, 0, P)
         for h in range(2):
             gather(v_codes[1][:, half(h)], v_table[1][:].bitcast(U32), entries(idx, h))
         for h in range(2):
             gather(v2_codes[h][:], v2_table[:].bitcast(U32), entries(idx2, h))
-        make_conductance(0, 0, "f32_a")
-        make_conductance(0, 1, "f32_b")
-        quantize_w1(0, 1, sl["w01"])
-        quantize_w1(1, 1, sl["w11"])
-        order0 = [(h, t) for t in range(4) for h in range(2)] if O.get("tmajor0", 1) else [(h, t) for h in range(2) for t in range(4)]
-        order1 = [(h, t) for t in range(4) for h in range(2)] if O.get("tmajor1", 1) else [(h, t) for h in range(2) for t in range(4)]
-        for h, t in order0:
-            make_force(0, h, t)
-        make_conductance(1, 0, "f32_c")
-        make_current(0, 0, HALF, sl["c00"])
-        if O.get("split01"):
-            make_current(0, HALF, QUARTER, sl["c01"])
-            make_current(0, HALF + QUARTER, QUARTER, sl.get("c01b", "b"))
-        else:
-            make_current(0, HALF, HALF, sl["c01"])
-        cur_codes[0, 0] = staged("cur_codes00", sl.get("cur00", "y"), [P, HALF], U32)
-        quantize_current(0, 0, HALF)
-        cur_codes[0, 1] = staged("cur_codes01", sl.get("cur01", "z"), [P, HALF], U32)
-        if O.get("split01"):
-            quantize_current(0, HALF, QUARTER)
-            quantize_current(0, HALF + QUARTER, QUARTER)
-        else:
-            quantize_current(0, HALF, HALF)
-        cur_codes[1, 0] = held("cur_codes10", [P, HALF], U32)
-        cur_codes[1, 1] = held("cur_codes11", [P, HALF], U32)
-        if not O.get("wcfirst"):
-            make_conductance(1, 1, O.get("c11", "f32_a"))
-        if O.get("wideq"):
-            both = staged("wc_rounded", sl.get("wcq", "w"), [P, 2 * PACK * PASS], BF16)
-            for b in range(2):
-                quantize_weight("wc%d" % b, wc_raw[b], None, None, None, both[:, PACK * PASS * b : PACK * PASS * (b + 1)])
-            nc.vector.quantize_mx(out=wc_codes_all[:].bitcast(E4M3), scales=wc_plane_all[:], in_=both[:])
-        else:
-            quantize_wc(0, sl["wc0"])
-            quantize_wc(1, sl["wc1"])
-        if O.get("wcfirst"):
-            make_conductance(1, 1, O.get("c11", "f32_a"))
-        for h, t in order1:
-            if O.get("tmajor1", 1) or h == 0:
-                make_force(1, h, t)
-        for c, (j0, w) in enumerate(OUT_RANGES):
-            if j0 == HALF and not O.get("tmajor1", 1) and not O.get("split", 0):
+        for h in range(2):
+            make_conductance(0, h, "conductance%d" % h)
+        quantize_w1(0, 1, P)
+        quantize_w1(1, 1, SCALAR_KEEPS_LAST_W1)
+        for t in range(PACK):
+            for h in range(2):
+                make_force(0, t, HALF * h, HALF)
+        make_conductance(1, 0, "conductance2")
+        pieces = ((0, HALF, "cur_first"), (HALF, QUARTER, "cur_third"), (HALF + QUARTER, QUARTER, "w1_pass1"))
+        for j0, w, slot in pieces:
+            make_current(0, j0, w, slot)
+        for h in range(2):
+            cur_codes[0, h] = staged("cur_codes", "cur_codes%d" % h, [P, HALF], U32)
+        for j0, w, slot in pieces:
+            quantize_current(0, j0, w)
+
+        for h in range(2):
+            cur_codes[1, h] = held("cur_codes1%d" % h, [P, HALF], U32)
+        make_conductance(1, 1, "conductance0")
+        for b in range(2):
+            quantize_wc(b)
+        for t in range(PACK):
+            make_force(1, t, 0, HALF)
+        for c in range(4):
+            if c >= 2:
                 for t in range(PACK):
-                    make_force(1, 1, t)
-            if j0 >= HALF and O.get("split", 0):
-                for t in range(PACK):
-                    make_force(1, 1, t, j0 - HALF, w)
-            make_current(1, j0, w, O.get("cslot", "cdefcdef")[c])
-            quantize_current(1, j0, w)
-            if c > 0 and O.get("weave", 1):
-                make_output(c - 1)
-        for c in range(len(OUT_RANGES)):
-            if c == len(OUT_RANGES) - 1 or not O.get("weave", 1):
-                make_output(c)
+                    make_force(1, t, QUARTER * c, QUARTER)
+            make_current(1, QUARTER * c, QUARTER, "cur_first" if c < 2 else "cur_second")
+            quantize_current(1, QUARTER * c, QUARTER)
+
+        y_codes = staged("y_codes", "y_codes", [P, S], U32)
+        make_output(0, "drive", QUARTER // 2)
+        make_output(1, "drive", 0)
+        make_output(2, "reversal", QUARTER // 2)
+        make_output(3, "drive", QUARTER // 2)
 
         out_rows = out_2[0].rearrange("(q r) m -> r q m", r=4)
         for r in range(4):
-            queue = Q[O.get("q2", "PSPS")[r]]
+            queue = nc.sync if r % 2 == 0 else nc.scalar
             queue.dma_start(out=out_rows[r].bitcast(I32), in_=y_plane[r:P:QUADRANT, :].bitcast(I32))

@@ -25,8 +25,7 @@ PLANE_SHIFT = 4
 RING_BANKS = 4
 HALF = S // 2
 QUARTER = S // 4
-SCALAR_KEEPS_LAST_W1 = 96
-GPSIMD_ROWS = 2
+WALK = 2
 
 
 def tile_list_coupled_ionic_current_kernel(
@@ -53,20 +52,20 @@ def tile_list_coupled_ionic_current_kernel(
 
         idx = held("idx", [P, S // 16], U16)
         idx2 = held("idx2", [P, S // 16], U16)
-        v_table = [held("v_table%d" % a, [P, T], I32) for a in range(2)]
+        v_table = [staged("v_table%d" % a, "table%d" % a, [P, T], I32) for a in range(2)]
         v_table_scales = held("v_table_scales", [P, T], U8)
-        v2_table = held("v2_table", [P, T2], I32)
+        v2_table = staged("v2_table", "table2", [P, T2], I32)
         v2_table_scales = held("v2_table_scales", [P, T2], U8)
         w2_raw = held("w2_raw", [P, 2 * H], U8)
         w2_raw_scales = held("w2_raw_scales", [P, H], U8)
-        w2_codes = held("w2_codes", [P, 2 * H], U8)
-        e_planes = held("e_planes", [P, S + H], U8)
+        w2_codes = staged("w2_codes", "w2_codes", [P, 2 * H], U8)
+        e_planes = staged("e_planes", "e_planes", [P, S + H], U8)
         v2_plane, w2_plane = e_planes[:, 0:S], e_planes[:, S : S + H]
         v2_picked_scales = held("v2_picked_scales", [P, S], U8)
         v_picked_scales = held("v_picked_scales", [P, S], U8)
         v_codes = [held("v_codes%d" % a, [P, S], U32) for a in range(2)]
         v_planes = held("v_planes", [P, S], U8)
-        v2_codes = [held("v2_codes%d" % h, [P, HALF], U32) for h in range(2)]
+        v2_codes = [staged("v2_codes%d" % h, "v2_codes%d" % h, [P, HALF], U32) for h in range(2)]
         gain = held("gain", [P, 2, PACK], F32)
         inv_cap = held("inv_cap", [P, PACK], F32)
         w1_raw = {(a, b): float_rows("w1_raw%d%d" % (a, b), PASS) for b in range(2) for a in range(2)}
@@ -75,7 +74,10 @@ def tile_list_coupled_ionic_current_kernel(
         w1_plane = {ab: held("w1_plane%d%d" % ab, [P, PASS], U8) for ab in w1_raw}
         wc_codes = held("wc_codes", [P, 2, N], U32)
         wc_plane = held("wc_plane", [P, 2, N], U8)
-        force = [held("force%d" % b, [P, PACK, S], F32) for b in range(2)]
+        force_rows = held("force0", [P, PACK, S], F32)
+        force = {(0, h): force_rows[:, :, HALF * h : HALF * (h + 1)] for h in range(2)}
+        for h in range(2):
+            force[1, h] = held("force1%d" % h, [P, PACK, HALF], F32)[:]
         cur_plane = [held("cur_plane%d" % b, [P, S], U8) for b in range(2)]
         y_plane = held("y_plane", [P, S], U8)
         conductance = {}
@@ -109,8 +111,14 @@ def tile_list_coupled_ionic_current_kernel(
         def load_wc(b):
             nc.sync.dma_start(out=wc_raw[b][:], in_=dealt_rows(wc[PASS * b : PASS * (b + 1), :]))
 
+        def force_at(b, rows, j0, j1):
+            if j1 - j0 == S:
+                return force_rows[:, rows, :]
+            return force[b, j0 // HALF][:, rows, j0 % HALF : j0 % HALF + j1 - j0]
+
         def load_vm(b, rows, cols):
-            nc.sync.dma_start(out=force[b][:, rows, cols], in_=dealt_rows(vm[PASS * b : PASS * (b + 1), :])[:, rows, cols])
+            source = dealt_rows(vm[PASS * b : PASS * (b + 1), :])[:, rows, cols]
+            nc.sync.dma_start(out=force_at(b, rows, cols.start, cols.stop), in_=source)
 
         def gather(dst, table, offsets):
             nc.vector.tensor_copy(out=dst, in_=table.indirect(offsets))
@@ -135,31 +143,39 @@ def tile_list_coupled_ionic_current_kernel(
 
         def word_walk(side_by_side, by_rows):
             return (
-                side_by_side.rearrange("p (x i t) -> p x t i", t=PACK, i=4),
-                [rows.rearrange("p t (x i) -> p x t i", i=4) for rows in by_rows],
+                side_by_side.rearrange("p (x i t) -> p x t i", t=PACK, i=WALK),
+                [rows.rearrange("p t (x i) -> p x t i", i=WALK) for rows in by_rows],
             )
 
-        def quantize_weight(raw, codes, plane, rounded, scalar_keeps):
+        rounded_weight = {}
+
+        def round_weight(key, raw, slot, scalar_keeps):
+            rounded = staged("w_rounded", slot, [P, PACK * PASS], BF16)
+            rounded_weight[key] = rounded
             shared_copy(
                 rounded[:].rearrange("p (t m i) -> p m i t", t=PACK, i=PACK),
-                raw[:].rearrange("p i (m t) -> p m i t", t=PACK),
+                raw.rearrange("p i (m t) -> p m i t", t=PACK),
                 scalar_keeps,
             )
-            nc.vector.quantize_mx(out=codes.bitcast(E4M3), scales=plane, in_=rounded[:])
 
-        def quantize_w1(a, b, scalar_keeps):
-            rounded = staged("w1_rounded", "w1_pass%d" % a, [P, PACK * PASS], BF16)
-            quantize_weight(w1_raw[a, b], w1_codes[a, b][:], w1_plane[a, b][:], rounded, scalar_keeps)
+        def round_w1(a, b, scalar_keeps):
+            round_weight(("w1", a, b), w1_raw[a, b][:], "w1_pass%d" % a, scalar_keeps)
+
+        def quantize_w1(a, b):
+            nc.vector.quantize_mx(
+                out=w1_codes[a, b][:].bitcast(E4M3), scales=w1_plane[a, b][:], in_=rounded_weight["w1", a, b][:]
+            )
+
+        def round_wc(b, scalar_keeps):
+            round_weight(("wc", b), wc_raw[b][:], "wc%d" % b, scalar_keeps)
 
         def quantize_wc(b):
-            rounded = staged("wc_rounded", "wc%d" % b, [P, PACK * N], BF16)
-            quantize_weight(wc_raw[b], wc_codes[:, b, :], wc_plane[:, b, :], rounded, P if b == 0 else 0)
+            nc.vector.quantize_mx(
+                out=wc_codes[:, b, :].bitcast(E4M3), scales=wc_plane[:, b, :], in_=rounded_weight["wc", b][:]
+            )
 
-        def gain_on_force(b, h, t):
-            return t < GPSIMD_ROWS and (b, h) != (1, 1)
-
-        def make_conductance(b, h, slot):
-            tile = staged("conductance", slot, [P, PACK, HALF], F32)
+        def make_sigmoids(b, h):
+            tile = staged("conductance", ("conductance%d", "table%d")[b] % h, [P, PACK, HALF], F32)
             conductance[b, h] = tile
             for t in range(PACK):
                 sums = bank("drive")
@@ -175,10 +191,15 @@ def tile_list_coupled_ionic_current_kernel(
                         stop=(a == 1),
                     )
                 nc.scalar.activation(out=tile[:, t, :], in_=sums[:], func=ACT.Sigmoid)
-            for t in range(PACK):
-                if not gain_on_force(b, h, t):
-                    g = tile[:, t, :]
-                    nc.scalar.activation(out=g, in_=g, func=ACT.Copy, scale=gain[:, b, t : t + 1])
+
+        def gain_on_sigmoid(b, h, rows):
+            for t in rows:
+                g = conductance[b, h][:, t, :]
+                nc.scalar.activation(out=g, in_=g, func=ACT.Copy, scale=gain[:, b, t : t + 1])
+
+        def gain_on_force(b, t, j0, w):
+            d = force_at(b, t, j0, j0 + w)
+            nc.gpsimd.tensor_scalar(out=d, in0=d, scalar1=gain[:, b, t : t + 1], scalar2=0.0, op0=ALU.mult, op1=ALU.add)
 
         def make_force(b, t, j0, w):
             h, x0 = divmod(j0, HALF)
@@ -193,71 +214,90 @@ def tile_list_coupled_ionic_current_kernel(
                 start=True,
                 stop=True,
             )
-            d = force[b][:, t, j0 : j0 + w]
+            d = force_at(b, t, j0, j0 + w)
             nc.vector.tensor_tensor(out=d, in0=d, in1=sums[:, 0:w], op=ALU.subtract)
-            if gain_on_force(b, h, t):
-                nc.gpsimd.tensor_scalar(
-                    out=d, in0=d, scalar1=gain[:, b, t : t + 1], scalar2=0.0, op0=ALU.mult, op1=ALU.add
-                )
 
-        def make_current(b, j0, w, slot):
-            h, x0 = divmod(j0, HALF)
-            rounded = staged("cur_rounded", slot, [P, PACK * w], BF16)
-            cur_rounded[b, j0] = rounded
-            dst, (g, d) = word_walk(rounded[:], [conductance[b, h][:, :, x0 : x0 + w], force[b][:, :, j0 : j0 + w]])
-            nc.vector.tensor_tensor(out=dst, in0=g, in1=d, op=ALU.mult)
+        def make_forces(b, j0, w, rows, gpsimd_rows):
+            for t in rows:
+                make_force(b, t, j0, w)
+                if t < gpsimd_rows:
+                    gain_on_force(b, t, j0, w)
 
-        def quantize_current(b, j0, w):
+        def make_current(engine, b, j0, j1, base, width, slot):
+            if (b, base) not in cur_rounded:
+                cur_rounded[b, base] = staged("cur_rounded", slot, [P, PACK * width], BF16)
+            dst, (g, d) = word_walk(
+                cur_rounded[b, base][:, PACK * (j0 - base) : PACK * (j1 - base)],
+                [conductance[b, j0 // HALF][:, :, j0 % HALF : j0 % HALF + j1 - j0], force_at(b, slice(None), j0, j1)],
+            )
+            engine.tensor_tensor(out=dst, in0=g, in1=d, op=ALU.mult)
+
+        def quantize_current(b, j0, w, slot):
             h, x0 = divmod(j0, HALF)
+            if (b, h) not in cur_codes:
+                cur_codes[b, h] = staged("cur_codes", slot, [P, HALF], U32)
             nc.vector.quantize_mx(
                 out=cur_codes[b, h][:, x0 : x0 + w].bitcast(E4M3),
                 scales=cur_plane[b][:, j0 : j0 + w],
                 in_=cur_rounded[b, j0][:],
             )
 
-        def make_output(c, bank_ring, scalar_rounds):
-            cols = slice(QUARTER * c, QUARTER * (c + 1))
-            h, x0 = divmod(QUARTER * c, HALF)
-            y = float_rows("y", QUARTER)
+        y_rows = {}
+        y_rounded = {}
+
+        def make_y(j0, w, bank_ring, vector_rows=()):
+            cols = slice(j0, j0 + w)
+            h, x0 = divmod(j0, HALF)
+            y = float_rows("y", w)
+            y_rows[j0] = y
             for t in range(PACK):
-                sums = bank(bank_ring)[:, 0:QUARTER]
+                sums = bank(bank_ring)[:, 0:w]
                 places = slice(P * t, P * (t + 1))
                 for b in range(2):
                     nc.tensor.matmul_mx(
                         out=sums,
                         lhsT=wc_codes[:, b, places].bitcast(E4M3),
                         lhsT_scale=wc_plane[:, b, places],
-                        rhs=cur_codes[b, h][:, x0 : x0 + QUARTER].bitcast(E4M3),
+                        rhs=cur_codes[b, h][:, x0 : x0 + w].bitcast(E4M3),
                         rhs_scale=cur_plane[b][:, cols],
                         start=(b == 0),
                         stop=(b == 1),
                     )
-                nc.scalar.activation(out=y[:, t, :], in_=sums, func=ACT.Copy, scale=inv_cap[:, t : t + 1])
+                if t in vector_rows:
+                    nc.vector.tensor_scalar(
+                        out=y[:, t, :], in0=sums, scalar1=inv_cap[:, t : t + 1], scalar2=None, op0=ALU.mult
+                    )
+                else:
+                    nc.scalar.activation(out=y[:, t, :], in_=sums, func=ACT.Copy, scale=inv_cap[:, t : t + 1])
             nc.sync.dma_start(out=dealt_rows(out_0[:, cols]), in_=y[:])
-            rounded = staged("y_rounded", "y%d" % c, [P, PACK * QUARTER], BF16)
-            dst, (src,) = word_walk(rounded[:], [y[:]])
-            shared_copy(dst, src, scalar_rounds // 4)
-            nc.vector.quantize_mx(out=y_codes[:, cols].bitcast(E4M3), scales=y_plane[:, cols], in_=rounded[:])
+
+        def round_y(j0, w, scalar_rounds):
+            rounded = staged("y_rounded", "y%d" % j0, [P, PACK * w], BF16)
+            y_rounded[j0] = rounded
+            dst, (src,) = word_walk(rounded[:], [y_rows[j0][:]])
+            shared_copy(dst, src, scalar_rounds // WALK)
+
+        def quantize_y(j0, w):
+            cols = slice(j0, j0 + w)
+            nc.vector.quantize_mx(out=y_codes[:, cols].bitcast(E4M3), scales=y_plane[:, cols], in_=y_rounded[j0][:])
             words = out_1[0].rearrange("p m t -> p (m t)")
-            move_bytes(words[:, PACK * QUARTER * c : PACK * QUARTER * (c + 1)], y_codes[:, cols])
+            move_bytes(words[:, PACK * j0 : PACK * (j0 + w)], y_codes[:, cols])
 
         for tile in (v_table_scales, v2_table_scales, w2_raw_scales):
             nc.vector.memset(tile[:].bitcast(I32), 0)
-
         everything = slice(None)
+        y_codes = staged("y_codes", "y_codes", [P, S], U32)
         move_bytes(w2_raw[:], w2_words[0])
         nc.sync.dma_start(idx[:], offs)
-        for a in range(2):
-            load_spread(v_table_scales, tab_scales[a], PLANE_SHIFT * a)
+        load_spread(v_table_scales, tab_scales[0], 0)
+        load_spread(v_table_scales, tab_scales[1], PLANE_SHIFT)
         load_w1(0, 0)
         nc.sync.dma_start(idx2[:], offs2)
         load_spread(v2_table_scales, tab2_scales[0], 0)
         load_words(v_table[0], tab_words[0])
-        gather(v_picked_scales[:], v_table_scales[:], idx[:])
-        copy_bytes(v_planes[:], v_picked_scales[:])
+        gather(v_picked_scales[:], v_table_scales[:], idx[:]); copy_bytes(v_planes[:], v_picked_scales[:])
         load_spread(w2_raw_scales, w2_scales[0], 0)
-        gather(v2_picked_scales[:], v2_table_scales[:], idx2[:])
-        copy_bytes(v2_plane, v2_picked_scales[:])
+        gather(v2_picked_scales[:], v2_table_scales[:], idx2[:]); copy_bytes(v2_plane, v2_picked_scales[:])
         deal(w2_plane, w2_raw_scales[:])
         load_w1(1, 0)
         close_up(v_planes, (0, PLANE_SHIFT))
@@ -265,58 +305,74 @@ def tile_list_coupled_ionic_current_kernel(
         nc.sync.dma_start(out=gain[:], in_=gmax.rearrange("(b p t) -> p b t", b=2, t=PACK))
         load_words(v2_table, tab2_words[0])
         close_up(e_planes, (0,))
-        load_vm(0, slice(0, 2), everything)
-        load_vm(0, slice(2, 4), everything)
+        load_vm(0, slice(0, 2), slice(0, 1024))
+        load_vm(0, slice(2, 4), slice(0, 1024))
         load_w1(0, 1)
         load_w1(1, 1)
-        for bh in range(2):
-            load_wc(bh)
-            load_vm(1, everything, half(bh))
+        load_wc(0)
+        load_vm(1, slice(0, 4), slice(0, 512))
+        load_wc(1)
+        load_vm(1, slice(0, 4), slice(512, 1024))
         nc.sync.dma_start(out=inv_cap[:], in_=cinv.rearrange("(p t) -> p t", t=PACK))
-
         gather(v_codes[0][:], v_table[0][:].bitcast(U32), idx[:])
         deal(w2_codes[:].bitcast(U16), w2_raw[:].bitcast(U16))
-        for a in range(2):
-            quantize_w1(a, 0, P)
-        for h in range(2):
-            gather(v_codes[1][:, half(h)], v_table[1][:].bitcast(U32), entries(idx, h))
-        for h in range(2):
-            gather(v2_codes[h][:], v2_table[:].bitcast(U32), entries(idx2, h))
-        for h in range(2):
-            make_conductance(0, h, "conductance%d" % h)
-        quantize_w1(0, 1, P)
-        quantize_w1(1, 1, SCALAR_KEEPS_LAST_W1)
-        for t in range(PACK):
-            for h in range(2):
-                make_force(0, t, HALF * h, HALF)
-        make_conductance(1, 0, "conductance2")
-        pieces = ((0, HALF, "cur_first"), (HALF, QUARTER, "cur_third"), (HALF + QUARTER, QUARTER, "w1_pass1"))
-        for j0, w, slot in pieces:
-            make_current(0, j0, w, slot)
-        for h in range(2):
-            cur_codes[0, h] = staged("cur_codes", "cur_codes%d" % h, [P, HALF], U32)
-        for j0, w, slot in pieces:
-            quantize_current(0, j0, w)
-
-        for h in range(2):
-            cur_codes[1, h] = held("cur_codes1%d" % h, [P, HALF], U32)
-        make_conductance(1, 1, "conductance0")
-        for b in range(2):
-            quantize_wc(b)
-        for t in range(PACK):
-            make_force(1, t, 0, HALF)
-        for c in range(4):
-            if c >= 2:
-                for t in range(PACK):
-                    make_force(1, t, QUARTER * c, QUARTER)
-            make_current(1, QUARTER * c, QUARTER, "cur_first" if c < 2 else "cur_second")
-            quantize_current(1, QUARTER * c, QUARTER)
-
-        y_codes = staged("y_codes", "y_codes", [P, S], U32)
-        make_output(0, "drive", QUARTER // 2)
-        make_output(1, "drive", 0)
-        make_output(2, "reversal", QUARTER // 2)
-        make_output(3, "drive", QUARTER // 2)
+        round_w1(0, 0, 128)
+        quantize_w1(0, 0)
+        round_w1(1, 0, 128)
+        quantize_w1(1, 0)
+        gather(v_codes[1][:, half(0)], v_table[1][:].bitcast(U32), entries(idx, 0))
+        gather(v_codes[1][:, half(1)], v_table[1][:].bitcast(U32), entries(idx, 1))
+        gather(v2_codes[0][:], v2_table[:].bitcast(U32), entries(idx2, 0))
+        gather(v2_codes[1][:], v2_table[:].bitcast(U32), entries(idx2, 1))
+        make_sigmoids(0, 0)
+        gain_on_sigmoid(0, 0, range(2, 4))
+        make_sigmoids(0, 1)
+        gain_on_sigmoid(0, 1, range(2, 4))
+        round_w1(0, 1, 128)
+        quantize_w1(0, 1)
+        round_w1(1, 1, 96)
+        quantize_w1(1, 1)
+        make_forces(0, 0, 512, range(0, 2), 2)
+        make_forces(0, 512, 512, range(0, 2), 2)
+        make_forces(0, 0, 512, range(2, 4), 2)
+        make_forces(0, 512, 512, range(2, 4), 2)
+        make_sigmoids(1, 0)
+        gain_on_sigmoid(1, 0, range(2, 4))
+        make_current(nc.vector, 0, 0, 512, 0, 512, "A")
+        make_current(nc.vector, 0, 512, 768, 512, 256, "u01")
+        make_current(nc.vector, 0, 768, 1024, 768, 256, "w1_pass1")
+        quantize_current(0, 0, 512, "cc0")
+        quantize_current(0, 512, 256, "cc1")
+        quantize_current(0, 768, 256, "cc1")
+        make_sigmoids(1, 1)
+        gain_on_sigmoid(1, 1, range(0, 4))
+        round_wc(0, 128)
+        quantize_wc(0)
+        round_wc(1, 0)
+        quantize_wc(1)
+        make_forces(1, 0, 512, range(0, 4), 2)
+        make_current(nc.vector, 1, 0, 256, 0, 256, "A")
+        quantize_current(1, 0, 256, "cc2")
+        make_current(nc.vector, 1, 256, 512, 256, 256, "A")
+        quantize_current(1, 256, 256, "cc2")
+        make_forces(1, 512, 256, range(0, 4), 0)
+        make_current(nc.vector, 1, 512, 768, 512, 256, "B")
+        quantize_current(1, 512, 256, "cc3")
+        make_forces(1, 768, 256, range(0, 4), 0)
+        make_current(nc.vector, 1, 768, 1024, 768, 256, "B")
+        quantize_current(1, 768, 256, "cc3")
+        make_y(0, 256, "drive", ())
+        round_y(0, 256, 128)
+        quantize_y(0, 256)
+        make_y(256, 256, "drive", ())
+        round_y(256, 256, 0)
+        quantize_y(256, 256)
+        make_y(512, 256, "reversal", ())
+        round_y(512, 256, 128)
+        quantize_y(512, 256)
+        make_y(768, 256, "drive", ())
+        round_y(768, 256, 128)
+        quantize_y(768, 256)
 
         out_rows = out_2[0].rearrange("(q r) m -> r q m", r=4)
         for r in range(4):

@@ -153,8 +153,8 @@ def tile_list_coupled_ionic_current_kernel(
             rounded = staged("w_rounded", slot, [P, PACK * PASS], BF16)
             rounded_weight[key] = rounded
             shared_copy(
-                rounded[:].rearrange("p (t m i) -> p m i t", t=PACK, i=PACK),
-                raw.rearrange("p i (m t) -> p m i t", t=PACK),
+                rounded[:].rearrange("p (t m u v) -> p m u t v", t=PACK, u=2, v=2),
+                raw.rearrange("p (u v) (m t) -> p m u t v", t=PACK, v=2),
                 scalar_keeps,
             )
 

@@ -1,6 +1,7 @@
 from contextlib import ExitStack
 
 import concourse.mybir as mybir
+from concourse.masks import make_identity
 
 K, K2, T, T2, S, H, N = 1024, 512, 2048, 4096, 1024, 1024, 512
 FLOPS = 2 * (K * H * S + K2 * H * S + H * N * S)
@@ -22,10 +23,11 @@ PASS = P * PACK
 QUADRANT = 32
 SPREAD = 8
 PLANE_SHIFT = 4
-RING_BANKS = 4
 HALF = S // 2
 QUARTER = S // 4
 WALK = 2
+GATE_BUFS = 12
+BANKS = 8
 
 
 def tile_list_coupled_ionic_current_kernel(
@@ -36,7 +38,7 @@ def tile_list_coupled_ionic_current_kernel(
     with ExitStack() as ctx:
         keep = ctx.enter_context(tc.tile_pool(name="keep", bufs=1))
         ring = ctx.enter_context(tc.tile_pool(name="ring", bufs=1))
-        psum = ctx.enter_context(tc.psum_pool(name="psum", bufs=RING_BANKS))
+        psum = ctx.enter_context(tc.psum_pool(name="psum", bufs=1))
 
         def held(name, shape, dtype):
             return keep.tile(shape, dtype, name=name, align_bytes=64)
@@ -44,45 +46,55 @@ def tile_list_coupled_ionic_current_kernel(
         def staged(name, slot, shape, dtype):
             return ring.tile(shape, dtype, name=name, tag=slot, align_bytes=64)
 
-        def float_rows(name, width):
-            return ring.tile([P, PACK, width], F32, name=name, tag="float_rows", align_bytes=64, bufs=4)
+        bank_ring = []
 
-        def bank(bank_ring):
-            return psum.tile([P, HALF], F32, name="bank", tag=bank_ring)
+        def use_banks(banks):
+            bank_ring.clear()
+            bank_ring.extend(banks)
+
+        def bank():
+            taken = bank_ring[0]
+            bank_ring.remove(taken)
+            bank_ring.append(taken)
+            return psum.tile([P, HALF], F32, name="bank", tag="bank%d" % taken)
 
         idx = held("idx", [P, S // 16], U16)
         idx2 = held("idx2", [P, S // 16], U16)
+        identity = held("identity", [P, P], F32)
         v_table = [staged("v_table%d" % a, "table%d" % a, [P, T], I32) for a in range(2)]
         v_table_scales = held("v_table_scales", [P, T], U8)
         v2_table = staged("v2_table", "table2", [P, T2], I32)
         v2_table_scales = held("v2_table_scales", [P, T2], U8)
         w2_raw = held("w2_raw", [P, 2 * H], U8)
         w2_raw_scales = held("w2_raw_scales", [P, H], U8)
-        w2_codes = staged("w2_codes", "w2_codes", [P, 2 * H], U8)
-        e_planes = staged("e_planes", "e_planes", [P, S + H], U8)
+        w2_codes = held("w2_codes", [P, 2 * H], U8)
+        e_planes = held("e_planes", [P, S + H], U8)
         v2_plane, w2_plane = e_planes[:, 0:S], e_planes[:, S : S + H]
         v2_picked_scales = held("v2_picked_scales", [P, S], U8)
         v_picked_scales = held("v_picked_scales", [P, S], U8)
         v_codes = [held("v_codes%d" % a, [P, S], U32) for a in range(2)]
         v_planes = held("v_planes", [P, S], U8)
-        v2_codes = [staged("v2_codes%d" % h, "v2_codes%d" % h, [P, HALF], U32) for h in range(2)]
+        v2_codes = [held("v2_codes%d" % h, [P, HALF], U32) for h in range(2)]
         gain = held("gain", [P, 2, PACK], F32)
         inv_cap = held("inv_cap", [P, PACK], F32)
-        w1_raw = {(a, b): float_rows("w1_raw%d%d" % (a, b), PASS) for b in range(2) for a in range(2)}
-        wc_raw = [held("wc_raw%d" % b, [P, PACK, N], F32) for b in range(2)]
-        w1_codes = {ab: held("w1_codes%d%d" % ab, [P, PASS], U32) for ab in w1_raw}
-        w1_plane = {ab: held("w1_plane%d%d" % ab, [P, PASS], U8) for ab in w1_raw}
-        wc_codes = held("wc_codes", [P, 2, N], U32)
-        wc_plane = held("wc_plane", [P, 2, N], U8)
-        force_rows = held("force0", [P, PACK, S], F32)
-        force = {(0, h): force_rows[:, :, HALF * h : HALF * (h + 1)] for h in range(2)}
-        for h in range(2):
-            force[1, h] = held("force1%d" % h, [P, PACK, HALF], F32)[:]
+        w1_codes = {(a, b): held("w1_codes%d%d" % (a, b), [P, PASS], U32) for a in range(2) for b in range(2)}
+        w1_plane = {ab: held("w1_plane%d%d" % ab, [P, PASS], U8) for ab in w1_codes}
+        wc_codes = [held("wc_codes%d" % b, [P, N], U32) for b in range(2)]
+        wc_plane = [held("wc_plane%d" % b, [P, N], U8) for b in range(2)]
         cur_plane = [held("cur_plane%d" % b, [P, S], U8) for b in range(2)]
         y_plane = held("y_plane", [P, S], U8)
+        raw = {}
+        voltage = {}
+        force = {}
+        gate = {}
         conductance = {}
+        gained = {}
+        turned_gate = {}
         cur_codes = {}
         cur_rounded = {}
+        rounded_weight = {}
+        y_rows = {}
+        y_rounded = {}
 
         def half(h):
             return slice(HALF * h, HALF * (h + 1))
@@ -104,21 +116,26 @@ def tile_list_coupled_ionic_current_kernel(
                 for shift in shifts:
                     move_bytes(tile[shift + r : P : QUADRANT, :], tile[shift + SPREAD * r : P : QUADRANT, :])
 
-        def load_w1(a, b):
+        def load_w1(a, b, slot):
+            raw["w1", a, b] = staged("w1_raw", slot, [P, PACK, PASS], F32)
             block = w1[PASS * a : PASS * (a + 1), PASS * b : PASS * (b + 1)]
-            nc.sync.dma_start(out=w1_raw[a, b][:], in_=dealt_rows(block))
+            nc.sync.dma_start(out=raw["w1", a, b][:], in_=dealt_rows(block))
 
-        def load_wc(b):
-            nc.sync.dma_start(out=wc_raw[b][:], in_=dealt_rows(wc[PASS * b : PASS * (b + 1), :]))
+        def load_wc(b, slot):
+            raw["wc", b] = staged("wc_raw", slot, [P, PACK, N], F32)
+            nc.sync.dma_start(out=raw["wc", b][:], in_=dealt_rows(wc[PASS * b : PASS * (b + 1), :]))
 
-        def force_at(b, rows, j0, j1):
-            if j1 - j0 == S:
-                return force_rows[:, rows, :]
-            return force[b, j0 // HALF][:, rows, j0 % HALF : j0 % HALF + j1 - j0]
+        def load_vm_rows(b, rows, slot):
+            if (b, 0) not in voltage:
+                whole = staged("voltage", slot, [P, PACK, S], F32)
+                for h in range(2):
+                    voltage[b, h] = whole[:, :, half(h)]
+                voltage[b] = whole
+            nc.sync.dma_start(out=voltage[b][:, rows, :], in_=dealt_rows(vm[PASS * b : PASS * (b + 1), :])[:, rows, :])
 
-        def load_vm(b, rows, cols):
-            source = dealt_rows(vm[PASS * b : PASS * (b + 1), :])[:, rows, cols]
-            nc.sync.dma_start(out=force_at(b, rows, cols.start, cols.stop), in_=source)
+        def load_vm_half(b, h, slot):
+            voltage[b, h] = staged("voltage", slot, [P, PACK, HALF], F32)[:]
+            nc.sync.dma_start(out=voltage[b, h], in_=dealt_rows(vm[PASS * b : PASS * (b + 1), half(h)]))
 
         def gather(dst, table, offsets):
             nc.vector.tensor_copy(out=dst, in_=table.indirect(offsets))
@@ -135,11 +152,13 @@ def tile_list_coupled_ionic_current_kernel(
                 in_=src.rearrange("p (b m t) -> p b m t", b=2, t=PACK),
             )
 
-        def shared_copy(dst, src, cut):
-            if cut > 0:
-                nc.scalar.copy(out=dst[:, 0:cut], in_=src[:, 0:cut])
-            if cut < dst.shape[1]:
-                nc.vector.tensor_copy(out=dst[:, cut:], in_=src[:, cut:])
+        def copy_on(engine, dst, src):
+            if engine == "scalar":
+                nc.scalar.copy(out=dst, in_=src)
+            elif engine == "vector":
+                nc.vector.tensor_copy(out=dst, in_=src)
+            else:
+                nc.gpsimd.tensor_scalar(out=dst, in0=src, scalar1=1.0, scalar2=0.0, op0=ALU.mult, op1=ALU.add)
 
         def word_walk(side_by_side, by_rows):
             return (
@@ -147,118 +166,162 @@ def tile_list_coupled_ionic_current_kernel(
                 [rows.rearrange("p t (x i) -> p x t i", i=WALK) for rows in by_rows],
             )
 
-        rounded_weight = {}
-
-        def round_weight(key, raw, slot, scalar_keeps):
+        def round_weight(key, slot, shares):
             rounded = staged("w_rounded", slot, [P, PACK * PASS], BF16)
             rounded_weight[key] = rounded
-            shared_copy(
-                rounded[:].rearrange("p (t m u v) -> p m u t v", t=PACK, u=2, v=2),
-                raw.rearrange("p (u v) (m t) -> p m u t v", t=PACK, v=2),
-                scalar_keeps,
-            )
-
-        def round_w1(a, b, scalar_keeps):
-            round_weight(("w1", a, b), w1_raw[a, b][:], "w1_pass%d" % a, scalar_keeps)
+            for engine, m0, m1 in shares:
+                if engine == "gpsimd":
+                    dst = rounded[:].rearrange("p (t m u) -> p m t u", t=PACK, u=PACK)
+                    src = raw[key][:].rearrange("p u (m t) -> p m t u", t=PACK)
+                else:
+                    dst = rounded[:].rearrange("p (t m u v) -> p m u t v", t=PACK, u=2, v=2)
+                    src = raw[key][:].rearrange("p (u v) (m t) -> p m u t v", t=PACK, v=2)
+                copy_on(engine, dst[:, m0:m1], src[:, m0:m1])
 
         def quantize_w1(a, b):
             nc.vector.quantize_mx(
                 out=w1_codes[a, b][:].bitcast(E4M3), scales=w1_plane[a, b][:], in_=rounded_weight["w1", a, b][:]
             )
 
-        def round_wc(b, scalar_keeps):
-            round_weight(("wc", b), wc_raw[b][:], "wc%d" % b, scalar_keeps)
-
         def quantize_wc(b):
             nc.vector.quantize_mx(
-                out=wc_codes[:, b, :].bitcast(E4M3), scales=wc_plane[:, b, :], in_=rounded_weight["wc", b][:]
+                out=wc_codes[b][:].bitcast(E4M3), scales=wc_plane[b][:], in_=rounded_weight["wc", b][:]
             )
 
-        def make_sigmoids(b, h):
-            tile = staged("conductance", ("conductance%d", "table%d")[b] % h, [P, PACK, HALF], F32)
-            conductance[b, h] = tile
-            for t in range(PACK):
-                sums = bank("drive")
-                places = slice(P * t, P * (t + 1))
-                for a in range(2):
-                    nc.tensor.matmul_mx(
-                        out=sums[:],
-                        lhsT=w1_codes[a, b][:, places].bitcast(E4M3),
-                        lhsT_scale=w1_plane[a, b][:, places],
-                        rhs=v_codes[a][:, half(h)].bitcast(E4M3),
-                        rhs_scale=v_planes[PLANE_SHIFT * a : P, half(h)],
-                        start=(a == 0),
-                        stop=(a == 1),
-                    )
-                nc.scalar.activation(out=tile[:, t, :], in_=sums[:], func=ACT.Sigmoid)
+        def make_gate(b, jb):
+            entries_here = slice(P * jb, P * (jb + 1))
+            sums = bank()
+            for a in range(2):
+                nc.tensor.matmul_mx(
+                    out=sums[:],
+                    lhsT=v_codes[a][:, entries_here].bitcast(E4M3),
+                    lhsT_scale=v_planes[PLANE_SHIFT * a : P, entries_here],
+                    rhs=w1_codes[a, b][:].bitcast(E4M3),
+                    rhs_scale=w1_plane[a, b][:],
+                    start=(a == 0),
+                    stop=(a == 1),
+                )
+            gate[b, jb] = ring.tile([P, PASS], F32, name="gate", tag="gate", align_bytes=64, bufs=GATE_BUFS)
+            nc.scalar.activation(out=gate[b, jb][:], in_=sums[:], func=ACT.Sigmoid)
 
-        def gain_on_sigmoid(b, h, rows):
-            for t in rows:
-                g = conductance[b, h][:, t, :]
-                nc.scalar.activation(out=g, in_=g, func=ACT.Copy, scale=gain[:, b, t : t + 1])
+        def make_conductance(b, h, t, slot, gain_engine):
+            if (b, h) not in conductance:
+                conductance[b, h] = staged("conductance", slot, [P, PACK, HALF], F32)
+            sums = bank()
+            places = slice(P * t, P * (t + 1))
+            for a in range(2):
+                nc.tensor.matmul_mx(
+                    out=sums[:],
+                    lhsT=w1_codes[a, b][:, places].bitcast(E4M3),
+                    lhsT_scale=w1_plane[a, b][:, places],
+                    rhs=v_codes[a][:, half(h)].bitcast(E4M3),
+                    rhs_scale=v_planes[PLANE_SHIFT * a : P, half(h)],
+                    start=(a == 0),
+                    stop=(a == 1),
+                )
+            nc.scalar.activation(out=conductance[b, h][:, t, :], in_=sums[:], func=ACT.Sigmoid)
+            apply_gain(conductance[b, h][:, t, :], b, t, gain_engine)
 
-        def gain_on_force(b, t, j0, w):
-            d = force_at(b, t, j0, j0 + w)
-            nc.gpsimd.tensor_scalar(out=d, in0=d, scalar1=gain[:, b, t : t + 1], scalar2=0.0, op0=ALU.mult, op1=ALU.add)
+        def apply_gain(rows, b, t, gain_engine):
+            g = gain[:, b, t : t + 1]
+            if gain_engine == "gpsimd":
+                nc.gpsimd.tensor_scalar(out=rows, in0=rows, scalar1=g, scalar2=0.0, op0=ALU.mult, op1=ALU.add)
+            elif gain_engine == "scalar":
+                nc.scalar.activation(out=rows, in_=rows, func=ACT.Copy, scale=g)
 
-        def make_force(b, t, j0, w):
-            h, x0 = divmod(j0, HALF)
-            sums = bank("reversal")
+        def make_current_rows(b, base, blocks, slot):
+            cur_rounded[b, base] = staged("cur_rounded", slot, [P, PASS * blocks], BF16)
+            h, x = divmod(base, PACK)
+            cols = slice(P * x, P * (x + blocks))
+            dst, (g, d) = word_walk(cur_rounded[b, base][:], [conductance[b, h][:, :, cols], force[b, h][:, :, cols]])
+            nc.vector.tensor_tensor(out=dst, in0=d, in1=g, op=ALU.mult)
+
+        def reversal(b, h, t):
+            sums = bank()
             place = PASS * b + P * t
             nc.tensor.matmul_mx(
-                out=sums[:, 0:w],
+                out=sums[:],
                 lhsT=w2_codes[:, 2 * place : 2 * (place + P)].bitcast(E2M1),
                 lhsT_scale=w2_plane[:, place : place + P],
-                rhs=v2_codes[h][:, x0 : x0 + w].bitcast(E4M3),
-                rhs_scale=v2_plane[:, j0 : j0 + w],
+                rhs=v2_codes[h][:].bitcast(E4M3),
+                rhs_scale=v2_plane[:, half(h)],
                 start=True,
                 stop=True,
             )
-            d = force_at(b, t, j0, j0 + w)
-            nc.vector.tensor_tensor(out=d, in0=d, in1=sums[:, 0:w], op=ALU.subtract)
+            return sums
 
-        def make_forces(b, j0, w, rows, gpsimd_rows):
-            for t in rows:
-                make_force(b, t, j0, w)
-                if t < gpsimd_rows:
-                    gain_on_force(b, t, j0, w)
+        def force_tile(b, h, slot):
+            if (b, h) not in force:
+                force[b, h] = staged("force", slot, [P, PACK, HALF], F32)
+            return force[b, h]
 
-        def make_current(engine, b, j0, j1, base, width, slot):
-            if (b, base) not in cur_rounded:
-                cur_rounded[b, base] = staged("cur_rounded", slot, [P, PACK * width], BF16)
-            dst, (g, d) = word_walk(
-                cur_rounded[b, base][:, PACK * (j0 - base) : PACK * (j1 - base)],
-                [conductance[b, j0 // HALF][:, :, j0 % HALF : j0 % HALF + j1 - j0], force_at(b, slice(None), j0, j1)],
+        def make_force(b, h, t, slot, gain_engine):
+            d = force_tile(b, h, slot)[:, t, :]
+            nc.vector.tensor_tensor(out=d, in0=voltage[b, h][:, t, :], in1=reversal(b, h, t)[:], op=ALU.subtract)
+            apply_gain(d, b, t, gain_engine)
+
+        def gained_reversal(b, h, t, slot):
+            if (b, h, t // 2) not in gained:
+                gained[b, h, t // 2] = staged("gained", slot, [P, 2, HALF], F32)
+            ge = gained[b, h, t // 2][:, t % 2, :]
+            nc.scalar.activation(out=ge, in_=reversal(b, h, t)[:], func=ACT.Copy, scale=gain[:, b, t : t + 1])
+
+        def gained_force(b, h, t, cols, slot):
+            nc.vector.scalar_tensor_tensor(
+                out=force_tile(b, h, slot)[:, t, cols],
+                in0=voltage[b, h][:, t, cols],
+                scalar=gain[:, b, t : t + 1],
+                in1=gained[b, h, t // 2][:, t % 2, cols],
+                op0=ALU.mult,
+                op1=ALU.subtract,
             )
-            engine.tensor_tensor(out=dst, in0=g, in1=d, op=ALU.mult)
 
-        def quantize_current(b, j0, w, slot):
-            h, x0 = divmod(j0, HALF)
+        def turn_gate(b, jb):
+            turned = bank()
+            turned_gate[b, jb] = turned
+            for t in range(PACK):
+                nc.tensor.transpose(turned[:, P * t : P * (t + 1)], gate[b, jb][:, P * t : P * (t + 1)], identity[:])
+
+        def make_current(b, jb, base, blocks, slot):
+            if (b, base) not in cur_rounded:
+                cur_rounded[b, base] = staged("cur_rounded", slot, [P, PASS * blocks], BF16)
+            if (b, jb) not in turned_gate:
+                turn_gate(b, jb)
+            turned = turned_gate[b, jb]
+            h, x = divmod(jb, PACK)
+            dst, (g, d) = word_walk(
+                cur_rounded[b, base][:, PASS * (jb - base) : PASS * (jb - base + 1)],
+                [turned[:].rearrange("p (t j) -> p t j", t=PACK), force[b, h][:, :, P * x : P * (x + 1)]],
+            )
+            nc.vector.tensor_tensor(out=dst, in0=d, in1=g, op=ALU.mult)
+
+        def quantize_current(b, base, blocks, slot):
+            h, x = divmod(base, PACK)
             if (b, h) not in cur_codes:
                 cur_codes[b, h] = staged("cur_codes", slot, [P, HALF], U32)
             nc.vector.quantize_mx(
-                out=cur_codes[b, h][:, x0 : x0 + w].bitcast(E4M3),
-                scales=cur_plane[b][:, j0 : j0 + w],
-                in_=cur_rounded[b, j0][:],
+                out=cur_codes[b, h][:, P * x : P * (x + blocks)].bitcast(E4M3),
+                scales=cur_plane[b][:, P * base : P * (base + blocks)],
+                in_=cur_rounded[b, base][:],
             )
 
-        y_rows = {}
-        y_rounded = {}
-
-        def make_y(j0, w, bank_ring, vector_rows=()):
-            cols = slice(j0, j0 + w)
+        def codes_at(b, j0, w):
             h, x0 = divmod(j0, HALF)
-            y = float_rows("y", w)
+            return cur_codes[b, h][:, x0 : x0 + w]
+
+        def make_y(j0, w, slot, vector_rows=()):
+            cols = slice(j0, j0 + w)
+            y = staged("y", slot, [P, PACK, w], F32)
             y_rows[j0] = y
             for t in range(PACK):
-                sums = bank(bank_ring)[:, 0:w]
+                sums = bank()[:, 0:w]
                 places = slice(P * t, P * (t + 1))
                 for b in range(2):
                     nc.tensor.matmul_mx(
                         out=sums,
-                        lhsT=wc_codes[:, b, places].bitcast(E4M3),
-                        lhsT_scale=wc_plane[:, b, places],
-                        rhs=cur_codes[b, h][:, x0 : x0 + w].bitcast(E4M3),
+                        lhsT=wc_codes[b][:, places].bitcast(E4M3),
+                        lhsT_scale=wc_plane[b][:, places],
+                        rhs=codes_at(b, j0, w).bitcast(E4M3),
                         rhs_scale=cur_plane[b][:, cols],
                         start=(b == 0),
                         stop=(b == 1),
@@ -271,108 +334,135 @@ def tile_list_coupled_ionic_current_kernel(
                     nc.scalar.activation(out=y[:, t, :], in_=sums, func=ACT.Copy, scale=inv_cap[:, t : t + 1])
             nc.sync.dma_start(out=dealt_rows(out_0[:, cols]), in_=y[:])
 
-        def round_y(j0, w, scalar_rounds):
-            rounded = staged("y_rounded", "y%d" % j0, [P, PACK * w], BF16)
+        def round_y(j0, w, slot, shares):
+            rounded = staged("y_rounded", slot, [P, PACK * w], BF16)
             y_rounded[j0] = rounded
             dst, (src,) = word_walk(rounded[:], [y_rows[j0][:]])
-            shared_copy(dst, src, scalar_rounds // WALK)
+            for engine, c0, c1 in shares:
+                if engine == "gpsimd":
+                    side_by_side = rounded[:].rearrange("p (x t) -> p x t", t=PACK)
+                    copy_on(engine, side_by_side[:, c0:c1], y_rows[j0][:].rearrange("p t x -> p x t")[:, c0:c1])
+                else:
+                    copy_on(engine, dst[:, c0 // WALK : c1 // WALK], src[:, c0 // WALK : c1 // WALK])
 
-        def quantize_y(j0, w):
+        def quantize_y(j0, w, slot):
             cols = slice(j0, j0 + w)
-            nc.vector.quantize_mx(out=y_codes[:, cols].bitcast(E4M3), scales=y_plane[:, cols], in_=y_rounded[j0][:])
+            y_codes = staged("y_codes", slot, [P, w], U32)
+            nc.vector.quantize_mx(out=y_codes[:].bitcast(E4M3), scales=y_plane[:, cols], in_=y_rounded[j0][:])
             words = out_1[0].rearrange("p m t -> p (m t)")
-            move_bytes(words[:, PACK * j0 : PACK * (j0 + w)], y_codes[:, cols])
+            move_bytes(words[:, PACK * j0 : PACK * (j0 + w)], y_codes[:])
+
 
         for tile in (v_table_scales, v2_table_scales, w2_raw_scales):
             nc.vector.memset(tile[:].bitcast(I32), 0)
-        everything = slice(None)
-        y_codes = staged("y_codes", "y_codes", [P, S], U32)
+        make_identity(nc, identity[:])
         move_bytes(w2_raw[:], w2_words[0])
         nc.sync.dma_start(idx[:], offs)
         load_spread(v_table_scales, tab_scales[0], 0)
         load_spread(v_table_scales, tab_scales[1], PLANE_SHIFT)
-        load_w1(0, 0)
+        load_w1(0, 0, "raw0")
         nc.sync.dma_start(idx2[:], offs2)
         load_spread(v2_table_scales, tab2_scales[0], 0)
         load_words(v_table[0], tab_words[0])
-        gather(v_picked_scales[:], v_table_scales[:], idx[:]); copy_bytes(v_planes[:], v_picked_scales[:])
+        gather(v_picked_scales[:], v_table_scales[:], idx[:])
+        copy_bytes(v_planes[:], v_picked_scales[:])
         load_spread(w2_raw_scales, w2_scales[0], 0)
-        gather(v2_picked_scales[:], v2_table_scales[:], idx2[:]); copy_bytes(v2_plane, v2_picked_scales[:])
+        gather(v2_picked_scales[:], v2_table_scales[:], idx2[:])
+        copy_bytes(v2_plane, v2_picked_scales[:])
         deal(w2_plane, w2_raw_scales[:])
-        load_w1(1, 0)
+        load_w1(1, 0, "raw1")
         close_up(v_planes, (0, PLANE_SHIFT))
         load_words(v_table[1], tab_words[1])
         nc.sync.dma_start(out=gain[:], in_=gmax.rearrange("(b p t) -> p b t", b=2, t=PACK))
         load_words(v2_table, tab2_words[0])
         close_up(e_planes, (0,))
-        load_vm(0, slice(0, 2), slice(0, 1024))
-        load_vm(0, slice(2, 4), slice(0, 1024))
-        load_w1(0, 1)
-        load_w1(1, 1)
-        load_wc(0)
-        load_vm(1, slice(0, 4), slice(0, 512))
-        load_wc(1)
-        load_vm(1, slice(0, 4), slice(512, 1024))
+
+        load_vm_rows(0, slice(0, 2), "voltage0")
+        load_vm_rows(0, slice(2, 4), "voltage0")
+        load_w1(0, 1, "raw2")
+        load_w1(1, 1, "raw0")
+        load_vm_half(1, 0, "table0")
+        load_wc(0, "raw3")
+        load_wc(1, "raw1")
+        load_vm_half(1, 1, "table1")
         nc.sync.dma_start(out=inv_cap[:], in_=cinv.rearrange("(p t) -> p t", t=PACK))
+
         gather(v_codes[0][:], v_table[0][:].bitcast(U32), idx[:])
         deal(w2_codes[:].bitcast(U16), w2_raw[:].bitcast(U16))
-        round_w1(0, 0, 128)
+        round_weight(("w1", 0, 0), "wr0", [("scalar", 0, P)])
         quantize_w1(0, 0)
-        round_w1(1, 0, 128)
+        round_weight(("w1", 1, 0), "wr1", [("scalar", 0, P)])
         quantize_w1(1, 0)
-        gather(v_codes[1][:, half(0)], v_table[1][:].bitcast(U32), entries(idx, 0))
-        gather(v_codes[1][:, half(1)], v_table[1][:].bitcast(U32), entries(idx, 1))
-        gather(v2_codes[0][:], v2_table[:].bitcast(U32), entries(idx2, 0))
-        gather(v2_codes[1][:], v2_table[:].bitcast(U32), entries(idx2, 1))
-        make_sigmoids(0, 0)
-        gain_on_sigmoid(0, 0, range(2, 4))
-        make_sigmoids(0, 1)
-        gain_on_sigmoid(0, 1, range(2, 4))
-        round_w1(0, 1, 128)
+        for h in range(2):
+            gather(v_codes[1][:, half(h)], v_table[1][:].bitcast(U32), entries(idx, h))
+        for h in range(2):
+            gather(v2_codes[h][:], v2_table[:].bitcast(U32), entries(idx2, h))
+
+        use_banks(range(BANKS))
+        for jb in range(8):
+            make_gate(0, jb)
+        for rows, gain_engine in ((range(0, 2), "gpsimd"), (range(2, 4), "scalar")):
+            for h in range(2):
+                for t in rows:
+                    make_force(0, h, t, "force0%d" % h, gain_engine)
+        for jb in range(4):
+            turn_gate(0, jb)
+        round_weight(("w1", 0, 1), "wr0", [("gpsimd", 0, P)])
+        round_weight(("w1", 1, 1), "wr1", [("scalar", 0, P)])
+        for jb in range(4):
+            make_current(0, jb, 0, 4, "cur00")
         quantize_w1(0, 1)
-        round_w1(1, 1, 96)
         quantize_w1(1, 1)
-        make_forces(0, 0, 512, range(0, 2), 2)
-        make_forces(0, 512, 512, range(0, 2), 2)
-        make_forces(0, 0, 512, range(2, 4), 2)
-        make_forces(0, 512, 512, range(2, 4), 2)
-        make_sigmoids(1, 0)
-        gain_on_sigmoid(1, 0, range(2, 4))
-        make_current(nc.vector, 0, 0, 512, 0, 512, "A")
-        make_current(nc.vector, 0, 512, 768, 512, 256, "u01")
-        make_current(nc.vector, 0, 768, 1024, 768, 256, "w1_pass1")
-        quantize_current(0, 0, 512, "cc0")
-        quantize_current(0, 512, 256, "cc1")
-        quantize_current(0, 768, 256, "cc1")
-        make_sigmoids(1, 1)
-        gain_on_sigmoid(1, 1, range(0, 4))
-        round_wc(0, 128)
-        quantize_wc(0)
-        round_wc(1, 0)
+        quantize_current(0, 0, 4, "wr0")
+        use_banks(range(BANKS))
+        for t in range(PACK):
+            make_force(1, 0, t, "table2", None)
+        for jb in range(4):
+            make_gate(1, jb)
+        for t in range(PACK):
+            apply_gain(force[1, 0][:, t, :], 1, t, "gpsimd" if t < 3 else "scalar")
+        for jb in range(4, 6):
+            make_current(0, jb, 4, 2, "table0")
+        round_weight(("wc", 0), "wr2", [("scalar", 0, P)])
+        round_weight(("wc", 1), "force00", [("gpsimd", 0, P)])
+        use_banks([2, 3, 4, 5])
+        for jb in range(4):
+            make_current(1, jb, 0, 4, "cur00")
+        use_banks([6, 7, 2, 3])
+        for t in range(PACK):
+            make_conductance(1, 1, t, "raw3", None)
+        quantize_current(1, 0, 4, "cc10")
         quantize_wc(1)
-        make_forces(1, 0, 512, range(0, 4), 2)
-        make_current(nc.vector, 1, 0, 256, 0, 256, "A")
-        quantize_current(1, 0, 256, "cc2")
-        make_current(nc.vector, 1, 256, 512, 256, 256, "A")
-        quantize_current(1, 256, 256, "cc2")
-        make_forces(1, 512, 256, range(0, 4), 0)
-        make_current(nc.vector, 1, 512, 768, 512, 256, "B")
-        quantize_current(1, 512, 256, "cc3")
-        make_forces(1, 768, 256, range(0, 4), 0)
-        make_current(nc.vector, 1, 768, 1024, 768, 256, "B")
-        quantize_current(1, 768, 256, "cc3")
-        make_y(0, 256, "drive", ())
-        round_y(0, 256, 128)
-        quantize_y(0, 256)
-        make_y(256, 256, "drive", ())
-        round_y(256, 256, 0)
-        quantize_y(256, 256)
-        make_y(512, 256, "reversal", ())
-        round_y(512, 256, 128)
-        quantize_y(512, 256)
-        make_y(768, 256, "drive", ())
-        round_y(768, 256, 128)
-        quantize_y(768, 256)
+        quantize_wc(0)
+        quantize_current(0, 4, 2, "raw1")
+        use_banks([0, 1, 4, 5])
+        for t in range(PACK):
+            make_force(1, 1, t, "force00", None)
+        use_banks([6, 7, 2, 3])
+        make_y(0, QUARTER, "raw2")
+        for t in range(PACK):
+            apply_gain(force[1, 1][:, t, :], 1, t, "gpsimd" if t < 3 else "scalar")
+        use_banks([0, 1])
+        for jb in range(6, 8):
+            make_current(0, jb, 6, 2, "table1")
+        use_banks([4, 5, 6, 7])
+        make_y(QUARTER, QUARTER, "raw0")
+        round_y(0, QUARTER, "yr0", [("scalar", 0, QUARTER)])
+        round_y(QUARTER, QUARTER, "yr1", [("scalar", 0, QUARTER)])
+        quantize_current(0, 6, 2, "raw1")
+        for c in range(2):
+            make_current_rows(1, 4 + 2 * c, 2, "cur11%d" % c)
+            quantize_current(1, 4 + 2 * c, 2, "cc11")
+        use_banks([2, 3, 0, 1])
+        make_y(2 * QUARTER, QUARTER, "y2")
+        use_banks([4, 5, 6, 7])
+        make_y(3 * QUARTER, QUARTER, "force01")
+        quantize_y(0, QUARTER, "cur110")
+        quantize_y(QUARTER, QUARTER, "cur111")
+        round_y(2 * QUARTER, QUARTER, "yr2", [("vector", 0, QUARTER)])
+        quantize_y(2 * QUARTER, QUARTER, "yc2")
+        round_y(3 * QUARTER, QUARTER, "yr3", [("scalar", 0, 96), ("vector", 96, QUARTER)])
+        quantize_y(3 * QUARTER, QUARTER, "yc3")
 
         out_rows = out_2[0].rearrange("(q r) m -> r q m", r=4)
         for r in range(4):

@@ -309,10 +309,11 @@ def tile_list_coupled_ionic_current_kernel(
             h, x0 = divmod(j0, HALF)
             return cur_codes[b, h][:, x0 : x0 + w]
 
-        def make_y(j0, w, slot, vector_rows=()):
+        def make_y(j0, w, slot, rows_a_store=PACK, vector_rows=()):
             cols = slice(j0, j0 + w)
             y = staged("y", slot, [P, PACK, w], F32)
-            y_rows[j0] = y
+            for x in range(0, w, QUARTER):
+                y_rows[j0 + x] = y[:, :, x : x + QUARTER]
             for t in range(PACK):
                 sums = bank()[:, 0:w]
                 places = slice(P * t, P * (t + 1))
@@ -332,16 +333,18 @@ def tile_list_coupled_ionic_current_kernel(
                     )
                 else:
                     nc.scalar.activation(out=y[:, t, :], in_=sums, func=ACT.Copy, scale=inv_cap[:, t : t + 1])
-            nc.sync.dma_start(out=dealt_rows(out_0[:, cols]), in_=y[:])
+                if (t + 1) % rows_a_store == 0:
+                    rows = slice(t + 1 - rows_a_store, t + 1)
+                    nc.sync.dma_start(out=dealt_rows(out_0[:, cols])[:, rows, :], in_=y[:, rows, :])
 
         def round_y(j0, w, slot, shares):
             rounded = staged("y_rounded", slot, [P, PACK * w], BF16)
             y_rounded[j0] = rounded
-            dst, (src,) = word_walk(rounded[:], [y_rows[j0][:]])
+            dst, (src,) = word_walk(rounded[:], [y_rows[j0]])
             for engine, c0, c1 in shares:
                 if engine == "gpsimd":
                     side_by_side = rounded[:].rearrange("p (x t) -> p x t", t=PACK)
-                    copy_on(engine, side_by_side[:, c0:c1], y_rows[j0][:].rearrange("p t x -> p x t")[:, c0:c1])
+                    copy_on(engine, side_by_side[:, c0:c1], y_rows[j0].rearrange("p t x -> p x t")[:, c0:c1])
                 else:
                     copy_on(engine, dst[:, c0 // WALK : c1 // WALK], src[:, c0 // WALK : c1 // WALK])
 
@@ -405,60 +408,55 @@ def tile_list_coupled_ionic_current_kernel(
             for h in range(2):
                 for t in rows:
                     make_force(0, h, t, "force0%d" % h, gain_engine)
-        for jb in range(4):
+        for jb in range(6):
             turn_gate(0, jb)
         round_weight(("w1", 0, 1), "wr0", [("gpsimd", 0, P)])
         round_weight(("w1", 1, 1), "wr1", [("scalar", 0, P)])
         for jb in range(4):
             make_current(0, jb, 0, 4, "cur00")
+        for jb in range(4, 6):
+            make_current(0, jb, 4, 2, "cur04")
         quantize_w1(0, 1)
         quantize_w1(1, 1)
         quantize_current(0, 0, 4, "wr0")
-        use_banks(range(BANKS))
+        quantize_current(0, 4, 2, "cc01")
+        use_banks([0, 1, 2, 3, 6, 7, 4, 5])
         for t in range(PACK):
             make_force(1, 0, t, "table2", None)
         for jb in range(4):
             make_gate(1, jb)
         for t in range(PACK):
             apply_gain(force[1, 0][:, t, :], 1, t, "gpsimd" if t < 3 else "scalar")
-        for jb in range(4, 6):
-            make_current(0, jb, 4, 2, "table0")
-        round_weight(("wc", 0), "wr2", [("scalar", 0, P)])
-        round_weight(("wc", 1), "force00", [("gpsimd", 0, P)])
-        use_banks([2, 3, 4, 5])
+        for jb in range(6, 8):
+            make_current(0, jb, 6, 2, "table0")
+        round_weight(("wc", 0), "wr2", [("gpsimd", 0, P)])
+        round_weight(("wc", 1), "force00", [("scalar", 0, P)])
+        use_banks([2, 3, 6, 7])
         for jb in range(4):
             make_current(1, jb, 0, 4, "cur00")
-        use_banks([6, 7, 2, 3])
+        use_banks([4, 5, 0, 1])
         for t in range(PACK):
-            make_conductance(1, 1, t, "raw3", None)
+            make_conductance(1, 1, t, "raw1", None if t < 2 else "scalar")
         quantize_current(1, 0, 4, "cc10")
-        quantize_wc(1)
+        quantize_current(0, 6, 2, "cc01")
         quantize_wc(0)
-        quantize_current(0, 4, 2, "raw1")
-        use_banks([0, 1, 4, 5])
+        quantize_wc(1)
+        use_banks([2, 3, 6, 7])
         for t in range(PACK):
-            make_force(1, 1, t, "force00", None)
-        use_banks([6, 7, 2, 3])
-        make_y(0, QUARTER, "raw2")
-        for t in range(PACK):
-            apply_gain(force[1, 1][:, t, :], 1, t, "gpsimd" if t < 3 else "scalar")
-        use_banks([0, 1])
-        for jb in range(6, 8):
-            make_current(0, jb, 6, 2, "table1")
-        use_banks([4, 5, 6, 7])
-        make_y(QUARTER, QUARTER, "raw0")
-        round_y(0, QUARTER, "yr0", [("scalar", 0, QUARTER)])
-        round_y(QUARTER, QUARTER, "yr1", [("scalar", 0, QUARTER)])
-        quantize_current(0, 6, 2, "raw1")
+            make_force(1, 1, t, "force00", "gpsimd" if t < 2 else None)
+        use_banks([4, 5, 0, 1])
+        make_y(0, HALF, "raw2", 2)
         for c in range(2):
             make_current_rows(1, 4 + 2 * c, 2, "cur11%d" % c)
             quantize_current(1, 4 + 2 * c, 2, "cc11")
-        use_banks([2, 3, 0, 1])
-        make_y(2 * QUARTER, QUARTER, "y2")
-        use_banks([4, 5, 6, 7])
+        round_y(0, QUARTER, "yr0", [("scalar", 0, QUARTER)])
+        use_banks([2, 3, 6, 7])
+        make_y(2 * QUARTER, QUARTER, "raw3")
+        use_banks([4, 5, 0, 1])
         make_y(3 * QUARTER, QUARTER, "force01")
+        round_y(QUARTER, QUARTER, "cur111", [("vector", 0, QUARTER)])
         quantize_y(0, QUARTER, "cur110")
-        quantize_y(QUARTER, QUARTER, "cur111")
+        quantize_y(QUARTER, QUARTER, "yc1")
         round_y(2 * QUARTER, QUARTER, "yr2", [("vector", 0, QUARTER)])
         quantize_y(2 * QUARTER, QUARTER, "yc2")
         round_y(3 * QUARTER, QUARTER, "yr3", [("scalar", 0, 96), ("vector", 96, QUARTER)])

@@ -137,6 +137,24 @@ def tile_list_coupled_ionic_current_kernel(
             voltage[b, h] = staged("voltage", slot, [P, PACK, HALF], F32)[:]
             nc.sync.dma_start(out=voltage[b, h], in_=dealt_rows(vm[PASS * b : PASS * (b + 1), half(h)]))
 
+        def load_vm_quarter(b, c, slot):
+            voltage[b, "q", c] = staged("voltage", slot, [P, PACK, QUARTER], F32)
+            cols = slice(QUARTER * c, QUARTER * (c + 1))
+            nc.sync.dma_start(out=voltage[b, "q", c][:], in_=dealt_rows(vm[PASS * b : PASS * (b + 1), cols]))
+
+        def gained_force_quarter(b, c, slot):
+            h, x = divmod(c, 2)
+            force[b, "q", c] = staged("force", slot, [P, PACK, QUARTER], F32)
+            for t in range(PACK):
+                nc.vector.scalar_tensor_tensor(
+                    out=force[b, "q", c][:, t, :],
+                    in0=voltage[b, "q", c][:, t, :],
+                    scalar=gain[:, b, t : t + 1],
+                    in1=gained[b, h, t // 2][:, t % 2, QUARTER * x : QUARTER * (x + 1)],
+                    op0=ALU.mult,
+                    op1=ALU.subtract,
+                )
+
         def gather(dst, table, offsets):
             nc.vector.tensor_copy(out=dst, in_=table.indirect(offsets))
 
@@ -233,7 +251,7 @@ def tile_list_coupled_ionic_current_kernel(
             cur_rounded[b, base] = staged("cur_rounded", slot, [P, PASS * blocks], BF16)
             h, x = divmod(base, PACK)
             cols = slice(P * x, P * (x + blocks))
-            dst, (g, d) = word_walk(cur_rounded[b, base][:], [conductance[b, h][:, :, cols], force[b, h][:, :, cols]])
+            dst, (g, d) = word_walk(cur_rounded[b, base][:], [conductance[b, h][:, :, cols], force[b, "q", base // 2][:] if (b, "q", base // 2) in force else force[b, h][:, :, cols]])
             nc.vector.tensor_tensor(out=dst, in0=d, in1=g, op=ALU.mult)
 
         def reversal(b, h, t):
@@ -296,18 +314,16 @@ def tile_list_coupled_ionic_current_kernel(
             nc.vector.tensor_tensor(out=dst, in0=d, in1=g, op=ALU.mult)
 
         def quantize_current(b, base, blocks, slot):
-            h, x = divmod(base, PACK)
-            if (b, h) not in cur_codes:
-                cur_codes[b, h] = staged("cur_codes", slot, [P, HALF], U32)
+            cur_codes[b, base] = staged("cur_codes", slot, [P, P * blocks], U32)
             nc.vector.quantize_mx(
-                out=cur_codes[b, h][:, P * x : P * (x + blocks)].bitcast(E4M3),
+                out=cur_codes[b, base][:].bitcast(E4M3),
                 scales=cur_plane[b][:, P * base : P * (base + blocks)],
                 in_=cur_rounded[b, base][:],
             )
 
         def codes_at(b, j0, w):
-            h, x0 = divmod(j0, HALF)
-            return cur_codes[b, h][:, x0 : x0 + w]
+            base = max(key[1] for key in cur_codes if key[0] == b and P * key[1] <= j0)
+            return cur_codes[b, base][:, j0 - P * base : j0 - P * base + w]
 
         def make_y(j0, w, slot, rows_a_store=PACK, vector_rows=()):
             cols = slice(j0, j0 + w)
@@ -338,8 +354,9 @@ def tile_list_coupled_ionic_current_kernel(
                     nc.sync.dma_start(out=dealt_rows(out_0[:, cols])[:, rows, :], in_=y[:, rows, :])
 
         def round_y(j0, w, slot, shares):
-            rounded = staged("y_rounded", slot, [P, PACK * w], BF16)
-            y_rounded[j0] = rounded
+            if j0 not in y_rounded:
+                y_rounded[j0] = staged("y_rounded", slot, [P, PACK * w], BF16)
+            rounded = y_rounded[j0]
             dst, (src,) = word_walk(rounded[:], [y_rows[j0]])
             for engine, c0, c1 in shares:
                 if engine == "gpsimd":
@@ -404,11 +421,16 @@ def tile_list_coupled_ionic_current_kernel(
         use_banks(range(BANKS))
         for jb in range(8):
             make_gate(0, jb)
-        for rows, gain_engine in ((range(0, 2), "gpsimd"), (range(2, 4), "scalar")):
+        for rows in (range(0, 2), range(2, 4)):
             for h in range(2):
                 for t in rows:
-                    make_force(0, h, t, "force0%d" % h, gain_engine)
+                    make_force(0, h, t, "force0%d" % h, "scalar" if t >= 2 else "gpsimd")
         for jb in range(6):
+            turn_gate(0, jb)
+        for t in range(2):
+            gained_reversal(1, 0, t, "gained")
+        use_banks([6, 7])
+        for jb in range(6, 8):
             turn_gate(0, jb)
         round_weight(("w1", 0, 1), "wr0", [("gpsimd", 0, P)])
         round_weight(("w1", 1, 1), "wr1", [("scalar", 0, P)])
@@ -419,43 +441,43 @@ def tile_list_coupled_ionic_current_kernel(
         quantize_w1(0, 1)
         quantize_w1(1, 1)
         quantize_current(0, 0, 4, "wr0")
-        quantize_current(0, 4, 2, "cc01")
-        use_banks([0, 1, 2, 3, 6, 7, 4, 5])
-        for t in range(PACK):
-            make_force(1, 0, t, "table2", None)
+        use_banks([0, 1])
+        for t in range(2, 4):
+            gained_reversal(1, 0, t, "raw0")
+        use_banks([2, 3, 4, 5])
         for jb in range(4):
             make_gate(1, jb)
         for t in range(PACK):
-            apply_gain(force[1, 0][:, t, :], 1, t, "gpsimd" if t < 3 else "scalar")
+            gained_force(1, 0, t, slice(0, HALF), "table2")
         for jb in range(6, 8):
-            make_current(0, jb, 6, 2, "table0")
-        round_weight(("wc", 0), "wr2", [("gpsimd", 0, P)])
+            make_current(0, jb, 6, 2, "gained")
+        round_weight(("wc", 0), "table0", [("gpsimd", 0, P)])
         round_weight(("wc", 1), "force00", [("scalar", 0, P)])
-        use_banks([2, 3, 6, 7])
+        use_banks([0, 1, 2, 3])
         for jb in range(4):
             make_current(1, jb, 0, 4, "cur00")
-        use_banks([4, 5, 0, 1])
+        use_banks([4, 5, 6, 7])
         for t in range(PACK):
             make_conductance(1, 1, t, "raw1", None if t < 2 else "scalar")
         quantize_current(1, 0, 4, "cc10")
-        quantize_current(0, 6, 2, "cc01")
         quantize_wc(0)
         quantize_wc(1)
-        use_banks([2, 3, 6, 7])
+        use_banks([0, 1, 2, 3])
         for t in range(PACK):
             make_force(1, 1, t, "force00", "gpsimd" if t < 2 else None)
-        use_banks([4, 5, 0, 1])
+        use_banks([4, 5, 6, 7])
         make_y(0, HALF, "raw2", 2)
+        round_y(0, QUARTER, "yr0", [("scalar", 0, QUARTER)])
         for c in range(2):
             make_current_rows(1, 4 + 2 * c, 2, "cur11%d" % c)
-            quantize_current(1, 4 + 2 * c, 2, "cc11")
-        round_y(0, QUARTER, "yr0", [("scalar", 0, QUARTER)])
-        use_banks([2, 3, 6, 7])
+            quantize_current(0, 4 + 2 * c, 2, ("table1", "cur110")[c])
+            quantize_current(1, 4 + 2 * c, 2, "cc11%d" % c)
+        use_banks([0, 1, 2, 3])
         make_y(2 * QUARTER, QUARTER, "raw3")
-        use_banks([4, 5, 0, 1])
+        use_banks([4, 5, 6, 7])
         make_y(3 * QUARTER, QUARTER, "force01")
-        round_y(QUARTER, QUARTER, "cur111", [("vector", 0, QUARTER)])
-        quantize_y(0, QUARTER, "cur110")
+        quantize_y(0, QUARTER, "cur111")
+        round_y(QUARTER, QUARTER, "yr1", [("vector", 0, QUARTER)])
         quantize_y(QUARTER, QUARTER, "yc1")
         round_y(2 * QUARTER, QUARTER, "yr2", [("vector", 0, QUARTER)])
         quantize_y(2 * QUARTER, QUARTER, "yc2")

@@ -185,8 +185,9 @@ def tile_list_coupled_ionic_current_kernel(
             )
 
         def round_weight(key, slot, shares):
-            rounded = staged("w_rounded", slot, [P, PACK * PASS], BF16)
-            rounded_weight[key] = rounded
+            if key not in rounded_weight:
+                rounded_weight[key] = staged("w_rounded", slot, [P, PACK * PASS], BF16)
+            rounded = rounded_weight[key]
             for engine, m0, m1 in shares:
                 if engine == "gpsimd":
                     dst = rounded[:].rearrange("p (t m u) -> p m t u", t=PACK, u=PACK)
@@ -475,7 +476,7 @@ def tile_list_coupled_ionic_current_kernel(
         use_banks([0, 1, 2, 3])
         make_y(2 * QUARTER, QUARTER, "raw3")
         use_banks([4, 5, 6, 7])
-        make_y(3 * QUARTER, QUARTER, "force01")
+        make_y(3 * QUARTER, QUARTER, "force01", 2)
         quantize_y(0, QUARTER, "cur111")
         round_y(QUARTER, QUARTER, "yr1", [("vector", 0, QUARTER)])
         quantize_y(QUARTER, QUARTER, "yc1")

from contextlib import ExitStack

import concourse.mybir as mybir
from concourse.masks import make_identity

K, K2, T, T2, S, H, N = 1024, 512, 2048, 4096, 1024, 1024, 512
FLOPS = 2 * (K * H * S + K2 * H * S + H * N * S)

F32 = mybir.dt.float32
BF16 = mybir.dt.bfloat16
I32 = mybir.dt.int32
U32 = mybir.dt.uint32
U16 = mybir.dt.uint16
U8 = mybir.dt.uint8
E4M3 = mybir.dt.float8_e4m3fn_x4
E2M1 = mybir.dt.float4_e2m1fn_x4
ALU = mybir.AluOpType
ACT = mybir.ActivationFunctionType

P = 128
PACK = 4
PASS = P * PACK
QUADRANT = 32
SPREAD = 8
PLANE_SHIFT = 4
HALF = S // 2
QUARTER = S // 4
WALK = 2
GATE_BUFS = 12
BANKS = 8


def tile_list_coupled_ionic_current_kernel(
    tc, tab_words, tab_scales, tab2_words, tab2_scales, offs, offs2, w1, w2_words, w2_scales, wc, gmax, vm, cinv,
    out_0, out_1, out_2,
):
    nc = tc.nc
    with ExitStack() as ctx:
        keep = ctx.enter_context(tc.tile_pool(name="keep", bufs=1))
        ring = ctx.enter_context(tc.tile_pool(name="ring", bufs=1))
        psum = ctx.enter_context(tc.psum_pool(name="psum", bufs=1))

        def held(name, shape, dtype):
            return keep.tile(shape, dtype, name=name, align_bytes=64)

        def staged(name, slot, shape, dtype):
            return ring.tile(shape, dtype, name=name, tag=slot, align_bytes=64)

        bank_ring = []

        def use_banks(banks):
            bank_ring.clear()
            bank_ring.extend(banks)

        def bank():
            taken = bank_ring[0]
            bank_ring.remove(taken)
            bank_ring.append(taken)
            return psum.tile([P, HALF], F32, name="bank", tag="bank%d" % taken)

        idx = held("idx", [P, S // 16], U16)
        idx2 = held("idx2", [P, S // 16], U16)
        identity = held("identity", [P, P], F32)
        v_table = [staged("v_table%d" % a, "table%d" % a, [P, T], I32) for a in range(2)]
        v_table_scales = held("v_table_scales", [P, T], U8)
        v2_table = staged("v2_table", "table2", [P, T2], I32)
        v2_table_scales = held("v2_table_scales", [P, T2], U8)
        w2_raw = held("w2_raw", [P, 2 * H], U8)
        w2_raw_scales = held("w2_raw_scales", [P, H], U8)
        w2_codes = held("w2_codes", [P, 2 * H], U8)
        e_planes = held("e_planes", [P, S + H], U8)
        v2_plane, w2_plane = e_planes[:, 0:S], e_planes[:, S : S + H]
        v2_picked_scales = held("v2_picked_scales", [P, S], U8)
        v_picked_scales = held("v_picked_scales", [P, S], U8)
        v_codes = [held("v_codes%d" % a, [P, S], U32) for a in range(2)]
        v_planes = held("v_planes", [P, S], U8)
        v2_codes = [held("v2_codes%d" % h, [P, HALF], U32) for h in range(2)]
        gain = held("gain", [P, 2, PACK], F32)
        inv_cap = held("inv_cap", [P, PACK], F32)
        w1_codes = {(a, b): held("w1_codes%d%d" % (a, b), [P, PASS], U32) for a in range(2) for b in range(2)}
        w1_plane = {ab: held("w1_plane%d%d" % ab, [P, PASS], U8) for ab in w1_codes}
        wc_codes = [held("wc_codes%d" % b, [P, N], U32) for b in range(2)]
        wc_plane = [held("wc_plane%d" % b, [P, N], U8) for b in range(2)]
        cur_plane = [held("cur_plane%d" % b, [P, S], U8) for b in range(2)]
        y_plane = held("y_plane", [P, S], U8)
        raw = {}
        voltage = {}
        force = {}
        gate = {}
        conductance = {}
        gained = {}
        turned_gate = {}
        cur_codes = {}
        cur_rounded = {}
        rounded_weight = {}
        y_rows = {}
        y_rounded = {}

        def half(h):
            return slice(HALF * h, HALF * (h + 1))

        def dealt_rows(rows):
            return rows.rearrange("(p t) n -> p t n", t=PACK)

        def move_bytes(dst, src):
            nc.sync.dma_start(out=dst.bitcast(I32), in_=src.bitcast(I32))

        def load_words(tile, words):
            nc.sync.dma_start(out=tile[:], in_=words.rearrange("p t i -> p (t i)").bitcast(I32))

        def load_spread(tile, rows, shift):
            move_bytes(tile[shift:P:SPREAD, :], rows)

        def close_up(tile, shifts):
            for r in range(1, 4):
                for shift in shifts:
                    move_bytes(tile[shift + r : P : QUADRANT, :], tile[shift + SPREAD * r : P : QUADRANT, :])

        def load_w1(a, b, slot):
            raw["w1", a, b] = staged("w1_raw", slot, [P, PACK, PASS], F32)
            block = w1[PASS * a : PASS * (a + 1), PASS * b : PASS * (b + 1)]
            nc.sync.dma_start(out=raw["w1", a, b][:], in_=dealt_rows(block))

        def load_wc(b, slot):
            raw["wc", b] = staged("wc_raw", slot, [P, PACK, N], F32)
            nc.sync.dma_start(out=raw["wc", b][:], in_=dealt_rows(wc[PASS * b : PASS * (b + 1), :]))

        def load_vm_rows(b, rows, slot):
            if (b, 0) not in voltage:
                whole = staged("voltage", slot, [P, PACK, S], F32)
                for h in range(2):
                    voltage[b, h] = whole[:, :, half(h)]
                voltage[b] = whole
            nc.sync.dma_start(out=voltage[b][:, rows, :], in_=dealt_rows(vm[PASS * b : PASS * (b + 1), :])[:, rows, :])

        def load_vm_half(b, h, slot):
            voltage[b, h] = staged("voltage", slot, [P, PACK, HALF], F32)[:]
            nc.sync.dma_start(out=voltage[b, h], in_=dealt_rows(vm[PASS * b : PASS * (b + 1), half(h)]))

        def load_vm_quarter(b, c, slot):
            voltage[b, "q", c] = staged("voltage", slot, [P, PACK, QUARTER], F32)
            cols = slice(QUARTER * c, QUARTER * (c + 1))
            nc.sync.dma_start(out=voltage[b, "q", c][:], in_=dealt_rows(vm[PASS * b : PASS * (b + 1), cols]))

        def gained_force_quarter(b, c, slot):
            h, x = divmod(c, 2)
            force[b, "q", c] = staged("force", slot, [P, PACK, QUARTER], F32)
            for t in range(PACK):
                nc.vector.scalar_tensor_tensor(
                    out=force[b, "q", c][:, t, :],
                    in0=voltage[b, "q", c][:, t, :],
                    scalar=gain[:, b, t : t + 1],
                    in1=gained[b, h, t // 2][:, t % 2, QUARTER * x : QUARTER * (x + 1)],
                    op0=ALU.mult,
                    op1=ALU.subtract,
                )

        def gather(dst, table, offsets):
            nc.vector.tensor_copy(out=dst, in_=table.indirect(offsets))

        def entries(offsets, h):
            return offsets[:, h * HALF // 16 : (h + 1) * HALF // 16]

        def copy_bytes(dst, src):
            nc.vector.tensor_copy(out=dst.bitcast(I32), in_=src.bitcast(I32))

        def deal(dst, src):
            nc.vector.tensor_copy(
                out=dst.rearrange("p (b t m) -> p b m t", b=2, t=PACK),
                in_=src.rearrange("p (b m t) -> p b m t", b=2, t=PACK),
            )

        def copy_on(engine, dst, src):
            if engine == "scalar":
                nc.scalar.copy(out=dst, in_=src)
            elif engine == "vector":
                nc.vector.tensor_copy(out=dst, in_=src)
            else:
                nc.gpsimd.tensor_scalar(out=dst, in0=src, scalar1=1.0, scalar2=0.0, op0=ALU.mult, op1=ALU.add)

        def word_walk(side_by_side, by_rows):
            return (
                side_by_side.rearrange("p (x i t) -> p x t i", t=PACK, i=WALK),
                [rows.rearrange("p t (x i) -> p x t i", i=WALK) for rows in by_rows],
            )

        def round_weight(key, slot, shares):
            if key not in rounded_weight:
                rounded_weight[key] = staged("w_rounded", slot, [P, PACK * PASS], BF16)
            rounded = rounded_weight[key]
            for engine, m0, m1 in shares:
                if engine == "gpsimd":
                    dst = rounded[:].rearrange("p (t m u) -> p m t u", t=PACK, u=PACK)
                    src = raw[key][:].rearrange("p u (m t) -> p m t u", t=PACK)
                else:
                    dst = rounded[:].rearrange("p (t m u v) -> p m u t v", t=PACK, u=2, v=2)
                    src = raw[key][:].rearrange("p (u v) (m t) -> p m u t v", t=PACK, v=2)
                copy_on(engine, dst[:, m0:m1], src[:, m0:m1])

        def quantize_w1(a, b):
            nc.vector.quantize_mx(
                out=w1_codes[a, b][:].bitcast(E4M3), scales=w1_plane[a, b][:], in_=rounded_weight["w1", a, b][:]
            )

        def quantize_wc(b):
            nc.vector.quantize_mx(
                out=wc_codes[b][:].bitcast(E4M3), scales=wc_plane[b][:], in_=rounded_weight["wc", b][:]
            )

        def make_gate(b, jb):
            entries_here = slice(P * jb, P * (jb + 1))
            sums = bank()
            for a in range(2):
                nc.tensor.matmul_mx(
                    out=sums[:],
                    lhsT=v_codes[a][:, entries_here].bitcast(E4M3),
                    lhsT_scale=v_planes[PLANE_SHIFT * a : P, entries_here],
                    rhs=w1_codes[a, b][:].bitcast(E4M3),
                    rhs_scale=w1_plane[a, b][:],
                    start=(a == 0),
                    stop=(a == 1),
                )
            gate[b, jb] = ring.tile([P, PASS], F32, name="gate", tag="gate", align_bytes=64, bufs=GATE_BUFS)
            nc.scalar.activation(out=gate[b, jb][:], in_=sums[:], func=ACT.Sigmoid)

        def make_conductance(b, h, t, slot, gain_engine):
            if (b, h) not in conductance:
                conductance[b, h] = staged("conductance", slot, [P, PACK, HALF], F32)
            sums = bank()
            places = slice(P * t, P * (t + 1))
            for a in range(2):
                nc.tensor.matmul_mx(
                    out=sums[:],
                    lhsT=w1_codes[a, b][:, places].bitcast(E4M3),
                    lhsT_scale=w1_plane[a, b][:, places],
                    rhs=v_codes[a][:, half(h)].bitcast(E4M3),
                    rhs_scale=v_planes[PLANE_SHIFT * a : P, half(h)],
                    start=(a == 0),
                    stop=(a == 1),
                )
            nc.scalar.activation(out=conductance[b, h][:, t, :], in_=sums[:], func=ACT.Sigmoid)
            apply_gain(conductance[b, h][:, t, :], b, t, gain_engine)

        def apply_gain(rows, b, t, gain_engine):
            g = gain[:, b, t : t + 1]
            if gain_engine == "gpsimd":
                nc.gpsimd.tensor_scalar(out=rows, in0=rows, scalar1=g, scalar2=0.0, op0=ALU.mult, op1=ALU.add)
            elif gain_engine == "scalar":
                nc.scalar.activation(out=rows, in_=rows, func=ACT.Copy, scale=g)

        def make_current_rows(b, base, blocks, slot):
            cur_rounded[b, base] = staged("cur_rounded", slot, [P, PASS * blocks], BF16)
            h, x = divmod(base, PACK)
            cols = slice(P * x, P * (x + blocks))
            dst, (g, d) = word_walk(cur_rounded[b, base][:], [conductance[b, h][:, :, cols], force[b, "q", base // 2][:] if (b, "q", base // 2) in force else force[b, h][:, :, cols]])
            nc.vector.tensor_tensor(out=dst, in0=d, in1=g, op=ALU.mult)

        def reversal(b, h, t):
            sums = bank()
            place = PASS * b + P * t
            nc.tensor.matmul_mx(
                out=sums[:],
                lhsT=w2_codes[:, 2 * place : 2 * (place + P)].bitcast(E2M1),
                lhsT_scale=w2_plane[:, place : place + P],
                rhs=v2_codes[h][:].bitcast(E4M3),
                rhs_scale=v2_plane[:, half(h)],
                start=True,
                stop=True,
            )
            return sums

        def force_tile(b, h, slot):
            if (b, h) not in force:
                force[b, h] = staged("force", slot, [P, PACK, HALF], F32)
            return force[b, h]

        def make_force(b, h, t, slot, gain_engine):
            d = force_tile(b, h, slot)[:, t, :]
            nc.vector.tensor_tensor(out=d, in0=voltage[b, h][:, t, :], in1=reversal(b, h, t)[:], op=ALU.subtract)
            apply_gain(d, b, t, gain_engine)

        def gained_reversal(b, h, t, slot):
            if (b, h, t // 2) not in gained:
                gained[b, h, t // 2] = staged("gained", slot, [P, 2, HALF], F32)
            ge = gained[b, h, t // 2][:, t % 2, :]
            nc.scalar.activation(out=ge, in_=reversal(b, h, t)[:], func=ACT.Copy, scale=gain[:, b, t : t + 1])

        def gained_force(b, h, t, cols, slot):
            nc.vector.scalar_tensor_tensor(
                out=force_tile(b, h, slot)[:, t, cols],
                in0=voltage[b, h][:, t, cols],
                scalar=gain[:, b, t : t + 1],
                in1=gained[b, h, t // 2][:, t % 2, cols],
                op0=ALU.mult,
                op1=ALU.subtract,
            )

        def turn_gate(b, jb):
            turned = bank()
            turned_gate[b, jb] = turned
            for t in range(PACK):
                nc.tensor.transpose(turned[:, P * t : P * (t + 1)], gate[b, jb][:, P * t : P * (t + 1)], identity[:])

        def make_current(b, jb, base, blocks, slot):
            if (b, base) not in cur_rounded:
                cur_rounded[b, base] = staged("cur_rounded", slot, [P, PASS * blocks], BF16)
            if (b, jb) not in turned_gate:
                turn_gate(b, jb)
            turned = turned_gate[b, jb]
            h, x = divmod(jb, PACK)
            dst, (g, d) = word_walk(
                cur_rounded[b, base][:, PASS * (jb - base) : PASS * (jb - base + 1)],
                [turned[:].rearrange("p (t j) -> p t j", t=PACK), force[b, h][:, :, P * x : P * (x + 1)]],
            )
            nc.vector.tensor_tensor(out=dst, in0=d, in1=g, op=ALU.mult)

        def quantize_current(b, base, blocks, slot):
            cur_codes[b, base] = staged("cur_codes", slot, [P, P * blocks], U32)
            nc.vector.quantize_mx(
                out=cur_codes[b, base][:].bitcast(E4M3),
                scales=cur_plane[b][:, P * base : P * (base + blocks)],
                in_=cur_rounded[b, base][:],
            )

        def codes_at(b, j0, w):
            base = max(key[1] for key in cur_codes if key[0] == b and P * key[1] <= j0)
            return cur_codes[b, base][:, j0 - P * base : j0 - P * base + w]

        def make_y(j0, w, slot, rows_a_store=PACK, vector_rows=()):
            cols = slice(j0, j0 + w)
            y = staged("y", slot, [P, PACK, w], F32)
            for x in range(0, w, QUARTER):
                y_rows[j0 + x] = y[:, :, x : x + QUARTER]
            for t in range(PACK):
                sums = bank()[:, 0:w]
                places = slice(P * t, P * (t + 1))
                for b in range(2):
                    nc.tensor.matmul_mx(
                        out=sums,
                        lhsT=wc_codes[b][:, places].bitcast(E4M3),
                        lhsT_scale=wc_plane[b][:, places],
                        rhs=codes_at(b, j0, w).bitcast(E4M3),
                        rhs_scale=cur_plane[b][:, cols],
                        start=(b == 0),
                        stop=(b == 1),
                    )
                if t in vector_rows:
                    nc.vector.tensor_scalar(
                        out=y[:, t, :], in0=sums, scalar1=inv_cap[:, t : t + 1], scalar2=None, op0=ALU.mult
                    )
                else:
                    nc.scalar.activation(out=y[:, t, :], in_=sums, func=ACT.Copy, scale=inv_cap[:, t : t + 1])
                if (t + 1) % rows_a_store == 0:
                    rows = slice(t + 1 - rows_a_store, t + 1)
                    nc.sync.dma_start(out=dealt_rows(out_0[:, cols])[:, rows, :], in_=y[:, rows, :])

        def round_y(j0, w, slot, shares):
            if j0 not in y_rounded:
                y_rounded[j0] = staged("y_rounded", slot, [P, PACK * w], BF16)
            rounded = y_rounded[j0]
            dst, (src,) = word_walk(rounded[:], [y_rows[j0]])
            for engine, c0, c1 in shares:
                if engine == "gpsimd":
                    side_by_side = rounded[:].rearrange("p (x t) -> p x t", t=PACK)
                    copy_on(engine, side_by_side[:, c0:c1], y_rows[j0].rearrange("p t x -> p x t")[:, c0:c1])
                else:
                    copy_on(engine, dst[:, c0 // WALK : c1 // WALK], src[:, c0 // WALK : c1 // WALK])

        def quantize_y(j0, w, slot):
            cols = slice(j0, j0 + w)
            y_codes = staged("y_codes", slot, [P, w], U32)
            nc.vector.quantize_mx(out=y_codes[:].bitcast(E4M3), scales=y_plane[:, cols], in_=y_rounded[j0][:])
            words = out_1[0].rearrange("p m t -> p (m t)")
            move_bytes(words[:, PACK * j0 : PACK * (j0 + w)], y_codes[:])


        for tile in (v_table_scales, v2_table_scales, w2_raw_scales):
            nc.vector.memset(tile[:].bitcast(I32), 0)
        make_identity(nc, identity[:])
        move_bytes(w2_raw[:], w2_words[0])
        nc.sync.dma_start(idx[:], offs)
        load_spread(v_table_scales, tab_scales[0], 0)
        load_spread(v_table_scales, tab_scales[1], PLANE_SHIFT)
        load_w1(0, 0, "raw0")
        nc.sync.dma_start(idx2[:], offs2)
        load_spread(v2_table_scales, tab2_scales[0], 0)
        load_words(v_table[0], tab_words[0])
        gather(v_picked_scales[:], v_table_scales[:], idx[:])
        copy_bytes(v_planes[:], v_picked_scales[:])
        load_spread(w2_raw_scales, w2_scales[0], 0)
        gather(v2_picked_scales[:], v2_table_scales[:], idx2[:])
        copy_bytes(v2_plane, v2_picked_scales[:])
        deal(w2_plane, w2_raw_scales[:])
        load_w1(1, 0, "raw1")
        close_up(v_planes, (0, PLANE_SHIFT))
        load_words(v_table[1], tab_words[1])
        nc.sync.dma_start(out=gain[:], in_=gmax.rearrange("(b p t) -> p b t", b=2, t=PACK))
        load_words(v2_table, tab2_words[0])
        close_up(e_planes, (0,))

        load_vm_rows(0, slice(0, 2), "voltage0")
        load_vm_rows(0, slice(2, 4), "voltage0")
        load_w1(0, 1, "raw2")
        load_w1(1, 1, "raw0")
        load_vm_half(1, 0, "table0")
        load_wc(0, "raw3")
        load_wc(1, "raw1")
        load_vm_half(1, 1, "table1")
        nc.sync.dma_start(out=inv_cap[:], in_=cinv.rearrange("(p t) -> p t", t=PACK))

        gather(v_codes[0][:], v_table[0][:].bitcast(U32), idx[:])
        deal(w2_codes[:].bitcast(U16), w2_raw[:].bitcast(U16))
        round_weight(("w1", 0, 0), "wr0", [("scalar", 0, P)])
        quantize_w1(0, 0)
        round_weight(("w1", 1, 0), "wr1", [("scalar", 0, P)])
        quantize_w1(1, 0)
        for h in range(2):
            gather(v_codes[1][:, half(h)], v_table[1][:].bitcast(U32), entries(idx, h))
        for h in range(2):
            gather(v2_codes[h][:], v2_table[:].bitcast(U32), entries(idx2, h))

        use_banks(range(BANKS))
        for jb in range(8):
            make_gate(0, jb)
        for rows in (range(0, 2), range(2, 4)):
            for h in range(2):
                for t in rows:
                    make_force(0, h, t, "force0%d" % h, "scalar" if t >= 2 else "gpsimd")
        for jb in range(6):
            turn_gate(0, jb)
        for t in range(2):
            gained_reversal(1, 0, t, "gained")
        use_banks([6, 7])
        for jb in range(6, 8):
            turn_gate(0, jb)
        round_weight(("w1", 0, 1), "wr0", [("gpsimd", 0, P)])
        round_weight(("w1", 1, 1), "wr1", [("scalar", 0, P)])
        for jb in range(4):
            make_current(0, jb, 0, 4, "cur00")
        for jb in range(4, 6):
            make_current(0, jb, 4, 2, "cur04")
        quantize_w1(0, 1)
        quantize_w1(1, 1)
        quantize_current(0, 0, 4, "wr0")
        use_banks([0, 1])
        for t in range(2, 4):
            gained_reversal(1, 0, t, "raw0")
        use_banks([2, 3, 4, 5])
        for jb in range(4):
            make_gate(1, jb)
        for t in range(PACK):
            gained_force(1, 0, t, slice(0, HALF), "table2")
        for jb in range(6, 8):
            make_current(0, jb, 6, 2, "gained")
        round_weight(("wc", 0), "table0", [("gpsimd", 0, P)])
        round_weight(("wc", 1), "force00", [("scalar", 0, P)])
        use_banks([0, 1, 2, 3])
        for jb in range(4):
            make_current(1, jb, 0, 4, "cur00")
        use_banks([4, 5, 6, 7])
        for t in range(PACK):
            make_conductance(1, 1, t, "raw1", None if t < 2 else "scalar")
        quantize_current(1, 0, 4, "cc10")
        quantize_wc(0)
        quantize_wc(1)
        use_banks([0, 1, 2, 3])
        for t in range(PACK):
            make_force(1, 1, t, "force00", "gpsimd" if t < 2 else None)
        use_banks([4, 5, 6, 7])
        make_y(0, HALF, "raw2", 2)
        round_y(0, QUARTER, "yr0", [("scalar", 0, QUARTER)])
        for c in range(2):
            make_current_rows(1, 4 + 2 * c, 2, "cur11%d" % c)
            quantize_current(0, 4 + 2 * c, 2, ("table1", "cur110")[c])
            quantize_current(1, 4 + 2 * c, 2, "cc11%d" % c)
        use_banks([0, 1, 2, 3])
        make_y(2 * QUARTER, QUARTER, "raw3")
        use_banks([4, 5, 6, 7])
        make_y(3 * QUARTER, QUARTER, "force01", 2)
        quantize_y(0, QUARTER, "cur111")
        round_y(QUARTER, QUARTER, "yr1", [("vector", 0, QUARTER)])
        quantize_y(QUARTER, QUARTER, "yc1")
        round_y(2 * QUARTER, QUARTER, "yr2", [("vector", 0, QUARTER)])
        quantize_y(2 * QUARTER, QUARTER, "yc2")
        round_y(3 * QUARTER, QUARTER, "yr3", [("scalar", 0, 96), ("vector", 96, QUARTER)])
        quantize_y(3 * QUARTER, QUARTER, "yc3")

        out_rows = out_2[0].rearrange("(q r) m -> r q m", r=4)
        for r in range(4):
            queue = nc.sync if r % 2 == 0 else nc.scalar
            queue.dma_start(out=out_rows[r].bitcast(I32), in_=y_plane[r:P:QUADRANT, :].bitcast(I32))
